import numpy as np
import ml_dtypes


def mxq(x, axis, fmt="e4m3"):
    dtype, down = {"e4m3": (ml_dtypes.float8_e4m3fn, 7), "e5m2": (ml_dtypes.float8_e5m2, 14)}[fmt]
    v = np.moveaxis(np.asarray(x, np.float32).astype(ml_dtypes.bfloat16).astype(np.float64), axis, -1)
    blocks = v.reshape(v.shape[:-1] + (-1, 32))
    amax = np.abs(blocks).max(-1, keepdims=True)
    byte = np.maximum(np.where(amax > 0, np.frexp(amax)[1] - 1 + 127, 0) - down, 1)
    scale = np.exp2(byte - 127.0)
    codes = (blocks / scale).astype(np.float32).astype(dtype).astype(np.float64)
    return np.moveaxis((codes * scale).reshape(v.shape), -1, axis)


WIDE = False


def mx_kscale(k):
    if not WIDE:
        return np.ones(k)
    levels = np.array([10, -10, 5, -5, 0])
    if k % 512:
        return np.exp2(np.random.permutation(np.resize(levels, k // 32))).repeat(32)
    a = np.empty((k // 512, 16))
    for p in range(k // 512):
        a[p, :8] = np.random.permutation(np.resize(levels, 8))
        for g in range(8):
            far = levels[np.abs(levels - a[p, g]) >= 10]
            a[p, g + 8] = far[np.random.randint(len(far))]
    return np.exp2(a.ravel()).repeat(32)


BF16 = ml_dtypes.bfloat16


def bf(x):
    return np.asarray(x, np.float32).astype(BF16)


def f64(x):
    return np.asarray(x).astype(np.float64)

def planes(Y):
    n, m = Y.shape
    b = f64(bf(Y)).reshape(n // 32, 32, m)
    amax = np.abs(b).max(1)
    byte = np.clip(np.where(amax > 0, np.frexp(amax)[1] - 1 + 127 - 7, 1), 1, 254)
    codes = (b * np.exp2(127.0 - byte)[:, None, :]).reshape(n, m).astype(np.float32).astype(ml_dtypes.float8_e4m3fn).view(np.uint8)
    words = codes.reshape(n // 512, 128, 4, m).transpose(0, 1, 3, 2)
    return np.ascontiguousarray(words), np.ascontiguousarray(byte.astype(np.uint8).reshape(n // 512, 16, m))


N, C, F = 1024, 512, 2048


def gelu_tanh(h):
    return 0.5 * h * (1.0 + np.tanh(np.sqrt(2.0 / np.pi) * (h + 0.044715 * (h * h * h))))


def setup_inputs():
    s = mx_kscale(C)
    t = mx_kscale(N)
    return {
        "x": bf(np.random.standard_normal((N, C)) * s[None, :]),
        "w1": bf(np.random.standard_normal((C, F)) / np.sqrt(C) / s[:, None]),
        "b1": bf(0.5 * np.random.standard_normal(F)),
        "r": bf((1.0 + 0.1 * np.random.standard_normal(N)) * t),
        "dy": bf(np.random.standard_normal((N, C)) / np.sqrt(N) / t[:, None]),
        "gamma": bf(1.0 + 0.1 * np.random.standard_normal(C)),
    }


def core(x, w1, b1, r, dy, gamma):
    h = (mxq(f64(x), 1, "e4m3") @ mxq(f64(w1), 0, "e4m3")) + f64(b1)[None, :]
    a = gelu_tanh(h)
    u = f64(r)[:, None] * a
    e = f64(dy) * f64(gamma)[None, :]
    return mxq(u, 0, "e4m3").T @ mxq(e, 0, "e4m3")


def reference(x, w1, b1, r, dy, gamma):
    R_out = core(x, w1, b1, r, dy, gamma)
    words, scales = planes(R_out.T)
    return R_out, words, scales

@@ -1,0 +1,411 @@
+from contextlib import ExitStack
+
+import concourse.mybir as mybir
+from concourse.masks import make_identity
+
+N, C, F = 1024, 512, 2048
+FLOPS = 4 * N * C * F
+
+F32 = mybir.dt.float32
+BF16 = mybir.dt.bfloat16
+I32 = mybir.dt.int32
+U32 = mybir.dt.uint32
+U8 = mybir.dt.uint8
+FP8X4 = mybir.dt.float8_e4m3fn_x4
+GELU = mybir.ActivationFunctionType.Gelu_apprx_tanh
+MULT = mybir.AluOpType.mult
+
+P = 128
+G = N // 512
+TILES = F // P
+W_LOADS = ((0, 2), (2, 4), (4, 8), (8, 12), (12, 16))
+S_HALVES = {2: 12, 3: 13}
+V_GROUPS = {1: 8, 2: 10, 4: 14}
+QUANTS = {2: 8, 3: 10, 4: 12, 5: 14}
+DIRECT = 12
+
+
+def tile_convnextdroppathlayerscaleweightgrad_x1_kernel(tc, x, w1, b1, r, dy, gamma, out_0, out_1, out_2):
+    nc = tc.nc
+    vcopy, scopy = nc.vector.tensor_copy, nc.scalar.copy
+    with ExitStack() as ctx:
+        keep = ctx.enter_context(tc.tile_pool(name="keep", bufs=1))
+        work = ctx.enter_context(tc.tile_pool(name="work", bufs=3))
+        psum = ctx.enter_context(tc.psum_pool(name="psum", bufs=1))
+        ctx.enter_context(tc.manual_schedule())
+
+        ident = keep.tile([P, P], F32, name="ident")
+        ident_bf = keep.tile([P, P], BF16, name="ident_bf")
+        rows = keep.tile([P, P], BF16, name="rows")
+        cols = keep.tile([P, 20], F32, name="cols")
+        gcols = keep.tile([P, 4], BF16, name="gcols")
+        gam = keep.tile([P, C], BF16, name="gam")
+        r_sb = keep.tile([P, G, 4], BF16, name="r_sb")
+        warm = keep.tile([P, 1], F32, name="warm")
+        x_raw = [keep.tile([P, 4, C], BF16, name=f"x_raw{g}") for g in range(G)]
+        x_bf = [keep.tile([P, 4 * P, 4], BF16, name=f"x_bf{g}", align_bytes=64) for g in range(G)]
+        x_codes = keep.tile([P, G, 512], U32, name="x_codes", align_bytes=64)
+        x_scales = keep.tile([P, G, 512], U8, name="x_scales", align_bytes=64)
+        w_raw = {}
+        for i0, i1 in W_LOADS:
+            raw = keep.tile([P, 4, (i1 - i0) * P], BF16, name=f"w_raw{i0}")
+            for i in range(i0, i1):
+                w_raw[i] = raw, i - i0
+        w_codes = keep.tile([P, F], U32, name="w_codes", align_bytes=64)
+        w_scales = keep.tile([P, F], U8, name="w_scales", align_bytes=64)
+        dy_raw = [keep.tile([P, 4, C], BF16, name=f"dy_raw{g}") for g in range(G)]
+        e_bf = [keep.tile([P, C, 4], BF16, name=f"e_bf{g}", align_bytes=64) for g in range(G)]
+        e_codes = keep.tile([P, G, C], U32, name="e_codes", align_bytes=64)
+        e_scales = keep.tile([P, G, C], U8, name="e_scales", align_bytes=64)
+        p_codes = keep.tile([P, F], U32, name="p_codes", align_bytes=64)
+        p_scales = keep.tile([P, F], U8, name="p_scales", align_bytes=64)
+
+        def load_x(g, t0, t1):
+            src = x[512 * g : 512 * g + 512, :].rearrange("(m t) k -> m t k", t=4)
+            nc.sync.dma_start(out=x_raw[g][:, t0:t1, :], in_=src[:, t0:t1, :])
+
+        def load_w(i0, i1):
+            c = slice(i0 * P, i1 * P)
+            nc.sync.dma_start(out=w_raw[i0][0][:], in_=w1[:, c].rearrange("(p j) f -> p j f", j=4))
+
+        def load_dy(g):
+            src = dy[512 * g : 512 * g + 512, :].rearrange("(p j) c -> p j c", j=4)
+            nc.sync.dma_start(out=dy_raw[g][:], in_=src)
+
+        def x_transpose(g, half):
+            words = x_raw[g][:].rearrange("p t k -> p (t k)").bitcast(F32)
+            bank = psum.tile([P, 2, 2, P], F32, name="x_bank", tag="t", bufs=3)
+            for n in range(2):
+                t = 2 * half + n
+                for u in range(2):
+                    nc.tensor.transpose(bank[:, n, u, :], words[:, 256 * t + u : 256 * (t + 1) : 2], ident[:])
+            return bank
+
+        def x_exit(copy, g, half, bank):
+            dst = x_bf[g][:, 256 * half : 256 * half + 256, :].rearrange("p c j -> p (c j)").bitcast(F32)
+            copy(
+                out=dst.rearrange("p (t m u) -> p t m u", t=2, u=2),
+                in_=bank[:].rearrange("p t u m -> p t m u"),
+            )
+
+        def x_quant(g):
+            nc.vector.quantize_mx(
+                out=x_codes[:, g, :].bitcast(FP8X4),
+                scales=x_scales[:, g, :],
+                in_=x_bf[g][:].rearrange("p c j -> p (c j)"),
+            )
+
+        wg = {}
+
+        def w_group(copy, i, n):
+            raw, at = w_raw[i]
+            first = i - i % 2
+            if i == first:
+                wg[i] = work.tile([P, 2 * P, 4], BF16, name="w_bf", bufs=5, align_bytes=64)
+            src = raw[:, :, at * P : (at + n) * P]
+            dst = wg[first][:, (i - first) * P : (i - first + n) * P, :]
+            copy(
+                out=dst.rearrange("p (c q) j -> p c j q", q=4),
+                in_=src.rearrange("p j (c q) -> p c j q", q=4),
+            )
+
+        def w_quant(i, n):
+            c = slice(i * P, (i + n) * P)
+            nc.vector.quantize_mx(
+                out=w_codes[:, c].bitcast(FP8X4),
+                scales=w_scales[:, c],
+                in_=wg[i][:, : n * P, :].rearrange("p c j -> p (c j)"),
+            )
+
+        def e_mult(g, t0, t1):
+            nc.vector.tensor_tensor(
+                out=e_bf[g][:, t0 * P : t1 * P, :].rearrange("p (t m) j -> p t m j", m=P),
+                in0=dy_raw[g][:].rearrange("p j (m t) -> p t m j", t=4)[:, t0:t1],
+                in1=gam[:].rearrange("p (m t) -> p t m", t=4)[:, t0:t1].unsqueeze(3).to_broadcast([P, t1 - t0, P, 4]),
+                op=MULT,
+            )
+
+        def e_quant(g):
+            nc.vector.quantize_mx(
+                out=e_codes[:, g, :].bitcast(FP8X4),
+                scales=e_scales[:, g, :],
+                in_=e_bf[g][:].rearrange("p c j -> p (c j)"),
+            )
+
+        a = {}
+
+        def stage1(i, g):
+            bank = psum.tile([P, 512], F32, name="h_bank", tag="h", bufs=3)
+            c = slice(i * P, (i + 1) * P)
+            nc.tensor.matmul_mx(
+                out=bank[:],
+                lhsT=w_codes[:, c].bitcast(FP8X4),
+                lhsT_scale=w_scales[:, c],
+                rhs=x_codes[:, g, :].bitcast(FP8X4),
+                rhs_scale=x_scales[:, g, :],
+                start=True,
+                stop=True,
+            )
+            a[i, g] = work.tile([P, 512], F32, name="a_sb", bufs=8)
+            nc.scalar.activation(out=a[i, g][:], in_=bank[:], func=GELU, bias=cols[:, i : i + 1])
+
+        turned = {}
+        u = {}
+
+        def turn(i, g):
+            turned[i, g] = psum.tile([P, 4, P], F32, name="t_bank", tag="t", bufs=3)
+            for t in range(4):
+                nc.tensor.transpose(turned[i, g][:, t, :], a[i, g][:, t * P : (t + 1) * P], ident[:])
+
+        def u_mult(i, g):
+            if g == 0:
+                u[i] = work.tile([P, G, P, 4], BF16, name="u_bf", bufs=4, align_bytes=64)
+            nc.vector.tensor_tensor(
+                out=u[i][:, g, :, :],
+                in0=turned[i, g][:].rearrange("p t f -> p f t"),
+                in1=r_sb[:, g, :].unsqueeze(1).to_broadcast([P, P, 4]),
+                op=MULT,
+            )
+
+        uq = {}
+
+        def u_quant(i):
+            codes = work.tile([P, G, P], U32, name="u_codes", bufs=8, align_bytes=64)
+            scales = work.tile([P, G, P], U8, name="u_scales", bufs=8, align_bytes=64)
+            nc.vector.quantize_mx(
+                out=codes[:].rearrange("p g f -> p (g f)").bitcast(FP8X4),
+                scales=scales[:].rearrange("p g f -> p (g f)"),
+                in_=u[i][:].rearrange("p g f t -> p (g f t)"),
+            )
+            uq[i] = codes, scales
+
+        r_out = {}
+
+        def stage2_r(i, copy):
+            codes, scales = uq[i]
+            bank = psum.tile([P, C], F32, name="r_bank", tag="r", bufs=2)
+            for g in range(G):
+                nc.tensor.matmul_mx(
+                    out=bank[:],
+                    lhsT=codes[:, g, :].bitcast(FP8X4),
+                    lhsT_scale=scales[:, g, :],
+                    rhs=e_codes[:, g, :].bitcast(FP8X4),
+                    rhs_scale=e_scales[:, g, :],
+                    start=(g == 0),
+                    stop=(g == G - 1),
+                )
+            j, n = divmod(i, 2)
+            if n == 0:
+                r_out[j] = work.tile([P, 2, C], F32, name="r_out", bufs=4)
+            dst = r_out[j][:, n, :]
+            copy(
+                out=dst.rearrange("p (m t) -> p m t", t=4),
+                in_=bank[:].rearrange("p (t m) -> p m t", t=4),
+            )
+            nc.sync.dma_start(out=out_0[i * P : (i + 1) * P, :], in_=dst)
+
+        r_bf = {}
+        p_turned = {}
+        p_bf = {}
+
+        def p_cast(j):
+            r_bf[j] = work.tile([P, 2, 2, P, 2], BF16, name="r_bf", bufs=2)
+            vcopy(
+                out=r_bf[j][:].rearrange("p v n m c -> p v (n m) c"),
+                in_=r_out[j][:].rearrange("p n (m v c) -> p v (n m) c", v=2, c=2),
+            )
+
+        def p_turn(j):
+            words = r_bf[j][:].rearrange("p v n m c -> p (v n m c)").bitcast(F32)
+            p_turned[j] = psum.tile([P, 2, 2, P], F32, name="p_bank", tag="r", bufs=2)
+            for n in range(2):
+                for v in range(2):
+                    nc.tensor.transpose(p_turned[j][:, n, v, :], words[:, 128 * (2 * v + n) : 128 * (2 * v + n + 1)], ident[:])
+
+        def p_exit(j, copy):
+            p_bf[j] = work.tile([P, 2, P, 4], BF16, name="p_bf", bufs=3, align_bytes=64)
+            dst = p_bf[j][:].rearrange("p n f c -> p (n f c)").bitcast(F32)
+            copy(
+                out=dst.rearrange("p (n f v) -> p n f v", n=2, v=2),
+                in_=p_turned[j][:].rearrange("p n v f -> p n f v"),
+            )
+
+        def store_words(i0, i1):
+            nc.sync.dma_start(
+                out=out_1[0, :, i0 * P : i1 * P, :].rearrange("p m t -> p (m t)").bitcast(I32),
+                in_=p_codes[:, i0 * P : i1 * P].bitcast(I32),
+            )
+
+        def store_scales(i0, i1):
+            for quadrant in range(4):
+                queue = nc.scalar if i1 == TILES and quadrant % 2 else nc.sync
+                queue.dma_start(
+                    out=out_2[0, 4 * quadrant : 4 * quadrant + 4, i0 * P : i1 * P].bitcast(I32),
+                    in_=p_scales[32 * quadrant : 32 * quadrant + 4, i0 * P : i1 * P].bitcast(I32),
+                )
+
+        def p_quant(j):
+            c = slice(2 * j * P, (2 * j + 2) * P)
+            nc.vector.quantize_mx(
+                out=p_codes[:, c].bitcast(FP8X4),
+                scales=p_scales[:, c],
+                in_=p_bf[j][:].rearrange("p n f c -> p (n f c)"),
+            )
+            if j % 2 == 1:
+                store_words(2 * j - 2, 2 * j + 2)
+            elif 2 * j + 2 == DIRECT:
+                store_words(2 * j, 2 * j + 2)
+            if 2 * j + 2 == DIRECT:
+                store_scales(0, DIRECT)
+
+        d_bf = {}
+
+        def stage2_p(i, copy):
+            codes, scales = uq[i]
+            bank = psum.tile([P, 4, P], F32, name="d_bank", tag="h", bufs=3)
+            for t in range(4):
+                for g in range(G):
+                    nc.tensor.matmul_mx(
+                        out=bank[:, t, :],
+                        lhsT=e_codes[:, g, t * P : (t + 1) * P].bitcast(FP8X4),
+                        lhsT_scale=e_scales[:, g, t * P : (t + 1) * P],
+                        rhs=codes[:, g, :].bitcast(FP8X4),
+                        rhs_scale=scales[:, g, :],
+                        start=(g == 0),
+                        stop=(g == G - 1),
+                    )
+            d_bf[i] = work.tile([P, P, 4], BF16, name="d_bf", bufs=4, align_bytes=64)
+            copy(out=d_bf[i][:], in_=bank[:].rearrange("p t f -> p f t"))
+
+        def d_quant(i):
+            c = slice(i * P, (i + 1) * P)
+            nc.vector.quantize_mx(
+                out=p_codes[:, c].bitcast(FP8X4),
+                scales=p_scales[:, c],
+                in_=d_bf[i][:].rearrange("p f t -> p (f t)"),
+            )
+            if i % 2 == 1:
+                store_words(i - 1, i + 1)
+            if i == TILES - 1:
+                store_scales(DIRECT, TILES)
+
+        nc.gpsimd.memset(rows[:], 0.0)
+        nc.gpsimd.memset(warm[:], 0.0)
+        make_identity(nc, ident[:])
+        nc.scalar.dma_start(out=rows[0:16, :], in_=b1.rearrange("(i f) -> i f", f=P))
+        nc.scalar.dma_start(out=rows[16:20, :], in_=gamma.rearrange("(i f) -> i f", f=P))
+        nc.scalar.dma_start(out=r_sb[:], in_=r.rearrange("(g p t) -> p g t", g=G, t=4))
+        load_x(0, 0, 2)
+        load_x(0, 2, 4)
+        load_w(0, 2)
+        load_x(1, 0, 4)
+        load_w(2, 4)
+        load_dy(0)
+        load_dy(1)
+        load_w(4, 8)
+        load_w(8, 12)
+        load_w(12, 16)
+
+        nc.scalar.activation(out=warm[:], in_=warm[:], func=GELU)
+        vcopy(out=ident_bf[:], in_=ident[:])
+        x00 = x_transpose(0, 0)
+        c_bank = psum.tile([P, P], BF16, name="c_bank", tag="r", bufs=2)
+        nc.tensor.transpose(c_bank[:], rows[:], ident_bf[:])
+        x01 = x_transpose(0, 1)
+        w_group(vcopy, 0, 2)
+        x_exit(vcopy, 0, 0, x00)
+        scopy(out=gcols[:], in_=c_bank[:, 16:20])
+        scopy(out=cols[:], in_=c_bank[:, 0:20])
+        x_exit(scopy, 0, 1, x01)
+        w_quant(0, 2)
+        g_bank = psum.tile([P, C], BF16, name="g_bank", tag="r", bufs=2)
+        for q in range(4):
+            nc.tensor.transpose(g_bank[:, q * P : (q + 1) * P], gcols[:, q : q + 1].to_broadcast([P, P]), ident_bf[:])
+        scopy(out=gam[:], in_=g_bank[:])
+        x_quant(0)
+
+        x10 = x_transpose(1, 0)
+        x11 = x_transpose(1, 1)
+        x_exit(scopy, 1, 0, x10)
+        x_exit(scopy, 1, 1, x11)
+        stage1(0, 0)
+        stage1(1, 0)
+        w_group(vcopy, 2, 2)
+        e_mult(0, 0, 1)
+        x_quant(1)
+        stage1(0, 1)
+        stage1(1, 1)
+        e_mult(0, 1, 4)
+        w_quant(2, 2)
+        w_group(scopy, 4, 2)
+        e_quant(0)
+        e_mult(1, 0, 4)
+        w_quant(4, 2)
+
+        for k in range(1, TILES // 2 + 2):
+            lead, even, odd = 2 * k, 2 * k - 2, 2 * k - 1
+            ahead = [i for i in (2 * k - 5, 2 * k - 4) if i >= 0]
+            pair = k - 3
+            paired = 0 <= 2 * pair < DIRECT
+            late = pair >= 9
+            for n in range(2):
+                if lead < TILES:
+                    stage1(lead, n)
+                for i in ahead[n : n + 1] if len(ahead) == 2 else ahead[n - 1 : n]:
+                    if i >= DIRECT:
+                        stage2_p(i, scopy)
+                    stage2_r(i, scopy)
+            if k == 1:
+                w_group(scopy, 6, 2)
+            if lead < TILES:
+                stage1(lead + 1, 0)
+            if paired and not late:
+                p_cast(pair)
+            if even < TILES:
+                turn(even, 0)
+                turn(even, 1)
+            if lead < TILES:
+                stage1(lead + 1, 1)
+            if paired and not late:
+                p_turn(pair)
+                p_exit(pair, scopy)
+            if k in S_HALVES:
+                w_group(scopy, S_HALVES[k], 1)
+            if even < TILES:
+                u_mult(even, 0)
+                u_mult(even, 1)
+            if paired and late:
+                p_cast(pair)
+            if k == 1:
+                e_quant(1)
+            if k in QUANTS:
+                w_quant(QUANTS[k], 2)
+            if even < TILES:
+                u_quant(even)
+                turn(odd, 0)
+                turn(odd, 1)
+            if paired and late:
+                p_turn(pair)
+                p_exit(pair, scopy)
+            if even < TILES:
+                u_mult(odd, 0)
+                u_mult(odd, 1)
+            if k == 1:
+                w_quant(6, 2)
+            if k in V_GROUPS:
+                w_group(vcopy, V_GROUPS[k], 2)
+            if paired and not late:
+                p_quant(pair)
+            if pair >= 1 and 2 * pair - 2 < DIRECT and pair - 1 >= 9 and even + 2 < TILES:
+                p_quant(pair - 1)
+            if even < TILES:
+                u_quant(odd)
+            if pair >= 1 and 2 * pair - 2 < DIRECT and pair - 1 >= 9 and even + 2 >= TILES:
+                p_quant(pair - 1)
+            for i in ahead:
+                if i >= DIRECT:
+                    d_quant(i)
+        i = TILES - 1
+        stage2_p(i, scopy)
+        stage2_r(i, vcopy)
+        d_quant(i)

@@ -14,15 +14,30 @@ U8 = mybir.dt.uint8
 FP8X4 = mybir.dt.float8_e4m3fn_x4
 GELU = mybir.ActivationFunctionType.Gelu_apprx_tanh
 MULT = mybir.AluOpType.mult
+ADD = mybir.AluOpType.add
 
 P = 128
 G = N // 512
 TILES = F // P
 W_LOADS = ((0, 2), (2, 4), (4, 8), (8, 12), (12, 16))
-S_HALVES = {2: 12, 3: 13}
-V_GROUPS = {1: 8, 2: 10, 4: 14}
-QUANTS = {2: 8, 3: 10, 4: 12, 5: 14}
-DIRECT = 12
+H_BANKS, T_BANKS, R_BANKS, P_BANKS = 2, 3, 2, 1
+A_BUFS = 8
+W_BUFS = 5
+DIRECT = 15
+V_EXIT = 15
+LAST = 13
+EARLY = 1
+S_CAST = ()
+H_STEPS = {s: [(s + 2, 0), (s + 2, 1)] for s in range(0, TILES - 2)}
+R_STEPS = {s: [s - 3] for s in range(3, 14)}
+E_S = {}
+E_V = {0: [(1, 0, 4)]}
+E_Q = {0: [0], 1: [1]}
+W_S = {s: [s + 5] for s in (0, 1, 2, 4, 6, 8, 10)}
+W_V = {s: [s + 5] for s in (3, 5, 7, 9)}
+W_Q = {s: [s + 4] for s in range(0, 12)}
+WORD_STORES = {3: (0, 4), 7: (4, 8), 12: (8, 13), 14: (13, 16)}
+SCALE_STORES = {9: (0, 10), 14: (10, 16)}
 
 
 def tile_convnextdroppathlayerscaleweightgrad_x1_kernel(tc, x, w1, b1, r, dy, gamma, out_0, out_1, out_2):
@@ -36,13 +51,13 @@ def tile_convnextdroppathlayerscaleweightgrad_x1_kernel(tc, x, w1, b1, r, dy, ga
 
         ident = keep.tile([P, P], F32, name="ident")
         ident_bf = keep.tile([P, P], BF16, name="ident_bf")
-        rows = keep.tile([P, P], BF16, name="rows")
-        cols = keep.tile([P, 20], F32, name="cols")
+        b_rows = keep.tile([P, P], BF16, name="b_rows")
+        bias = keep.tile([P, TILES], F32, name="bias")
         gcols = keep.tile([P, 4], BF16, name="gcols")
         gam = keep.tile([P, C], BF16, name="gam")
         r_sb = keep.tile([P, G, 4], BF16, name="r_sb")
         warm = keep.tile([P, 1], F32, name="warm")
-        x_raw = [keep.tile([P, 4, C], BF16, name=f"x_raw{g}") for g in range(G)]
+        x_raw = {(g, h): keep.tile([P, 2 * C], BF16, name=f"x_raw{g}{h}") for g in range(G) for h in range(2)}
         x_bf = [keep.tile([P, 4 * P, 4], BF16, name=f"x_bf{g}", align_bytes=64) for g in range(G)]
         x_codes = keep.tile([P, G, 512], U32, name="x_codes", align_bytes=64)
         x_scales = keep.tile([P, G, 512], U8, name="x_scales", align_bytes=64)
@@ -54,15 +69,19 @@ def tile_convnextdroppathlayerscaleweightgrad_x1_kernel(tc, x, w1, b1, r, dy, ga
         w_codes = keep.tile([P, F], U32, name="w_codes", align_bytes=64)
         w_scales = keep.tile([P, F], U8, name="w_scales", align_bytes=64)
         dy_raw = [keep.tile([P, 4, C], BF16, name=f"dy_raw{g}") for g in range(G)]
+        e_nat = [keep.tile([P, 4, C], BF16, name=f"e_nat{g}") for g in range(G)]
         e_bf = [keep.tile([P, C, 4], BF16, name=f"e_bf{g}", align_bytes=64) for g in range(G)]
         e_codes = keep.tile([P, G, C], U32, name="e_codes", align_bytes=64)
         e_scales = keep.tile([P, G, C], U8, name="e_scales", align_bytes=64)
         p_codes = keep.tile([P, F], U32, name="p_codes", align_bytes=64)
         p_scales = keep.tile([P, F], U8, name="p_scales", align_bytes=64)
 
-        def load_x(g, t0, t1):
-            src = x[512 * g : 512 * g + 512, :].rearrange("(m t) k -> m t k", t=4)
-            nc.sync.dma_start(out=x_raw[g][:, t0:t1, :], in_=src[:, t0:t1, :])
+        def gcopy(out, in_):
+            nc.gpsimd.tensor_scalar(out=out, in0=in_, scalar1=1.0, scalar2=0.0, op0=MULT, op1=ADD)
+
+        def load_x(g, h):
+            src = x[512 * g : 512 * g + 512, :].rearrange("(m h t) k -> m h (t k)", h=2, t=2)
+            nc.sync.dma_start(out=x_raw[g, h][:], in_=src[:, h, :])
 
         def load_w(i0, i1):
             c = slice(i0 * P, i1 * P)
@@ -72,20 +91,20 @@ def tile_convnextdroppathlayerscaleweightgrad_x1_kernel(tc, x, w1, b1, r, dy, ga
             src = dy[512 * g : 512 * g + 512, :].rearrange("(p j) c -> p j c", j=4)
             nc.sync.dma_start(out=dy_raw[g][:], in_=src)
 
-        def x_transpose(g, half):
-            words = x_raw[g][:].rearrange("p t k -> p (t k)").bitcast(F32)
-            bank = psum.tile([P, 2, 2, P], F32, name="x_bank", tag="t", bufs=3)
-            for n in range(2):
-                t = 2 * half + n
-                for u in range(2):
-                    nc.tensor.transpose(bank[:, n, u, :], words[:, 256 * t + u : 256 * (t + 1) : 2], ident[:])
-            return bank
+        x_turned = {}
 
-        def x_exit(copy, g, half, bank):
-            dst = x_bf[g][:, 256 * half : 256 * half + 256, :].rearrange("p c j -> p (c j)").bitcast(F32)
+        def x_turn(g, h):
+            words = x_raw[g, h][:].bitcast(F32)
+            x_turned[g, h] = psum.tile([P, 2, 2, P], F32, name="x_bank", tag="t", bufs=T_BANKS)
+            for n in range(2):
+                for u in range(2):
+                    nc.tensor.transpose(x_turned[g, h][:, n, u, :], words[:, 256 * n + u : 256 * (n + 1) : 2], ident[:])
+
+        def x_exit(copy, g, h):
+            dst = x_bf[g][:, 256 * h : 256 * h + 256, :].rearrange("p c j -> p (c j)").bitcast(F32)
             copy(
                 out=dst.rearrange("p (t m u) -> p t m u", t=2, u=2),
-                in_=bank[:].rearrange("p t u m -> p t m u"),
+                in_=x_turned[g, h][:].rearrange("p t u m -> p t m u"),
             )
 
         def x_quant(g):
@@ -95,18 +114,26 @@ def tile_convnextdroppathlayerscaleweightgrad_x1_kernel(tc, x, w1, b1, r, dy, ga
                 in_=x_bf[g][:].rearrange("p c j -> p (c j)"),
             )
 
-        wg = {}
+        def bias_turn():
+            bank = psum.tile([P, P], BF16, name="b_bank", tag="r", bufs=R_BANKS)
+            nc.tensor.transpose(bank[:], b_rows[:], ident_bf[:])
+            scopy(out=bias[:], in_=bank[:, 0:TILES])
+
+        def gamma_spread(copy):
+            bank = psum.tile([P, 2, P], F32, name="g_bank", tag="p", bufs=P_BANKS)
+            words = gcols[:].bitcast(F32)
+            for u in range(2):
+                nc.tensor.transpose(bank[:, u, :], words[:, u : u + 1].to_broadcast([P, P]), ident[:])
+            copy(out=gam[:].bitcast(F32).rearrange("p (k u) -> p k u", u=2), in_=bank[:].rearrange("p u k -> p k u"))
+
+        w_bf = {}
 
         def w_group(copy, i, n):
             raw, at = w_raw[i]
-            first = i - i % 2
-            if i == first:
-                wg[i] = work.tile([P, 2 * P, 4], BF16, name="w_bf", bufs=5, align_bytes=64)
-            src = raw[:, :, at * P : (at + n) * P]
-            dst = wg[first][:, (i - first) * P : (i - first + n) * P, :]
+            w_bf[i] = work.tile([P, n * P, 4], BF16, name="w_bf", bufs=W_BUFS, align_bytes=64)
             copy(
-                out=dst.rearrange("p (c q) j -> p c j q", q=4),
-                in_=src.rearrange("p j (c q) -> p c j q", q=4),
+                out=w_bf[i][:].rearrange("p (c q) j -> p c j q", q=4),
+                in_=raw[:, :, at * P : (at + n) * P].rearrange("p j (c q) -> p c j q", q=4),
             )
 
         def w_quant(i, n):
@@ -114,15 +141,21 @@ def tile_convnextdroppathlayerscaleweightgrad_x1_kernel(tc, x, w1, b1, r, dy, ga
             nc.vector.quantize_mx(
                 out=w_codes[:, c].bitcast(FP8X4),
                 scales=w_scales[:, c],
-                in_=wg[i][:, : n * P, :].rearrange("p c j -> p (c j)"),
+                in_=w_bf[i][:].rearrange("p c j -> p (c j)"),
             )
 
-        def e_mult(g, t0, t1):
+        def e_mult(g):
             nc.vector.tensor_tensor(
-                out=e_bf[g][:, t0 * P : t1 * P, :].rearrange("p (t m) j -> p t m j", m=P),
-                in0=dy_raw[g][:].rearrange("p j (m t) -> p t m j", t=4)[:, t0:t1],
-                in1=gam[:].rearrange("p (m t) -> p t m", t=4)[:, t0:t1].unsqueeze(3).to_broadcast([P, t1 - t0, P, 4]),
+                out=e_nat[g][:],
+                in0=dy_raw[g][:],
+                in1=gam[:].unsqueeze(1).to_broadcast([P, 4, C]),
                 op=MULT,
+            )
+
+        def e_group(copy, g, t0, t1):
+            copy(
+                out=e_bf[g][:, t0 * P : t1 * P, :].rearrange("p (t m) j -> p t m j", m=P),
+                in_=e_nat[g][:].rearrange("p j (m t) -> p t m j", t=4)[:, t0:t1],
             )
 
         def e_quant(g):
@@ -135,7 +168,7 @@ def tile_convnextdroppathlayerscaleweightgrad_x1_kernel(tc, x, w1, b1, r, dy, ga
         a = {}
 
         def stage1(i, g):
-            bank = psum.tile([P, 512], F32, name="h_bank", tag="h", bufs=3)
+            bank = psum.tile([P, 512], F32, name="h_bank", tag="h", bufs=H_BANKS)
             c = slice(i * P, (i + 1) * P)
             nc.tensor.matmul_mx(
                 out=bank[:],
@@ -146,20 +179,20 @@ def tile_convnextdroppathlayerscaleweightgrad_x1_kernel(tc, x, w1, b1, r, dy, ga
                 start=True,
                 stop=True,
             )
-            a[i, g] = work.tile([P, 512], F32, name="a_sb", bufs=8)
-            nc.scalar.activation(out=a[i, g][:], in_=bank[:], func=GELU, bias=cols[:, i : i + 1])
+            a[i, g] = work.tile([P, 512], F32, name="a_sb", bufs=A_BUFS)
+            nc.scalar.activation(out=a[i, g][:], in_=bank[:], func=GELU, bias=bias[:, i : i + 1])
 
         turned = {}
         u = {}
 
         def turn(i, g):
-            turned[i, g] = psum.tile([P, 4, P], F32, name="t_bank", tag="t", bufs=3)
+            turned[i, g] = psum.tile([P, 4, P], F32, name="t_bank", tag="t", bufs=T_BANKS)
             for t in range(4):
                 nc.tensor.transpose(turned[i, g][:, t, :], a[i, g][:, t * P : (t + 1) * P], ident[:])
 
         def u_mult(i, g):
             if g == 0:
-                u[i] = work.tile([P, G, P, 4], BF16, name="u_bf", bufs=4, align_bytes=64)
+                u[i] = work.tile([P, G, P, 4], BF16, name="u_bf", bufs=3, align_bytes=64)
             nc.vector.tensor_tensor(
                 out=u[i][:, g, :, :],
                 in0=turned[i, g][:].rearrange("p t f -> p f t"),
@@ -179,14 +212,15 @@ def tile_convnextdroppathlayerscaleweightgrad_x1_kernel(tc, x, w1, b1, r, dy, ga
             )
             uq[i] = codes, scales
 
+        r_bank = {}
         r_out = {}
 
-        def stage2_r(i, copy):
+        def r_product(i):
             codes, scales = uq[i]
-            bank = psum.tile([P, C], F32, name="r_bank", tag="r", bufs=2)
+            r_bank[i] = psum.tile([P, C], F32, name="r_bank", tag="r", bufs=R_BANKS)
             for g in range(G):
                 nc.tensor.matmul_mx(
-                    out=bank[:],
+                    out=r_bank[i][:],
                     lhsT=codes[:, g, :].bitcast(FP8X4),
                     lhsT_scale=scales[:, g, :],
                     rhs=e_codes[:, g, :].bitcast(FP8X4),
@@ -194,41 +228,53 @@ def tile_convnextdroppathlayerscaleweightgrad_x1_kernel(tc, x, w1, b1, r, dy, ga
                     start=(g == 0),
                     stop=(g == G - 1),
                 )
-            j, n = divmod(i, 2)
-            if n == 0:
-                r_out[j] = work.tile([P, 2, C], F32, name="r_out", bufs=4)
-            dst = r_out[j][:, n, :]
+
+        def r_exit(copy, i):
+            r_out[i] = work.tile([P, C], F32, name="r_out", bufs=6)
             copy(
-                out=dst.rearrange("p (m t) -> p m t", t=4),
-                in_=bank[:].rearrange("p (t m) -> p m t", t=4),
+                out=r_out[i][:].rearrange("p (m t) -> p m t", t=4),
+                in_=r_bank[i][:].rearrange("p (t m) -> p m t", t=4),
             )
-            nc.sync.dma_start(out=out_0[i * P : (i + 1) * P, :], in_=dst)
+            nc.sync.dma_start(out=out_0[i * P : (i + 1) * P, :], in_=r_out[i][:])
 
         r_bf = {}
-        p_turned = {}
+        p_bank = {}
         p_bf = {}
 
-        def p_cast(j):
-            r_bf[j] = work.tile([P, 2, 2, P, 2], BF16, name="r_bf", bufs=2)
-            vcopy(
-                out=r_bf[j][:].rearrange("p v n m c -> p v (n m) c"),
-                in_=r_out[j][:].rearrange("p n (m v c) -> p v (n m) c", v=2, c=2),
-            )
+        def p_cast(copy, i):
+            r_bf[i] = work.tile([P, 2, P, 2], BF16, name="r_bf", bufs=3)
+            copy(out=r_bf[i][:], in_=r_out[i][:].rearrange("p (m v c) -> p v m c", v=2, c=2))
 
-        def p_turn(j):
-            words = r_bf[j][:].rearrange("p v n m c -> p (v n m c)").bitcast(F32)
-            p_turned[j] = psum.tile([P, 2, 2, P], F32, name="p_bank", tag="r", bufs=2)
-            for n in range(2):
-                for v in range(2):
-                    nc.tensor.transpose(p_turned[j][:, n, v, :], words[:, 128 * (2 * v + n) : 128 * (2 * v + n + 1)], ident[:])
+        def p_turn(i):
+            words = r_bf[i][:].rearrange("p v m c -> p (v m c)").bitcast(F32)
+            tag, bufs = ("p", P_BANKS) if i < TILES - 3 else ("t", T_BANKS)
+            p_bank[i] = psum.tile([P, 2, P], F32, name="p_bank", tag=tag, bufs=bufs)
+            for v in range(2):
+                nc.tensor.transpose(p_bank[i][:, v, :], words[:, P * v : P * (v + 1)], ident[:])
 
-        def p_exit(j, copy):
-            p_bf[j] = work.tile([P, 2, P, 4], BF16, name="p_bf", bufs=3, align_bytes=64)
-            dst = p_bf[j][:].rearrange("p n f c -> p (n f c)").bitcast(F32)
-            copy(
-                out=dst.rearrange("p (n f v) -> p n f v", n=2, v=2),
-                in_=p_turned[j][:].rearrange("p n v f -> p n f v"),
-            )
+        def p_exit(copy, i):
+            p_bf[i] = work.tile([P, P, 4], BF16, name="p_bf", bufs=5, align_bytes=64)
+            dst = p_bf[i][:].rearrange("p f c -> p (f c)").bitcast(F32)
+            copy(out=dst.rearrange("p (f v) -> p f v", v=2), in_=p_bank[i][:].rearrange("p v f -> p f v"))
+
+        def p_product(i):
+            codes, scales = uq[i]
+            p_bank[i] = psum.tile([P, 4, P], F32, name="d_bank", tag="h", bufs=H_BANKS)
+            for t in range(4):
+                for g in range(G):
+                    nc.tensor.matmul_mx(
+                        out=p_bank[i][:, t, :],
+                        lhsT=e_codes[:, g, t * P : (t + 1) * P].bitcast(FP8X4),
+                        lhsT_scale=e_scales[:, g, t * P : (t + 1) * P],
+                        rhs=codes[:, g, :].bitcast(FP8X4),
+                        rhs_scale=scales[:, g, :],
+                        start=(g == 0),
+                        stop=(g == G - 1),
+                    )
+
+        def d_exit(copy, i):
+            p_bf[i] = work.tile([P, P, 4], BF16, name="p_bf", bufs=5, align_bytes=64)
+            copy(out=p_bf[i][:], in_=p_bank[i][:].rearrange("p t f -> p f t"))
 
         def store_words(i0, i1):
             nc.sync.dma_start(
@@ -244,168 +290,151 @@ def tile_convnextdroppathlayerscaleweightgrad_x1_kernel(tc, x, w1, b1, r, dy, ga
                     in_=p_scales[32 * quadrant : 32 * quadrant + 4, i0 * P : i1 * P].bitcast(I32),
                 )
 
-        def p_quant(j):
-            c = slice(2 * j * P, (2 * j + 2) * P)
-            nc.vector.quantize_mx(
-                out=p_codes[:, c].bitcast(FP8X4),
-                scales=p_scales[:, c],
-                in_=p_bf[j][:].rearrange("p n f c -> p (n f c)"),
-            )
-            if j % 2 == 1:
-                store_words(2 * j - 2, 2 * j + 2)
-            elif 2 * j + 2 == DIRECT:
-                store_words(2 * j, 2 * j + 2)
-            if 2 * j + 2 == DIRECT:
-                store_scales(0, DIRECT)
-
-        d_bf = {}
-
-        def stage2_p(i, copy):
-            codes, scales = uq[i]
-            bank = psum.tile([P, 4, P], F32, name="d_bank", tag="h", bufs=3)
-            for t in range(4):
-                for g in range(G):
-                    nc.tensor.matmul_mx(
-                        out=bank[:, t, :],
-                        lhsT=e_codes[:, g, t * P : (t + 1) * P].bitcast(FP8X4),
-                        lhsT_scale=e_scales[:, g, t * P : (t + 1) * P],
-                        rhs=codes[:, g, :].bitcast(FP8X4),
-                        rhs_scale=scales[:, g, :],
-                        start=(g == 0),
-                        stop=(g == G - 1),
-                    )
-            d_bf[i] = work.tile([P, P, 4], BF16, name="d_bf", bufs=4, align_bytes=64)
-            copy(out=d_bf[i][:], in_=bank[:].rearrange("p t f -> p f t"))
-
-        def d_quant(i):
+        def p_quant(i):
             c = slice(i * P, (i + 1) * P)
             nc.vector.quantize_mx(
                 out=p_codes[:, c].bitcast(FP8X4),
                 scales=p_scales[:, c],
-                in_=d_bf[i][:].rearrange("p f t -> p (f t)"),
+                in_=p_bf[i][:].rearrange("p f c -> p (f c)"),
             )
-            if i % 2 == 1:
-                store_words(i - 1, i + 1)
-            if i == TILES - 1:
-                store_scales(DIRECT, TILES)
+            if i in WORD_STORES:
+                store_words(*WORD_STORES[i])
+            if i in SCALE_STORES:
+                store_scales(*SCALE_STORES[i])
 
-        nc.gpsimd.memset(rows[:], 0.0)
-        nc.gpsimd.memset(warm[:], 0.0)
+        nc.vector.memset(warm[:], 0.0)
+        nc.vector.memset(b_rows[:], 0.0)
         make_identity(nc, ident[:])
-        nc.scalar.dma_start(out=rows[0:16, :], in_=b1.rearrange("(i f) -> i f", f=P))
-        nc.scalar.dma_start(out=rows[16:20, :], in_=gamma.rearrange("(i f) -> i f", f=P))
-        nc.scalar.dma_start(out=r_sb[:], in_=r.rearrange("(g p t) -> p g t", g=G, t=4))
-        load_x(0, 0, 2)
-        load_x(0, 2, 4)
-        load_w(0, 2)
-        load_x(1, 0, 4)
-        load_w(2, 4)
-        load_dy(0)
-        load_dy(1)
-        load_w(4, 8)
-        load_w(8, 12)
-        load_w(12, 16)
-
+        make_identity(nc, ident_bf[:])
         nc.scalar.activation(out=warm[:], in_=warm[:], func=GELU)
-        vcopy(out=ident_bf[:], in_=ident[:])
-        x00 = x_transpose(0, 0)
-        c_bank = psum.tile([P, P], BF16, name="c_bank", tag="r", bufs=2)
-        nc.tensor.transpose(c_bank[:], rows[:], ident_bf[:])
-        x01 = x_transpose(0, 1)
-        w_group(vcopy, 0, 2)
-        x_exit(vcopy, 0, 0, x00)
-        scopy(out=gcols[:], in_=c_bank[:, 16:20])
-        scopy(out=cols[:], in_=c_bank[:, 0:20])
-        x_exit(scopy, 0, 1, x01)
-        w_quant(0, 2)
-        g_bank = psum.tile([P, C], BF16, name="g_bank", tag="r", bufs=2)
-        for q in range(4):
-            nc.tensor.transpose(g_bank[:, q * P : (q + 1) * P], gcols[:, q : q + 1].to_broadcast([P, P]), ident_bf[:])
-        scopy(out=gam[:], in_=g_bank[:])
-        x_quant(0)
+        nc.sync.dma_start(out=gcols[:], in_=gamma.rearrange("(k q) -> k q", q=4))
+        load_x(0, 0)
+        load_x(0, 1)
+        load_w(*W_LOADS[0])
+        nc.sync.dma_start(out=b_rows[0:TILES, :], in_=b1.rearrange("(i f) -> i f", f=P))
+        load_x(1, 0)
+        load_x(1, 1)
+        load_dy(0)
+        load_w(*W_LOADS[1])
+        load_dy(1)
+        nc.sync.dma_start(out=r_sb[:], in_=r.rearrange("(g p t) -> p g t", g=G, t=4))
+        load_w(*W_LOADS[2])
+        load_w(*W_LOADS[3])
+        load_w(*W_LOADS[4])
 
-        x10 = x_transpose(1, 0)
-        x11 = x_transpose(1, 1)
-        x_exit(scopy, 1, 0, x10)
-        x_exit(scopy, 1, 1, x11)
+        gamma_spread(vcopy)
+        x_turn(0, 0)
+        x_exit(scopy, 0, 0)
+        x_turn(0, 1)
+        w_group(vcopy, 0, 2)
+        x_exit(scopy, 0, 1)
+        bias_turn()
+        w_quant(0, 2)
+        x_quant(0)
+        x_turn(1, 0)
+        x_exit(scopy, 1, 0)
+        x_turn(1, 1)
+        x_exit(scopy, 1, 1)
         stage1(0, 0)
         stage1(1, 0)
-        w_group(vcopy, 2, 2)
-        e_mult(0, 0, 1)
+        e_mult(0)
         x_quant(1)
+        w_group(vcopy, 2, 2)
         stage1(0, 1)
         stage1(1, 1)
-        e_mult(0, 1, 4)
+        w_group(scopy, 4, 1)
+        e_mult(1)
         w_quant(2, 2)
-        w_group(scopy, 4, 2)
-        e_quant(0)
-        e_mult(1, 0, 4)
-        w_quant(4, 2)
+        e_group(vcopy, 0, 0, 4)
 
-        for k in range(1, TILES // 2 + 2):
-            lead, even, odd = 2 * k, 2 * k - 2, 2 * k - 1
-            ahead = [i for i in (2 * k - 5, 2 * k - 4) if i >= 0]
-            pair = k - 3
-            paired = 0 <= 2 * pair < DIRECT
-            late = pair >= 9
-            for n in range(2):
-                if lead < TILES:
-                    stage1(lead, n)
-                for i in ahead[n : n + 1] if len(ahead) == 2 else ahead[n - 1 : n]:
-                    if i >= DIRECT:
-                        stage2_p(i, scopy)
-                    stage2_r(i, scopy)
-            if k == 1:
-                w_group(scopy, 6, 2)
-            if lead < TILES:
-                stage1(lead + 1, 0)
-            if paired and not late:
-                p_cast(pair)
-            if even < TILES:
-                turn(even, 0)
-                turn(even, 1)
-            if lead < TILES:
-                stage1(lead + 1, 1)
-            if paired and not late:
-                p_turn(pair)
-                p_exit(pair, scopy)
-            if k in S_HALVES:
-                w_group(scopy, S_HALVES[k], 1)
-            if even < TILES:
-                u_mult(even, 0)
-                u_mult(even, 1)
-            if paired and late:
-                p_cast(pair)
-            if k == 1:
-                e_quant(1)
-            if k in QUANTS:
-                w_quant(QUANTS[k], 2)
-            if even < TILES:
-                u_quant(even)
-                turn(odd, 0)
-                turn(odd, 1)
-            if paired and late:
-                p_turn(pair)
-                p_exit(pair, scopy)
-            if even < TILES:
-                u_mult(odd, 0)
-                u_mult(odd, 1)
-            if k == 1:
-                w_quant(6, 2)
-            if k in V_GROUPS:
-                w_group(vcopy, V_GROUPS[k], 2)
-            if paired and not late:
-                p_quant(pair)
-            if pair >= 1 and 2 * pair - 2 < DIRECT and pair - 1 >= 9 and even + 2 < TILES:
-                p_quant(pair - 1)
-            if even < TILES:
-                u_quant(odd)
-            if pair >= 1 and 2 * pair - 2 < DIRECT and pair - 1 >= 9 and even + 2 >= TILES:
-                p_quant(pair - 1)
-            for i in ahead:
-                if i >= DIRECT:
-                    d_quant(i)
-        i = TILES - 1
-        stage2_p(i, scopy)
-        stage2_r(i, vcopy)
-        d_quant(i)
+        for s in range(LAST + 1):
+            if s < TILES and s < EARLY:
+                turn(s, 0)
+                turn(s, 1)
+            for i, g in H_STEPS.get(s, ()):
+                stage1(i, g)
+            for j in R_STEPS.get(s, ()):
+                if j >= DIRECT:
+                    p_product(j)
+                    d_exit(scopy, j)
+                r_product(j)
+                r_exit(scopy if j < V_EXIT else vcopy, j)
+            if EARLY <= s < TILES:
+                turn(s, 0)
+                turn(s, 1)
+            turned_now = [k for k in R_STEPS.get(s - 1, ()) if k < DIRECT]
+            for piece in E_S.get(s, ()):
+                e_group(scopy, *piece)
+            for i in W_S.get(s, ()):
+                w_group(scopy, i, 1)
+            for j in R_STEPS.get(s, ()):
+                if j < DIRECT and j in S_CAST:
+                    p_cast(scopy, j)
+            for k in turned_now:
+                p_turn(k)
+                p_exit(scopy, k)
+            if s < TILES:
+                u_mult(s, 0)
+            for i in W_Q.get(s, ()):
+                w_quant(i, 1)
+            if s < TILES:
+                u_mult(s, 1)
+            for j in R_STEPS.get(s, ()):
+                if j < DIRECT and j not in S_CAST:
+                    p_cast(vcopy, j)
+            for i in W_V.get(s, ()):
+                w_group(vcopy, i, 1)
+            for piece in E_V.get(s, ()):
+                e_group(vcopy, *piece)
+            for g in E_Q.get(s, ()):
+                e_quant(g)
+            if s < TILES:
+                u_quant(s)
+            for k in turned_now:
+                p_quant(k)
+            for j in R_STEPS.get(s, ()):
+                if j >= DIRECT:
+                    p_quant(j)
+
+        r_product(11)
+        r_exit(scopy, 11)
+        turn(14, 0)
+        turn(14, 1)
+        p_turn(10)
+        p_exit(scopy, 10)
+        turn(15, 0)
+        u_mult(14, 0)
+        r_product(12)
+        r_exit(scopy, 12)
+        turn(15, 1)
+        p_cast(vcopy, 11)
+        p_turn(11)
+        r_product(13)
+        u_mult(14, 1)
+        u_mult(15, 0)
+        p_exit(scopy, 11)
+        r_exit(scopy, 13)
+        u_quant(14)
+        u_mult(15, 1)
+        p_cast(vcopy, 12)
+        u_quant(15)
+        r_product(14)
+        p_turn(12)
+        r_exit(scopy, 14)
+        p_exit(scopy, 12)
+        p_cast(vcopy, 13)
+        p_quant(10)
+        p_quant(11)
+        p_product(15)
+        r_product(15)
+        p_cast(vcopy, 14)
+        d_exit(scopy, 15)
+        p_turn(13)
+        p_turn(14)
+        p_quant(12)
+        r_exit(vcopy, 15)
+        p_exit(scopy, 13)
+        p_exit(scopy, 14)
+        p_quant(15)
+        p_quant(13)
+        p_quant(14)

@@ -22,22 +22,21 @@ TILES = F // P
 W_LOADS = ((0, 2), (2, 4), (4, 8), (8, 12), (12, 16))
 H_BANKS, T_BANKS, R_BANKS, P_BANKS = 2, 3, 2, 1
 A_BUFS = 8
-W_BUFS = 5
-DIRECT = 15
-V_EXIT = 15
-LAST = 13
+W_BUFS = 4
+LAST = 11
 EARLY = 1
-S_CAST = ()
-H_STEPS = {s: [(s + 2, 0), (s + 2, 1)] for s in range(0, TILES - 2)}
-R_STEPS = {s: [s - 3] for s in range(3, 14)}
-E_S = {}
-E_V = {0: [(1, 0, 4)]}
+R_LAG = 3
+E_V = {0: [(1, 0, 2)]}
 E_Q = {0: [0], 1: [1]}
-W_S = {s: [s + 5] for s in (0, 1, 2, 4, 6, 8, 10)}
-W_V = {s: [s + 5] for s in (3, 5, 7, 9)}
-W_Q = {s: [s + 4] for s in range(0, 12)}
-WORD_STORES = {3: (0, 4), 7: (4, 8), 12: (8, 13), 14: (13, 16)}
-SCALE_STORES = {9: (0, 10), 14: (10, 16)}
+W_S = {}
+W_V = {}
+W_G = {s: [(s + 5, 1)] for s in range(11)}
+W_Q = {s: [(s + 5, 1)] for s in range(11)}
+WORD_STORES = {2: (0, 4), 6: (4, 8), 10: (8, 12), 12: (12, 15), 15: (15, 16)}
+SCALE_STORES = {6: (0, 8), 15: (8, 16)}
+E_S = {0: [(1, 2, 4)]}
+G_FIRST = 5
+S_CAST = ()
 
 
 def tile_convnextdroppathlayerscaleweightgrad_x1_kernel(tc, x, w1, b1, r, dy, gamma, out_0, out_1, out_2):
@@ -130,7 +129,14 @@ def tile_convnextdroppathlayerscaleweightgrad_x1_kernel(tc, x, w1, b1, r, dy, ga
 
         def w_group(copy, i, n):
             raw, at = w_raw[i]
-            w_bf[i] = work.tile([P, n * P, 4], BF16, name="w_bf", bufs=W_BUFS, align_bytes=64)
+            if copy is gcopy:
+                w_bf[i] = work.tile([P, P, 4], BF16, name="w_one", bufs=1, align_bytes=64)
+                gcopy(out=w_bf[i][:], in_=raw[:, :, at * P : (at + 1) * P].rearrange("p j c -> p c j"))
+                return
+            if i == G_FIRST - 1:
+                w_bf[i] = work.tile([P, P, 4], BF16, name="w_one", bufs=1, align_bytes=64)
+            else:
+                w_bf[i] = work.tile([P, n * P, 4], BF16, name="w_bf", bufs=W_BUFS, align_bytes=64)
             copy(
                 out=w_bf[i][:].rearrange("p (c q) j -> p c j q", q=4),
                 in_=raw[:, :, at * P : (at + n) * P].rearrange("p j (c q) -> p c j q", q=4),
@@ -185,16 +191,16 @@ def tile_convnextdroppathlayerscaleweightgrad_x1_kernel(tc, x, w1, b1, r, dy, ga
         turned = {}
         u = {}
 
-        def turn(i, g):
-            turned[i, g] = psum.tile([P, 4, P], F32, name="t_bank", tag="t", bufs=T_BANKS)
+        def turn(i, g, tag="t", bufs=T_BANKS):
+            turned[i, g] = psum.tile([P, 4, P], F32, name="t_bank", tag=tag, bufs=bufs)
             for t in range(4):
                 nc.tensor.transpose(turned[i, g][:, t, :], a[i, g][:, t * P : (t + 1) * P], ident[:])
 
         def u_mult(i, g):
-            if g == 0:
-                u[i] = work.tile([P, G, P, 4], BF16, name="u_bf", bufs=3, align_bytes=64)
+            if g == 0 and i % 2 == 0:
+                u[i // 2] = work.tile([P, 2, G, P, 4], BF16, name="u_bf", bufs=2, align_bytes=64)
             nc.vector.tensor_tensor(
-                out=u[i][:, g, :, :],
+                out=u[i // 2][:, i % 2, g, :, :],
                 in0=turned[i, g][:].rearrange("p t f -> p f t"),
                 in1=r_sb[:, g, :].unsqueeze(1).to_broadcast([P, P, 4]),
                 op=MULT,
@@ -202,15 +208,16 @@ def tile_convnextdroppathlayerscaleweightgrad_x1_kernel(tc, x, w1, b1, r, dy, ga
 
         uq = {}
 
-        def u_quant(i):
-            codes = work.tile([P, G, P], U32, name="u_codes", bufs=8, align_bytes=64)
-            scales = work.tile([P, G, P], U8, name="u_scales", bufs=8, align_bytes=64)
+        def u_quant(i, n):
+            codes = work.tile([P, n, G, P], U32, name="u_codes", bufs=4, align_bytes=64)
+            scales = work.tile([P, n, G, P], U8, name="u_scales", bufs=4, align_bytes=64)
             nc.vector.quantize_mx(
-                out=codes[:].rearrange("p g f -> p (g f)").bitcast(FP8X4),
-                scales=scales[:].rearrange("p g f -> p (g f)"),
-                in_=u[i][:].rearrange("p g f t -> p (g f t)"),
+                out=codes[:].rearrange("p n g f -> p (n g f)").bitcast(FP8X4),
+                scales=scales[:].rearrange("p n g f -> p (n g f)"),
+                in_=u[i // 2][:, i % 2 : i % 2 + n].rearrange("p n g f t -> p (n g f t)"),
             )
-            uq[i] = codes, scales
+            for m in range(n):
+                uq[i + m] = codes[:, m], scales[:, m]
 
         r_bank = {}
         r_out = {}
@@ -230,32 +237,36 @@ def tile_convnextdroppathlayerscaleweightgrad_x1_kernel(tc, x, w1, b1, r, dy, ga
                 )
 
         def r_exit(copy, i):
-            r_out[i] = work.tile([P, C], F32, name="r_out", bufs=6)
+            if i % 2 == 0:
+                r_out[i // 2] = work.tile([P, 2, C], F32, name="r_out", bufs=4)
+            dst = r_out[i // 2][:, i % 2, :]
             copy(
-                out=r_out[i][:].rearrange("p (m t) -> p m t", t=4),
+                out=dst.rearrange("p (m t) -> p m t", t=4),
                 in_=r_bank[i][:].rearrange("p (t m) -> p m t", t=4),
             )
-            nc.sync.dma_start(out=out_0[i * P : (i + 1) * P, :], in_=r_out[i][:])
+            nc.sync.dma_start(out=out_0[i * P : (i + 1) * P, :], in_=dst)
 
         r_bf = {}
         p_bank = {}
         p_bf = {}
 
-        def p_cast(copy, i):
-            r_bf[i] = work.tile([P, 2, P, 2], BF16, name="r_bf", bufs=3)
-            copy(out=r_bf[i][:], in_=r_out[i][:].rearrange("p (m v c) -> p v m c", v=2, c=2))
+        def p_cast(copy, i, n):
+            r_bf[i] = work.tile([P, 2, n * P, 2], BF16, name="r_bf", bufs=3)
+            src = r_out[i // 2][:, i % 2 : i % 2 + n, :]
+            copy(out=r_bf[i][:], in_=src.rearrange("p n (m v c) -> p v (n m) c", v=2, c=2))
 
-        def p_turn(i):
+        def p_turn(i, n, tag="p", bufs=P_BANKS):
             words = r_bf[i][:].rearrange("p v m c -> p (v m c)").bitcast(F32)
-            tag, bufs = ("p", P_BANKS) if i < TILES - 3 else ("t", T_BANKS)
-            p_bank[i] = psum.tile([P, 2, P], F32, name="p_bank", tag=tag, bufs=bufs)
-            for v in range(2):
-                nc.tensor.transpose(p_bank[i][:, v, :], words[:, P * v : P * (v + 1)], ident[:])
+            p_bank[i] = psum.tile([P, n, 2, P], F32, name="p_bank", tag=tag, bufs=bufs)
+            for m in range(n):
+                for v in range(2):
+                    at = (n * v + m) * P
+                    nc.tensor.transpose(p_bank[i][:, m, v, :], words[:, at : at + P], ident[:])
 
-        def p_exit(copy, i):
-            p_bf[i] = work.tile([P, P, 4], BF16, name="p_bf", bufs=5, align_bytes=64)
+        def p_exit(copy, i, n):
+            p_bf[i] = work.tile([P, n * P, 4], BF16, name="p_bf", bufs=4, align_bytes=64)
             dst = p_bf[i][:].rearrange("p f c -> p (f c)").bitcast(F32)
-            copy(out=dst.rearrange("p (f v) -> p f v", v=2), in_=p_bank[i][:].rearrange("p v f -> p f v"))
+            copy(out=dst.rearrange("p (n f v) -> p n f v", n=n, v=2), in_=p_bank[i][:].rearrange("p n v f -> p n f v"))
 
         def p_product(i):
             codes, scales = uq[i]
@@ -273,7 +284,7 @@ def tile_convnextdroppathlayerscaleweightgrad_x1_kernel(tc, x, w1, b1, r, dy, ga
                     )
 
         def d_exit(copy, i):
-            p_bf[i] = work.tile([P, P, 4], BF16, name="p_bf", bufs=5, align_bytes=64)
+            p_bf[i] = work.tile([P, P, 4], BF16, name="p_bf", bufs=4, align_bytes=64)
             copy(out=p_bf[i][:], in_=p_bank[i][:].rearrange("p t f -> p f t"))
 
         def store_words(i0, i1):
@@ -290,8 +301,8 @@ def tile_convnextdroppathlayerscaleweightgrad_x1_kernel(tc, x, w1, b1, r, dy, ga
                     in_=p_scales[32 * quadrant : 32 * quadrant + 4, i0 * P : i1 * P].bitcast(I32),
                 )
 
-        def p_quant(i):
-            c = slice(i * P, (i + 1) * P)
+        def p_quant(i, n):
+            c = slice(i * P, (i + n) * P)
             nc.vector.quantize_mx(
                 out=p_codes[:, c].bitcast(FP8X4),
                 scales=p_scales[:, c],
@@ -346,95 +357,106 @@ def tile_convnextdroppathlayerscaleweightgrad_x1_kernel(tc, x, w1, b1, r, dy, ga
         e_mult(1)
         w_quant(2, 2)
         e_group(vcopy, 0, 0, 4)
+        w_quant(4, 1)
 
         for s in range(LAST + 1):
-            if s < TILES and s < EARLY:
+            j = s - R_LAG
+            if s < EARLY:
                 turn(s, 0)
                 turn(s, 1)
-            for i, g in H_STEPS.get(s, ()):
-                stage1(i, g)
-            for j in R_STEPS.get(s, ()):
-                if j >= DIRECT:
-                    p_product(j)
-                    d_exit(scopy, j)
+            stage1(s + 2, 0)
+            stage1(s + 2, 1)
+            if j >= 0:
                 r_product(j)
-                r_exit(scopy if j < V_EXIT else vcopy, j)
-            if EARLY <= s < TILES:
+                r_exit(scopy, j)
+            if EARLY <= s:
                 turn(s, 0)
                 turn(s, 1)
-            turned_now = [k for k in R_STEPS.get(s - 1, ()) if k < DIRECT]
+            k = j - 3
+            if k >= 0 and k % 2 == 0:
+                p_turn(k, 2)
+                p_exit(scopy, k, 2)
+            if j >= 0 and j % 2 == 1 and j - 1 in S_CAST:
+                p_cast(scopy, j - 1, 2)
             for piece in E_S.get(s, ()):
                 e_group(scopy, *piece)
-            for i in W_S.get(s, ()):
-                w_group(scopy, i, 1)
-            for j in R_STEPS.get(s, ()):
-                if j < DIRECT and j in S_CAST:
-                    p_cast(scopy, j)
-            for k in turned_now:
-                p_turn(k)
-                p_exit(scopy, k)
-            if s < TILES:
-                u_mult(s, 0)
-            for i in W_Q.get(s, ()):
-                w_quant(i, 1)
-            if s < TILES:
-                u_mult(s, 1)
-            for j in R_STEPS.get(s, ()):
-                if j < DIRECT and j not in S_CAST:
-                    p_cast(vcopy, j)
-            for i in W_V.get(s, ()):
-                w_group(vcopy, i, 1)
+            for i, n in W_S.get(s, ()):
+                w_group(scopy, i, n)
+            for i, n in W_G.get(s, ()):
+                w_group(gcopy, i, n)
+            u_mult(s, 0)
+            u_mult(s, 1)
+            if j >= 0 and j % 2 == 1 and j - 1 not in S_CAST:
+                p_cast(vcopy, j - 1, 2)
+            if k >= 1 and k % 2 == 1:
+                p_quant(k - 1, 2)
+            for i, n in W_V.get(s, ()):
+                w_group(vcopy, i, n)
             for piece in E_V.get(s, ()):
                 e_group(vcopy, *piece)
             for g in E_Q.get(s, ()):
                 e_quant(g)
-            if s < TILES:
-                u_quant(s)
-            for k in turned_now:
-                p_quant(k)
-            for j in R_STEPS.get(s, ()):
-                if j >= DIRECT:
-                    p_quant(j)
+            if s % 2 == 1:
+                u_quant(s - 1, 2)
+            for i, n in W_Q.get(s, ()):
+                w_quant(i, n)
 
+        stage1(14, 0)
+        stage1(14, 1)
+        r_product(9)
+        r_exit(scopy, 9)
+        turn(12, 0)
+        turn(12, 1)
+        p_turn(6, 2)
+        p_exit(scopy, 6, 2)
+        u_mult(12, 0)
+        u_mult(12, 1)
+        p_cast(vcopy, 8, 2)
+        u_quant(12, 1)
+        stage1(15, 0)
+        stage1(15, 1)
+        r_product(10)
+        r_exit(scopy, 10)
+        turn(13, 0)
+        turn(13, 1)
+        u_mult(13, 0)
+        u_mult(13, 1)
+        p_quant(6, 2)
+        u_quant(13, 1)
         r_product(11)
         r_exit(scopy, 11)
         turn(14, 0)
         turn(14, 1)
-        p_turn(10)
-        p_exit(scopy, 10)
+        p_turn(8, 2)
         turn(15, 0)
-        u_mult(14, 0)
+        p_cast(scopy, 10, 2)
         r_product(12)
+        turn(15, 1, "h", H_BANKS)
+        p_exit(scopy, 8, 2)
         r_exit(scopy, 12)
-        turn(15, 1)
-        p_cast(vcopy, 11)
-        p_turn(11)
         r_product(13)
+        p_turn(10, 2)
+        r_exit(scopy, 13)
+        p_exit(scopy, 10, 2)
+        u_mult(14, 0)
         u_mult(14, 1)
         u_mult(15, 0)
-        p_exit(scopy, 11)
-        r_exit(scopy, 13)
-        u_quant(14)
+        u_quant(14, 1)
         u_mult(15, 1)
-        p_cast(vcopy, 12)
-        u_quant(15)
+        p_cast(vcopy, 12, 2)
+        u_quant(15, 1)
         r_product(14)
-        p_turn(12)
+        p_product(14)
         r_exit(scopy, 14)
-        p_exit(scopy, 12)
-        p_cast(vcopy, 13)
-        p_quant(10)
-        p_quant(11)
+        d_exit(scopy, 14)
+        p_turn(12, 2)
+        p_exit(scopy, 12, 2)
+        p_quant(8, 2)
+        p_quant(10, 2)
         p_product(15)
         r_product(15)
-        p_cast(vcopy, 14)
         d_exit(scopy, 15)
-        p_turn(13)
-        p_turn(14)
-        p_quant(12)
+        p_quant(14, 1)
+        p_quant(12, 2)
         r_exit(vcopy, 15)
-        p_exit(scopy, 13)
-        p_exit(scopy, 14)
-        p_quant(15)
-        p_quant(13)
-        p_quant(14)
+        p_quant(15, 1)

@@ -23,20 +23,9 @@ W_LOADS = ((0, 2), (2, 4), (4, 8), (8, 12), (12, 16))
 H_BANKS, T_BANKS, R_BANKS, P_BANKS = 2, 3, 2, 1
 A_BUFS = 8
 W_BUFS = 4
-LAST = 11
-EARLY = 1
-R_LAG = 3
-E_V = {0: [(1, 0, 2)]}
-E_Q = {0: [0], 1: [1]}
-W_S = {}
-W_V = {}
-W_G = {s: [(s + 5, 1)] for s in range(11)}
-W_Q = {s: [(s + 5, 1)] for s in range(11)}
+G_FIRST = 5
 WORD_STORES = {2: (0, 4), 6: (4, 8), 10: (8, 12), 12: (12, 15), 15: (15, 16)}
 SCALE_STORES = {6: (0, 8), 15: (8, 16)}
-E_S = {0: [(1, 2, 4)]}
-G_FIRST = 5
-S_CAST = ()
 
 
 def tile_convnextdroppathlayerscaleweightgrad_x1_kernel(tc, x, w1, b1, r, dy, gamma, out_0, out_1, out_2):
@@ -68,7 +57,7 @@ def tile_convnextdroppathlayerscaleweightgrad_x1_kernel(tc, x, w1, b1, r, dy, ga
         w_codes = keep.tile([P, F], U32, name="w_codes", align_bytes=64)
         w_scales = keep.tile([P, F], U8, name="w_scales", align_bytes=64)
         dy_raw = [keep.tile([P, 4, C], BF16, name=f"dy_raw{g}") for g in range(G)]
-        e_nat = [keep.tile([P, 4, C], BF16, name=f"e_nat{g}") for g in range(G)]
+        e_nat = [keep.tile([P, 2, 4, P, 2], BF16, name=f"e_nat{g}") for g in range(G)]
         e_bf = [keep.tile([P, C, 4], BF16, name=f"e_bf{g}", align_bytes=64) for g in range(G)]
         e_codes = keep.tile([P, G, C], U32, name="e_codes", align_bytes=64)
         e_scales = keep.tile([P, G, C], U8, name="e_scales", align_bytes=64)
@@ -113,17 +102,23 @@ def tile_convnextdroppathlayerscaleweightgrad_x1_kernel(tc, x, w1, b1, r, dy, ga
                 in_=x_bf[g][:].rearrange("p c j -> p (c j)"),
             )
 
-        def bias_turn():
-            bank = psum.tile([P, P], BF16, name="b_bank", tag="r", bufs=R_BANKS)
-            nc.tensor.transpose(bank[:], b_rows[:], ident_bf[:])
-            scopy(out=bias[:], in_=bank[:, 0:TILES])
+        small = {}
 
-        def gamma_spread(copy):
-            bank = psum.tile([P, 2, P], F32, name="g_bank", tag="p", bufs=P_BANKS)
+        def bias_turn():
+            small["b"] = psum.tile([P, P], BF16, name="b_bank", tag="r", bufs=R_BANKS)
+            nc.tensor.transpose(small["b"][:], b_rows[:], ident_bf[:])
+
+        def bias_exit(copy):
+            copy(out=bias[:], in_=small["b"][:, 0:TILES])
+
+        def gamma_turn():
+            bank = small["g"] = psum.tile([P, 2, P], F32, name="g_bank", tag="p", bufs=P_BANKS)
             words = gcols[:].bitcast(F32)
             for u in range(2):
                 nc.tensor.transpose(bank[:, u, :], words[:, u : u + 1].to_broadcast([P, P]), ident[:])
-            copy(out=gam[:].bitcast(F32).rearrange("p (k u) -> p k u", u=2), in_=bank[:].rearrange("p u k -> p k u"))
+
+        def gamma_exit(copy):
+            copy(out=gam[:].bitcast(F32), in_=small["g"][:].rearrange("p u k -> p (u k)"))
 
         w_bf = {}
 
@@ -153,15 +148,15 @@ def tile_convnextdroppathlayerscaleweightgrad_x1_kernel(tc, x, w1, b1, r, dy, ga
         def e_mult(g):
             nc.vector.tensor_tensor(
                 out=e_nat[g][:],
-                in0=dy_raw[g][:],
-                in1=gam[:].unsqueeze(1).to_broadcast([P, 4, C]),
+                in0=dy_raw[g][:].rearrange("p j (m v c) -> p v j m c", v=2, c=2),
+                in1=gam[:].rearrange("p (v m c) -> p v m c", v=2, c=2).unsqueeze(2).to_broadcast([P, 2, 4, P, 2]),
                 op=MULT,
             )
 
-        def e_group(copy, g, t0, t1):
+        def e_group(copy, g, v):
             copy(
-                out=e_bf[g][:, t0 * P : t1 * P, :].rearrange("p (t m) j -> p t m j", m=P),
-                in_=e_nat[g][:].rearrange("p j (m t) -> p t m j", t=4)[:, t0:t1],
+                out=e_bf[g][:, 2 * v * P : 2 * (v + 1) * P, :].rearrange("p (c n m) j -> p n j m c", c=2, m=2),
+                in_=e_nat[g][:, v].rearrange("p j (n m) c -> p n j m c", m=2),
             )
 
         def e_quant(g):
@@ -173,8 +168,10 @@ def tile_convnextdroppathlayerscaleweightgrad_x1_kernel(tc, x, w1, b1, r, dy, ga
 
         a = {}
 
-        def stage1(i, g):
-            bank = psum.tile([P, 512], F32, name="h_bank", tag="h", bufs=H_BANKS)
+        h_bank = {}
+
+        def h_product(i, g):
+            bank = h_bank[i, g] = psum.tile([P, 512], F32, name="h_bank", tag="h", bufs=H_BANKS)
             c = slice(i * P, (i + 1) * P)
             nc.tensor.matmul_mx(
                 out=bank[:],
@@ -185,8 +182,10 @@ def tile_convnextdroppathlayerscaleweightgrad_x1_kernel(tc, x, w1, b1, r, dy, ga
                 start=True,
                 stop=True,
             )
+
+        def gelu(i, g):
             a[i, g] = work.tile([P, 512], F32, name="a_sb", bufs=A_BUFS)
-            nc.scalar.activation(out=a[i, g][:], in_=bank[:], func=GELU, bias=bias[:, i : i + 1])
+            nc.scalar.activation(out=a[i, g][:], in_=h_bank[i, g][:], func=GELU, bias=bias[:, i : i + 1])
 
         turned = {}
         u = {}
@@ -209,8 +208,8 @@ def tile_convnextdroppathlayerscaleweightgrad_x1_kernel(tc, x, w1, b1, r, dy, ga
         uq = {}
 
         def u_quant(i, n):
-            codes = work.tile([P, n, G, P], U32, name="u_codes", bufs=4, align_bytes=64)
-            scales = work.tile([P, n, G, P], U8, name="u_scales", bufs=4, align_bytes=64)
+            codes = work.tile([P, n, G, P], U32, name="u_codes", bufs=6, align_bytes=64)
+            scales = work.tile([P, n, G, P], U8, name="u_scales", bufs=6, align_bytes=64)
             nc.vector.quantize_mx(
                 out=codes[:].rearrange("p n g f -> p (n g f)").bitcast(FP8X4),
                 scales=scales[:].rearrange("p n g f -> p (n g f)"),
@@ -245,6 +244,21 @@ def tile_convnextdroppathlayerscaleweightgrad_x1_kernel(tc, x, w1, b1, r, dy, ga
                 in_=r_bank[i][:].rearrange("p (t m) -> p m t", t=4),
             )
             nc.sync.dma_start(out=out_0[i * P : (i + 1) * P, :], in_=dst)
+
+        def r_half(i, h):
+            codes, scales = uq[i]
+            r_bank[i, h] = psum.tile([P, 2, P], F32, name="r_half", tag="t", bufs=T_BANKS)
+            c = slice(2 * h * P, 2 * (h + 1) * P)
+            for g in range(G):
+                nc.tensor.matmul_mx(
+                    out=r_bank[i, h][:].rearrange("p t m -> p (t m)"),
+                    lhsT=codes[:, g, :].bitcast(FP8X4),
+                    lhsT_scale=scales[:, g, :],
+                    rhs=e_codes[:, g, c].bitcast(FP8X4),
+                    rhs_scale=e_scales[:, g, c],
+                    start=(g == 0),
+                    stop=(g == G - 1),
+                )
 
         r_bf = {}
         p_bank = {}
@@ -332,131 +346,262 @@ def tile_convnextdroppathlayerscaleweightgrad_x1_kernel(tc, x, w1, b1, r, dy, ga
         load_w(*W_LOADS[2])
         load_w(*W_LOADS[3])
         load_w(*W_LOADS[4])
-
-        gamma_spread(vcopy)
+        gamma_turn()
+        gamma_exit(scopy)
+        w_group(vcopy, 0, 2)
         x_turn(0, 0)
         x_exit(scopy, 0, 0)
-        x_turn(0, 1)
-        w_group(vcopy, 0, 2)
-        x_exit(scopy, 0, 1)
-        bias_turn()
         w_quant(0, 2)
+        x_turn(0, 1)
+        x_exit(scopy, 0, 1)
         x_quant(0)
+        bias_turn()
+        bias_exit(scopy)
+        e_mult(0)
         x_turn(1, 0)
         x_exit(scopy, 1, 0)
         x_turn(1, 1)
         x_exit(scopy, 1, 1)
-        stage1(0, 0)
-        stage1(1, 0)
-        e_mult(0)
         x_quant(1)
-        w_group(vcopy, 2, 2)
-        stage1(0, 1)
-        stage1(1, 1)
-        w_group(scopy, 4, 1)
+        h_product(0, 0)
+        w_group(scopy, 2, 1)
+        w_group(vcopy, 3, 1)
+        h_product(1, 0)
+        gelu(0, 0)
         e_mult(1)
-        w_quant(2, 2)
-        e_group(vcopy, 0, 0, 4)
+        h_product(0, 1)
+        gelu(1, 0)
+        w_quant(2, 1)
+        h_product(1, 1)
+        gelu(0, 1)
+        w_quant(3, 1)
+        turn(0, 0)
+        gelu(1, 1)
+        e_group(vcopy, 0, 0)
+        turn(0, 1)
+        w_group(scopy, 4, 1)
+        e_group(vcopy, 0, 1)
+        h_product(2, 0)
+        gelu(2, 0)
         w_quant(4, 1)
-
-        for s in range(LAST + 1):
-            j = s - R_LAG
-            if s < EARLY:
-                turn(s, 0)
-                turn(s, 1)
-            stage1(s + 2, 0)
-            stage1(s + 2, 1)
-            if j >= 0:
-                r_product(j)
-                r_exit(scopy, j)
-            if EARLY <= s:
-                turn(s, 0)
-                turn(s, 1)
-            k = j - 3
-            if k >= 0 and k % 2 == 0:
-                p_turn(k, 2)
-                p_exit(scopy, k, 2)
-            if j >= 0 and j % 2 == 1 and j - 1 in S_CAST:
-                p_cast(scopy, j - 1, 2)
-            for piece in E_S.get(s, ()):
-                e_group(scopy, *piece)
-            for i, n in W_S.get(s, ()):
-                w_group(scopy, i, n)
-            for i, n in W_G.get(s, ()):
-                w_group(gcopy, i, n)
-            u_mult(s, 0)
-            u_mult(s, 1)
-            if j >= 0 and j % 2 == 1 and j - 1 not in S_CAST:
-                p_cast(vcopy, j - 1, 2)
-            if k >= 1 and k % 2 == 1:
-                p_quant(k - 1, 2)
-            for i, n in W_V.get(s, ()):
-                w_group(vcopy, i, n)
-            for piece in E_V.get(s, ()):
-                e_group(vcopy, *piece)
-            for g in E_Q.get(s, ()):
-                e_quant(g)
-            if s % 2 == 1:
-                u_quant(s - 1, 2)
-            for i, n in W_Q.get(s, ()):
-                w_quant(i, n)
-
-        stage1(14, 0)
-        stage1(14, 1)
+        w_group(gcopy, 5, 1)
+        h_product(2, 1)
+        gelu(2, 1)
+        u_mult(0, 0)
+        h_product(3, 0)
+        e_group(scopy, 1, 1)
+        u_mult(0, 1)
+        h_product(3, 1)
+        gelu(3, 0)
+        e_group(vcopy, 1, 0)
+        turn(1, 0)
+        gelu(3, 1)
+        e_quant(0)
+        turn(1, 1)
+        w_quant(5, 1)
+        w_group(gcopy, 6, 1)
+        h_product(4, 0)
+        gelu(4, 0)
+        u_mult(1, 0)
+        h_product(4, 1)
+        gelu(4, 1)
+        u_mult(1, 1)
+        turn(2, 0)
+        e_quant(1)
+        turn(2, 1)
+        u_quant(0, 1)
+        h_product(5, 0)
+        gelu(5, 0)
+        w_quant(6, 1)
+        w_group(gcopy, 7, 1)
+        h_product(5, 1)
+        gelu(5, 1)
+        u_mult(2, 0)
+        r_product(0)
+        r_exit(scopy, 0)
+        u_mult(2, 1)
+        turn(3, 0)
+        u_quant(1, 1)
+        turn(3, 1)
+        w_quant(7, 1)
+        w_group(gcopy, 8, 1)
+        h_product(6, 0)
+        gelu(6, 0)
+        u_mult(3, 0)
+        h_product(6, 1)
+        gelu(6, 1)
+        u_mult(3, 1)
+        r_product(1)
+        r_exit(scopy, 1)
+        u_quant(2, 1)
+        turn(4, 0)
+        u_quant(3, 1)
+        turn(4, 1)
+        w_quant(8, 1)
+        w_group(gcopy, 9, 1)
+        h_product(7, 0)
+        gelu(7, 0)
+        u_mult(4, 0)
+        h_product(7, 1)
+        gelu(7, 1)
+        u_mult(4, 1)
+        r_product(2)
+        r_exit(scopy, 2)
+        p_cast(vcopy, 0, 2)
+        turn(5, 0)
+        w_quant(9, 1)
+        w_group(gcopy, 10, 1)
+        turn(5, 1)
+        u_mult(5, 0)
+        h_product(8, 0)
+        gelu(8, 0)
+        u_mult(5, 1)
+        h_product(8, 1)
+        gelu(8, 1)
+        u_quant(4, 1)
+        r_product(3)
+        r_exit(scopy, 3)
+        u_quant(5, 1)
+        turn(6, 0)
+        w_quant(10, 1)
+        w_group(gcopy, 11, 1)
+        turn(6, 1)
+        u_mult(6, 0)
+        p_turn(0, 2)
+        p_exit(scopy, 0, 2)
+        u_mult(6, 1)
+        h_product(9, 0)
+        gelu(9, 0)
+        p_cast(vcopy, 2, 2)
+        h_product(9, 1)
+        gelu(9, 1)
+        w_quant(11, 1)
+        w_group(gcopy, 12, 1)
+        r_product(4)
+        r_exit(scopy, 4)
+        turn(7, 0)
+        u_mult(7, 0)
+        turn(7, 1)
+        u_mult(7, 1)
+        h_product(10, 0)
+        gelu(10, 0)
+        p_quant(0, 2)
+        h_product(10, 1)
+        gelu(10, 1)
+        u_quant(6, 2)
+        r_product(5)
+        r_exit(scopy, 5)
+        w_quant(12, 1)
+        w_group(gcopy, 13, 1)
+        turn(8, 0)
+        u_mult(8, 0)
+        turn(8, 1)
+        u_mult(8, 1)
+        p_turn(2, 2)
+        p_exit(scopy, 2, 2)
+        p_cast(vcopy, 4, 2)
+        h_product(11, 0)
+        gelu(11, 0)
+        w_quant(13, 1)
+        w_group(gcopy, 14, 1)
+        h_product(11, 1)
+        gelu(11, 1)
+        r_product(6)
+        r_exit(scopy, 6)
+        turn(9, 0)
+        u_mult(9, 0)
+        turn(9, 1)
+        u_mult(9, 1)
+        h_product(12, 0)
+        gelu(12, 0)
+        p_quant(2, 2)
+        h_product(12, 1)
+        gelu(12, 1)
+        u_quant(8, 2)
+        r_product(7)
+        r_exit(scopy, 7)
+        w_quant(14, 1)
+        w_group(gcopy, 15, 1)
+        turn(10, 0)
+        u_mult(10, 0)
+        turn(10, 1)
+        u_mult(10, 1)
+        p_turn(4, 2)
+        p_exit(scopy, 4, 2)
+        p_cast(vcopy, 6, 2)
+        h_product(13, 0)
+        gelu(13, 0)
+        w_quant(15, 1)
+        h_product(13, 1)
+        gelu(13, 1)
+        r_product(8)
+        r_exit(scopy, 8)
+        turn(11, 0)
+        u_mult(11, 0)
+        turn(11, 1)
+        u_mult(11, 1)
+        h_product(14, 0)
+        gelu(14, 0)
+        p_quant(4, 2)
+        h_product(14, 1)
+        gelu(14, 1)
+        u_quant(10, 2)
         r_product(9)
         r_exit(scopy, 9)
         turn(12, 0)
+        u_mult(12, 0)
         turn(12, 1)
+        u_mult(12, 1)
         p_turn(6, 2)
         p_exit(scopy, 6, 2)
-        u_mult(12, 0)
-        u_mult(12, 1)
         p_cast(vcopy, 8, 2)
+        h_product(15, 0)
+        gelu(15, 0)
         u_quant(12, 1)
-        stage1(15, 0)
-        stage1(15, 1)
+        h_product(15, 1)
+        gelu(15, 1)
         r_product(10)
         r_exit(scopy, 10)
         turn(13, 0)
-        turn(13, 1)
         u_mult(13, 0)
+        turn(13, 1)
         u_mult(13, 1)
-        p_quant(6, 2)
-        u_quant(13, 1)
         r_product(11)
         r_exit(scopy, 11)
+        p_quant(6, 2)
         turn(14, 0)
-        turn(14, 1)
-        p_turn(8, 2)
-        turn(15, 0)
         p_cast(scopy, 10, 2)
-        r_product(12)
-        turn(15, 1, "h", H_BANKS)
-        p_exit(scopy, 8, 2)
-        r_exit(scopy, 12)
-        r_product(13)
-        p_turn(10, 2)
-        r_exit(scopy, 13)
-        p_exit(scopy, 10, 2)
+        u_quant(13, 1)
+        turn(14, 1)
         u_mult(14, 0)
+        p_turn(8, 2)
+        p_exit(scopy, 8, 2)
         u_mult(14, 1)
+        turn(15, 0)
         u_mult(15, 0)
+        r_product(12)
+        r_exit(scopy, 12)
         u_quant(14, 1)
+        turn(15, 1, "h", H_BANKS)
         u_mult(15, 1)
+        r_product(13)
+        r_exit(scopy, 13)
         p_cast(vcopy, 12, 2)
+        p_turn(10, 2)
+        p_exit(scopy, 10, 2)
         u_quant(15, 1)
         r_product(14)
-        p_product(14)
         r_exit(scopy, 14)
+        p_quant(8, 2)
+        p_product(14)
         d_exit(scopy, 14)
+        p_quant(10, 2)
         p_turn(12, 2)
         p_exit(scopy, 12, 2)
-        p_quant(8, 2)
-        p_quant(10, 2)
-        p_product(15)
-        r_product(15)
-        d_exit(scopy, 15)
         p_quant(14, 1)
+        p_product(15)
+        d_exit(scopy, 15)
         p_quant(12, 2)
+        r_product(15)
         r_exit(vcopy, 15)
         p_quant(15, 1)

@@ -21,11 +21,11 @@ G = N // 512
 TILES = F // P
 W_LOADS = ((0, 2), (2, 4), (4, 8), (8, 12), (12, 16))
 H_BANKS, T_BANKS, R_BANKS, P_BANKS = 2, 3, 2, 1
-A_BUFS = 8
+A_BUFS = 10
 W_BUFS = 4
 G_FIRST = 5
-WORD_STORES = {2: (0, 4), 6: (4, 8), 10: (8, 12), 12: (12, 15), 15: (15, 16)}
-SCALE_STORES = {6: (0, 8), 15: (8, 16)}
+WORD_STORES = {2: (0, 4), 6: (4, 8), 10: (8, 12), 14: (12, 16)}
+SCALE_STORES = {4: (0, 6), 14: (6, 16)}
 
 
 def tile_convnextdroppathlayerscaleweightgrad_x1_kernel(tc, x, w1, b1, r, dy, gamma, out_0, out_1, out_2):
@@ -170,8 +170,8 @@ def tile_convnextdroppathlayerscaleweightgrad_x1_kernel(tc, x, w1, b1, r, dy, ga
 
         h_bank = {}
 
-        def h_product(i, g):
-            bank = h_bank[i, g] = psum.tile([P, 512], F32, name="h_bank", tag="h", bufs=H_BANKS)
+        def h_product(i, g, tag="h", bufs=H_BANKS):
+            bank = h_bank[i, g] = psum.tile([P, 512], F32, name="h_bank", tag=tag, bufs=bufs)
             c = slice(i * P, (i + 1) * P)
             nc.tensor.matmul_mx(
                 out=bank[:],
@@ -196,7 +196,7 @@ def tile_convnextdroppathlayerscaleweightgrad_x1_kernel(tc, x, w1, b1, r, dy, ga
                 nc.tensor.transpose(turned[i, g][:, t, :], a[i, g][:, t * P : (t + 1) * P], ident[:])
 
         def u_mult(i, g):
-            if g == 0 and i % 2 == 0:
+            if i // 2 not in u:
                 u[i // 2] = work.tile([P, 2, G, P, 4], BF16, name="u_bf", bufs=2, align_bytes=64)
             nc.vector.tensor_tensor(
                 out=u[i // 2][:, i % 2, g, :, :],
@@ -219,6 +219,7 @@ def tile_convnextdroppathlayerscaleweightgrad_x1_kernel(tc, x, w1, b1, r, dy, ga
                 uq[i + m] = codes[:, m], scales[:, m]
 
         r_bank = {}
+        p_bank = {}
         r_out = {}
 
         def r_product(i):
@@ -260,22 +261,65 @@ def tile_convnextdroppathlayerscaleweightgrad_x1_kernel(tc, x, w1, b1, r, dy, ga
                     stop=(g == G - 1),
                 )
 
+        def last_quant(i, g):
+            if g == 0:
+                codes = work.tile([P, G, P], U32, name="l_codes", bufs=1, align_bytes=64)
+                scales = work.tile([P, G, P], U8, name="l_scales", bufs=1, align_bytes=64)
+                uq[i] = codes, scales
+            codes, scales = uq[i]
+            nc.vector.quantize_mx(
+                out=codes[:, g, :].bitcast(FP8X4),
+                scales=scales[:, g, :],
+                in_=u[i // 2][:, i % 2, g].rearrange("p f t -> p (f t)"),
+            )
+
+        def last_products(i, g):
+            codes, scales = uq[i]
+            if g == 0:
+                p_bank[i] = psum.tile([P, 4, P], F32, name="d_bank", tag="h", bufs=H_BANKS)
+                r_bank[i] = psum.tile([P, C], F32, name="r_bank", tag="r", bufs=R_BANKS)
+            for t in range(4):
+                nc.tensor.matmul_mx(
+                    out=p_bank[i][:, t, :],
+                    lhsT=e_codes[:, g, t * P : (t + 1) * P].bitcast(FP8X4),
+                    lhsT_scale=e_scales[:, g, t * P : (t + 1) * P],
+                    rhs=codes[:, g, :].bitcast(FP8X4),
+                    rhs_scale=scales[:, g, :],
+                    start=(g == 0 and t == 0),
+                    stop=(g == G - 1 and t == 3),
+                )
+            nc.tensor.matmul_mx(
+                out=r_bank[i][:],
+                lhsT=codes[:, g, :].bitcast(FP8X4),
+                lhsT_scale=scales[:, g, :],
+                rhs=e_codes[:, g, :].bitcast(FP8X4),
+                rhs_scale=e_scales[:, g, :],
+                start=(g == 0),
+                stop=(g == G - 1),
+            )
+
+        def half_exit(copy, i, h):
+            dst = r_out[i // 2][:, i % 2, h * 2 * P : (h + 1) * 2 * P]
+            src = r_bank[i][:].rearrange("p (t m) -> p m t", t=4)[:, h * P // 2 : (h + 1) * P // 2]
+            copy(out=dst.rearrange("p (m t) -> p m t", t=4), in_=src)
+            nc.sync.dma_start(out=out_0[i * P : (i + 1) * P, h * 2 * P : (h + 1) * 2 * P], in_=dst)
+
         r_bf = {}
-        p_bank = {}
         p_bf = {}
 
-        def p_cast(copy, i, n):
-            r_bf[i] = work.tile([P, 2, n * P, 2], BF16, name="r_bf", bufs=3)
+        def p_cast(copy, i, n, tag="r_bf", bufs=4):
+            cast = work.tile([P, 2, n * P, 2], BF16, name=tag, bufs=bufs, align_bytes=64)
             src = r_out[i // 2][:, i % 2 : i % 2 + n, :]
-            copy(out=r_bf[i][:], in_=src.rearrange("p n (m v c) -> p v (n m) c", v=2, c=2))
+            copy(out=cast[:], in_=src.rearrange("p n (m v c) -> p v (n m) c", v=2, c=2))
+            words = cast[:].rearrange("p v m c -> p (v m c)").bitcast(F32)
+            for m in range(n):
+                r_bf[i + m] = [words[:, (n * v + m) * P : (n * v + m + 1) * P] for v in range(2)]
 
         def p_turn(i, n, tag="p", bufs=P_BANKS):
-            words = r_bf[i][:].rearrange("p v m c -> p (v m c)").bitcast(F32)
             p_bank[i] = psum.tile([P, n, 2, P], F32, name="p_bank", tag=tag, bufs=bufs)
             for m in range(n):
                 for v in range(2):
-                    at = (n * v + m) * P
-                    nc.tensor.transpose(p_bank[i][:, m, v, :], words[:, at : at + P], ident[:])
+                    nc.tensor.transpose(p_bank[i][:, m, v, :], r_bf[i + m][v], ident[:])
 
         def p_exit(copy, i, n):
             p_bf[i] = work.tile([P, n * P, 4], BF16, name="p_bf", bufs=4, align_bytes=64)
@@ -369,10 +413,10 @@ def tile_convnextdroppathlayerscaleweightgrad_x1_kernel(tc, x, w1, b1, r, dy, ga
         h_product(1, 0)
         gelu(0, 0)
         e_mult(1)
-        h_product(0, 1)
+        h_product(0, 1, "r", R_BANKS)
         gelu(1, 0)
         w_quant(2, 1)
-        h_product(1, 1)
+        h_product(1, 1, "r", R_BANKS)
         gelu(0, 1)
         w_quant(3, 1)
         turn(0, 0)
@@ -388,18 +432,18 @@ def tile_convnextdroppathlayerscaleweightgrad_x1_kernel(tc, x, w1, b1, r, dy, ga
         h_product(2, 1)
         gelu(2, 1)
         u_mult(0, 0)
-        h_product(3, 0)
+        h_product(3, 0, "r", R_BANKS)
         e_group(scopy, 1, 1)
         u_mult(0, 1)
-        h_product(3, 1)
+        h_product(3, 1, "r", R_BANKS)
         gelu(3, 0)
         e_group(vcopy, 1, 0)
         turn(1, 0)
         gelu(3, 1)
-        e_quant(0)
-        turn(1, 1)
         w_quant(5, 1)
         w_group(gcopy, 6, 1)
+        turn(1, 1)
+        e_quant(0)
         h_product(4, 0)
         gelu(4, 0)
         u_mult(1, 0)
@@ -408,200 +452,204 @@ def tile_convnextdroppathlayerscaleweightgrad_x1_kernel(tc, x, w1, b1, r, dy, ga
         u_mult(1, 1)
         turn(2, 0)
         e_quant(1)
-        turn(2, 1)
-        u_quant(0, 1)
-        h_product(5, 0)
+        h_product(5, 0, "r", R_BANKS)
         gelu(5, 0)
         w_quant(6, 1)
         w_group(gcopy, 7, 1)
-        h_product(5, 1)
+        h_product(5, 1, "p", P_BANKS)
         gelu(5, 1)
+        u_quant(0, 1)
+        turn(2, 1)
         u_mult(2, 0)
-        r_product(0)
-        r_exit(scopy, 0)
-        u_mult(2, 1)
-        turn(3, 0)
-        u_quant(1, 1)
-        turn(3, 1)
-        w_quant(7, 1)
-        w_group(gcopy, 8, 1)
         h_product(6, 0)
         gelu(6, 0)
-        u_mult(3, 0)
+        u_mult(2, 1)
         h_product(6, 1)
         gelu(6, 1)
+        w_quant(7, 1)
+        w_group(gcopy, 8, 1)
+        r_product(0)
+        r_exit(scopy, 0)
+        u_quant(1, 1)
+        turn(3, 0)
+        u_mult(3, 0)
+        turn(3, 1)
         u_mult(3, 1)
-        r_product(1)
-        r_exit(scopy, 1)
-        u_quant(2, 1)
-        turn(4, 0)
-        u_quant(3, 1)
-        turn(4, 1)
-        w_quant(8, 1)
-        w_group(gcopy, 9, 1)
         h_product(7, 0)
         gelu(7, 0)
-        u_mult(4, 0)
+        u_quant(2, 1)
         h_product(7, 1)
         gelu(7, 1)
+        w_quant(8, 1)
+        w_group(gcopy, 9, 1)
+        r_product(1)
+        r_exit(scopy, 1)
+        u_quant(3, 1)
+        turn(4, 0)
+        u_mult(4, 0)
+        turn(4, 1)
         u_mult(4, 1)
-        r_product(2)
-        r_exit(scopy, 2)
-        p_cast(vcopy, 0, 2)
-        turn(5, 0)
-        w_quant(9, 1)
-        w_group(gcopy, 10, 1)
-        turn(5, 1)
-        u_mult(5, 0)
         h_product(8, 0)
         gelu(8, 0)
-        u_mult(5, 1)
+        w_quant(9, 1)
+        w_group(gcopy, 10, 1)
         h_product(8, 1)
         gelu(8, 1)
+        p_cast(vcopy, 0, 2)
+        r_product(2)
+        r_exit(scopy, 2)
+        turn(5, 0)
+        u_mult(5, 0)
+        turn(5, 1)
+        u_mult(5, 1)
+        h_product(9, 0)
+        gelu(9, 0)
         u_quant(4, 1)
+        h_product(9, 1)
+        gelu(9, 1)
+        w_quant(10, 1)
+        w_group(gcopy, 11, 1)
         r_product(3)
         r_exit(scopy, 3)
         u_quant(5, 1)
         turn(6, 0)
-        w_quant(10, 1)
-        w_group(gcopy, 11, 1)
-        turn(6, 1)
         u_mult(6, 0)
+        turn(6, 1)
+        u_mult(6, 1)
         p_turn(0, 2)
         p_exit(scopy, 0, 2)
-        u_mult(6, 1)
-        h_product(9, 0)
-        gelu(9, 0)
-        p_cast(vcopy, 2, 2)
-        h_product(9, 1)
-        gelu(9, 1)
         w_quant(11, 1)
         w_group(gcopy, 12, 1)
+        h_product(10, 0)
+        gelu(10, 0)
+        p_cast(vcopy, 2, 2)
+        h_product(10, 1)
+        gelu(10, 1)
         r_product(4)
         r_exit(scopy, 4)
         turn(7, 0)
         u_mult(7, 0)
         turn(7, 1)
         u_mult(7, 1)
-        h_product(10, 0)
-        gelu(10, 0)
+        h_product(11, 0)
+        gelu(11, 0)
         p_quant(0, 2)
-        h_product(10, 1)
-        gelu(10, 1)
-        u_quant(6, 2)
-        r_product(5)
-        r_exit(scopy, 5)
+        h_product(11, 1)
+        gelu(11, 1)
         w_quant(12, 1)
         w_group(gcopy, 13, 1)
+        r_product(5)
+        r_exit(scopy, 5)
+        u_quant(6, 2)
         turn(8, 0)
         u_mult(8, 0)
         turn(8, 1)
         u_mult(8, 1)
         p_turn(2, 2)
         p_exit(scopy, 2, 2)
-        p_cast(vcopy, 4, 2)
-        h_product(11, 0)
-        gelu(11, 0)
         w_quant(13, 1)
         w_group(gcopy, 14, 1)
-        h_product(11, 1)
-        gelu(11, 1)
+        h_product(12, 0)
+        gelu(12, 0)
+        p_cast(vcopy, 4, 2)
+        h_product(12, 1)
+        gelu(12, 1)
         r_product(6)
         r_exit(scopy, 6)
         turn(9, 0)
         u_mult(9, 0)
         turn(9, 1)
         u_mult(9, 1)
-        h_product(12, 0)
-        gelu(12, 0)
+        h_product(13, 0)
+        gelu(13, 0)
         p_quant(2, 2)
-        h_product(12, 1)
-        gelu(12, 1)
-        u_quant(8, 2)
-        r_product(7)
-        r_exit(scopy, 7)
+        h_product(13, 1)
+        gelu(13, 1)
         w_quant(14, 1)
         w_group(gcopy, 15, 1)
+        r_product(7)
+        r_exit(scopy, 7)
+        u_quant(8, 2)
         turn(10, 0)
         u_mult(10, 0)
         turn(10, 1)
         u_mult(10, 1)
         p_turn(4, 2)
         p_exit(scopy, 4, 2)
-        p_cast(vcopy, 6, 2)
-        h_product(13, 0)
-        gelu(13, 0)
         w_quant(15, 1)
-        h_product(13, 1)
-        gelu(13, 1)
+        h_product(14, 0)
+        gelu(14, 0)
+        p_cast(vcopy, 6, 2)
+        h_product(14, 1)
+        gelu(14, 1)
         r_product(8)
         r_exit(scopy, 8)
         turn(11, 0)
         u_mult(11, 0)
         turn(11, 1)
         u_mult(11, 1)
-        h_product(14, 0)
-        gelu(14, 0)
+        h_product(15, 0)
+        gelu(15, 0)
         p_quant(4, 2)
-        h_product(14, 1)
-        gelu(14, 1)
+        h_product(15, 1)
+        gelu(15, 1)
         u_quant(10, 2)
         r_product(9)
         r_exit(scopy, 9)
         turn(12, 0)
         u_mult(12, 0)
+        p_cast(gcopy, 8, 2, "u_bf", 2)
         turn(12, 1)
         u_mult(12, 1)
         p_turn(6, 2)
         p_exit(scopy, 6, 2)
-        p_cast(vcopy, 8, 2)
-        h_product(15, 0)
-        gelu(15, 0)
-        u_quant(12, 1)
-        h_product(15, 1)
-        gelu(15, 1)
-        r_product(10)
-        r_exit(scopy, 10)
         turn(13, 0)
         u_mult(13, 0)
+        r_product(10)
+        r_exit(scopy, 10)
+        u_quant(12, 1)
         turn(13, 1)
         u_mult(13, 1)
+        turn(14, 0, "h", H_BANKS)
+        p_quant(6, 2)
         r_product(11)
         r_exit(scopy, 11)
-        p_quant(6, 2)
-        turn(14, 0)
-        p_cast(scopy, 10, 2)
         u_quant(13, 1)
-        turn(14, 1)
-        u_mult(14, 0)
+        p_cast(gcopy, 10, 2, "u_bf", 2)
+        turn(14, 1, "h", H_BANKS)
         p_turn(8, 2)
         p_exit(scopy, 8, 2)
-        u_mult(14, 1)
-        turn(15, 0)
-        u_mult(15, 0)
+        u_mult(14, 0)
         r_product(12)
         r_exit(scopy, 12)
+        u_mult(14, 1)
+        turn(15, 0)
+        p_cast(scopy, 12, 1)
+        u_mult(15, 0)
+        turn(15, 1)
         u_quant(14, 1)
-        turn(15, 1, "h", H_BANKS)
-        u_mult(15, 1)
         r_product(13)
         r_exit(scopy, 13)
-        p_cast(vcopy, 12, 2)
+        u_mult(15, 1)
         p_turn(10, 2)
         p_exit(scopy, 10, 2)
-        u_quant(15, 1)
+        last_quant(15, 0)
         r_product(14)
         r_exit(scopy, 14)
-        p_quant(8, 2)
-        p_product(14)
-        d_exit(scopy, 14)
-        p_quant(10, 2)
-        p_turn(12, 2)
-        p_exit(scopy, 12, 2)
-        p_quant(14, 1)
-        p_product(15)
+        last_quant(15, 1)
+        last_products(15, 0)
+        p_cast(vcopy, 13, 1)
+        last_products(15, 1)
         d_exit(scopy, 15)
-        p_quant(12, 2)
-        r_product(15)
-        r_exit(vcopy, 15)
+        p_quant(8, 2)
+        p_turn(12, 2, "t", T_BANKS)
+        p_exit(scopy, 12, 2)
+        p_quant(10, 2)
+        p_cast(vcopy, 14, 1)
+        p_turn(14, 1, "t", T_BANKS)
+        p_exit(scopy, 14, 1)
+        half_exit(vcopy, 15, 0)
+        half_exit(vcopy, 15, 1)
         p_quant(15, 1)
+        p_quant(12, 2)
+        p_quant(14, 1)

@@ -19,13 +19,10 @@ ADD = mybir.AluOpType.add
 P = 128
 G = N // 512
 TILES = F // P
-W_LOADS = ((0, 2), (2, 4), (4, 8), (8, 12), (12, 16))
-H_BANKS, T_BANKS, R_BANKS, P_BANKS = 2, 3, 2, 1
-A_BUFS = 10
-W_BUFS = 4
-G_FIRST = 5
-WORD_STORES = {2: (0, 4), 6: (4, 8), 10: (8, 12), 14: (12, 16)}
-SCALE_STORES = {4: (0, 6), 14: (6, 16)}
+PAIRS = TILES // 2
+W_LOADS = ((0, 2), (2, 4), (4, 6), (6, 8))
+BANKS = 8
+A_BUFS = 12
 
 
 def tile_convnextdroppathlayerscaleweightgrad_x1_kernel(tc, x, w1, b1, r, dy, gamma, out_0, out_1, out_2):
@@ -50,19 +47,22 @@ def tile_convnextdroppathlayerscaleweightgrad_x1_kernel(tc, x, w1, b1, r, dy, ga
         x_codes = keep.tile([P, G, 512], U32, name="x_codes", align_bytes=64)
         x_scales = keep.tile([P, G, 512], U8, name="x_scales", align_bytes=64)
         w_raw = {}
-        for i0, i1 in W_LOADS:
-            raw = keep.tile([P, 4, (i1 - i0) * P], BF16, name=f"w_raw{i0}")
-            for i in range(i0, i1):
-                w_raw[i] = raw, i - i0
+        for j0, j1 in W_LOADS:
+            raw = keep.tile([P, 4, (j1 - j0) * 2 * P], BF16, name=f"w_raw{j0}")
+            for j in range(j0, j1):
+                w_raw[j] = raw, j - j0
         w_codes = keep.tile([P, F], U32, name="w_codes", align_bytes=64)
         w_scales = keep.tile([P, F], U8, name="w_scales", align_bytes=64)
-        dy_raw = [keep.tile([P, 4, C], BF16, name=f"dy_raw{g}") for g in range(G)]
+        dy_raw = {(g, h): keep.tile([P, 2, C], BF16, name=f"dy_raw{g}{h}") for g in range(G) for h in range(2)}
         e_nat = [keep.tile([P, 2, 4, P, 2], BF16, name=f"e_nat{g}") for g in range(G)]
         e_bf = [keep.tile([P, C, 4], BF16, name=f"e_bf{g}", align_bytes=64) for g in range(G)]
         e_codes = keep.tile([P, G, C], U32, name="e_codes", align_bytes=64)
         e_scales = keep.tile([P, G, C], U8, name="e_scales", align_bytes=64)
         p_codes = keep.tile([P, F], U32, name="p_codes", align_bytes=64)
         p_scales = keep.tile([P, F], U8, name="p_scales", align_bytes=64)
+
+        def new_bank(shape, dtype, name):
+            return psum.tile(shape, dtype, name=name, tag="bank", bufs=BANKS)
 
         def gcopy(out, in_):
             nc.gpsimd.tensor_scalar(out=out, in0=in_, scalar1=1.0, scalar2=0.0, op0=MULT, op1=ADD)
@@ -71,19 +71,19 @@ def tile_convnextdroppathlayerscaleweightgrad_x1_kernel(tc, x, w1, b1, r, dy, ga
             src = x[512 * g : 512 * g + 512, :].rearrange("(m h t) k -> m h (t k)", h=2, t=2)
             nc.sync.dma_start(out=x_raw[g, h][:], in_=src[:, h, :])
 
-        def load_w(i0, i1):
-            c = slice(i0 * P, i1 * P)
-            nc.sync.dma_start(out=w_raw[i0][0][:], in_=w1[:, c].rearrange("(p j) f -> p j f", j=4))
+        def load_w(j0, j1):
+            c = slice(j0 * 2 * P, j1 * 2 * P)
+            nc.sync.dma_start(out=w_raw[j0][0][:], in_=w1[:, c].rearrange("(p j) f -> p j f", j=4))
 
-        def load_dy(g):
+        def load_dy(g, h):
             src = dy[512 * g : 512 * g + 512, :].rearrange("(p j) c -> p j c", j=4)
-            nc.sync.dma_start(out=dy_raw[g][:], in_=src)
+            nc.sync.dma_start(out=dy_raw[g, h][:], in_=src[:, 2 * h : 2 * h + 2, :])
 
         x_turned = {}
 
         def x_turn(g, h):
             words = x_raw[g, h][:].bitcast(F32)
-            x_turned[g, h] = psum.tile([P, 2, 2, P], F32, name="x_bank", tag="t", bufs=T_BANKS)
+            x_turned[g, h] = new_bank([P, 2, 2, P], F32, "x_bank")
             for n in range(2):
                 for u in range(2):
                     nc.tensor.transpose(x_turned[g, h][:, n, u, :], words[:, 256 * n + u : 256 * (n + 1) : 2], ident[:])
@@ -105,14 +105,14 @@ def tile_convnextdroppathlayerscaleweightgrad_x1_kernel(tc, x, w1, b1, r, dy, ga
         small = {}
 
         def bias_turn():
-            small["b"] = psum.tile([P, P], BF16, name="b_bank", tag="r", bufs=R_BANKS)
+            small["b"] = new_bank([P, P], BF16, "b_bank")
             nc.tensor.transpose(small["b"][:], b_rows[:], ident_bf[:])
 
         def bias_exit(copy):
             copy(out=bias[:], in_=small["b"][:, 0:TILES])
 
         def gamma_turn():
-            bank = small["g"] = psum.tile([P, 2, P], F32, name="g_bank", tag="p", bufs=P_BANKS)
+            bank = small["g"] = new_bank([P, 2, P], F32, "g_bank")
             words = gcols[:].bitcast(F32)
             for u in range(2):
                 nc.tensor.transpose(bank[:, u, :], words[:, u : u + 1].to_broadcast([P, P]), ident[:])
@@ -122,34 +122,28 @@ def tile_convnextdroppathlayerscaleweightgrad_x1_kernel(tc, x, w1, b1, r, dy, ga
 
         w_bf = {}
 
-        def w_group(copy, i, n):
-            raw, at = w_raw[i]
+        def w_group(copy, j, tag="w_bf", bufs=3):
+            raw, at = w_raw[j]
+            w_bf[j] = work.tile([P, 2 * P, 4], BF16, name=tag, bufs=bufs, align_bytes=64)
+            src = raw[:, :, at * 2 * P : (at + 1) * 2 * P]
             if copy is gcopy:
-                w_bf[i] = work.tile([P, P, 4], BF16, name="w_one", bufs=1, align_bytes=64)
-                gcopy(out=w_bf[i][:], in_=raw[:, :, at * P : (at + 1) * P].rearrange("p j c -> p c j"))
-                return
-            if i == G_FIRST - 1:
-                w_bf[i] = work.tile([P, P, 4], BF16, name="w_one", bufs=1, align_bytes=64)
+                gcopy(out=w_bf[j][:], in_=src.rearrange("p j c -> p c j"))
             else:
-                w_bf[i] = work.tile([P, n * P, 4], BF16, name="w_bf", bufs=W_BUFS, align_bytes=64)
-            copy(
-                out=w_bf[i][:].rearrange("p (c q) j -> p c j q", q=4),
-                in_=raw[:, :, at * P : (at + n) * P].rearrange("p j (c q) -> p c j q", q=4),
-            )
+                copy(out=w_bf[j][:].rearrange("p (c q) j -> p c j q", q=4), in_=src.rearrange("p j (c q) -> p c j q", q=4))
 
-        def w_quant(i, n):
-            c = slice(i * P, (i + n) * P)
+        def w_quant(j):
+            c = slice(j * 2 * P, (j + 1) * 2 * P)
             nc.vector.quantize_mx(
                 out=w_codes[:, c].bitcast(FP8X4),
                 scales=w_scales[:, c],
-                in_=w_bf[i][:].rearrange("p c j -> p (c j)"),
+                in_=w_bf[j][:].rearrange("p c j -> p (c j)"),
             )
 
-        def e_mult(g):
+        def e_mult(g, h):
             nc.vector.tensor_tensor(
-                out=e_nat[g][:],
-                in0=dy_raw[g][:].rearrange("p j (m v c) -> p v j m c", v=2, c=2),
-                in1=gam[:].rearrange("p (v m c) -> p v m c", v=2, c=2).unsqueeze(2).to_broadcast([P, 2, 4, P, 2]),
+                out=e_nat[g][:, :, 2 * h : 2 * h + 2],
+                in0=dy_raw[g, h][:].rearrange("p j (m v c) -> p v j m c", v=2, c=2),
+                in1=gam[:].rearrange("p (v m c) -> p v m c", v=2, c=2).unsqueeze(2).to_broadcast([P, 2, 2, P, 2]),
                 op=MULT,
             )
 
@@ -167,11 +161,10 @@ def tile_convnextdroppathlayerscaleweightgrad_x1_kernel(tc, x, w1, b1, r, dy, ga
             )
 
         a = {}
-
         h_bank = {}
 
-        def h_product(i, g, tag="h", bufs=H_BANKS):
-            bank = h_bank[i, g] = psum.tile([P, 512], F32, name="h_bank", tag=tag, bufs=bufs)
+        def h_product(i, g):
+            bank = h_bank[i, g] = new_bank([P, 512], F32, "h_bank")
             c = slice(i * P, (i + 1) * P)
             nc.tensor.matmul_mx(
                 out=bank[:],
@@ -190,8 +183,8 @@ def tile_convnextdroppathlayerscaleweightgrad_x1_kernel(tc, x, w1, b1, r, dy, ga
         turned = {}
         u = {}
 
-        def turn(i, g, tag="t", bufs=T_BANKS):
-            turned[i, g] = psum.tile([P, 4, P], F32, name="t_bank", tag=tag, bufs=bufs)
+        def turn(i, g):
+            turned[i, g] = new_bank([P, 4, P], F32, "t_bank")
             for t in range(4):
                 nc.tensor.transpose(turned[i, g][:, t, :], a[i, g][:, t * P : (t + 1) * P], ident[:])
 
@@ -208,8 +201,8 @@ def tile_convnextdroppathlayerscaleweightgrad_x1_kernel(tc, x, w1, b1, r, dy, ga
         uq = {}
 
         def u_quant(i, n):
-            codes = work.tile([P, n, G, P], U32, name="u_codes", bufs=6, align_bytes=64)
-            scales = work.tile([P, n, G, P], U8, name="u_scales", bufs=6, align_bytes=64)
+            codes = work.tile([P, n, G, P], U32, name="u_codes", bufs=4, align_bytes=64)
+            scales = work.tile([P, n, G, P], U8, name="u_scales", bufs=4, align_bytes=64)
             nc.vector.quantize_mx(
                 out=codes[:].rearrange("p n g f -> p (n g f)").bitcast(FP8X4),
                 scales=scales[:].rearrange("p n g f -> p (n g f)"),
@@ -224,7 +217,7 @@ def tile_convnextdroppathlayerscaleweightgrad_x1_kernel(tc, x, w1, b1, r, dy, ga
 
         def r_product(i):
             codes, scales = uq[i]
-            r_bank[i] = psum.tile([P, C], F32, name="r_bank", tag="r", bufs=R_BANKS)
+            r_bank[i] = new_bank([P, C], F32, "r_bank")
             for g in range(G):
                 nc.tensor.matmul_mx(
                     out=r_bank[i][:],
@@ -237,7 +230,7 @@ def tile_convnextdroppathlayerscaleweightgrad_x1_kernel(tc, x, w1, b1, r, dy, ga
                 )
 
         def r_exit(copy, i):
-            if i % 2 == 0:
+            if i // 2 not in r_out:
                 r_out[i // 2] = work.tile([P, 2, C], F32, name="r_out", bufs=4)
             dst = r_out[i // 2][:, i % 2, :]
             copy(
@@ -245,21 +238,6 @@ def tile_convnextdroppathlayerscaleweightgrad_x1_kernel(tc, x, w1, b1, r, dy, ga
                 in_=r_bank[i][:].rearrange("p (t m) -> p m t", t=4),
             )
             nc.sync.dma_start(out=out_0[i * P : (i + 1) * P, :], in_=dst)
-
-        def r_half(i, h):
-            codes, scales = uq[i]
-            r_bank[i, h] = psum.tile([P, 2, P], F32, name="r_half", tag="t", bufs=T_BANKS)
-            c = slice(2 * h * P, 2 * (h + 1) * P)
-            for g in range(G):
-                nc.tensor.matmul_mx(
-                    out=r_bank[i, h][:].rearrange("p t m -> p (t m)"),
-                    lhsT=codes[:, g, :].bitcast(FP8X4),
-                    lhsT_scale=scales[:, g, :],
-                    rhs=e_codes[:, g, c].bitcast(FP8X4),
-                    rhs_scale=e_scales[:, g, c],
-                    start=(g == 0),
-                    stop=(g == G - 1),
-                )
 
         def last_quant(i, g):
             if g == 0:
@@ -273,11 +251,10 @@ def tile_convnextdroppathlayerscaleweightgrad_x1_kernel(tc, x, w1, b1, r, dy, ga
                 in_=u[i // 2][:, i % 2, g].rearrange("p f t -> p (f t)"),
             )
 
-        def last_products(i, g):
+        def p_product(i, g):
             codes, scales = uq[i]
             if g == 0:
-                p_bank[i] = psum.tile([P, 4, P], F32, name="d_bank", tag="h", bufs=H_BANKS)
-                r_bank[i] = psum.tile([P, C], F32, name="r_bank", tag="r", bufs=R_BANKS)
+                p_bank[i] = new_bank([P, 4, P], F32, "d_bank")
             for t in range(4):
                 nc.tensor.matmul_mx(
                     out=p_bank[i][:, t, :],
@@ -288,35 +265,20 @@ def tile_convnextdroppathlayerscaleweightgrad_x1_kernel(tc, x, w1, b1, r, dy, ga
                     start=(g == 0 and t == 0),
                     stop=(g == G - 1 and t == 3),
                 )
-            nc.tensor.matmul_mx(
-                out=r_bank[i][:],
-                lhsT=codes[:, g, :].bitcast(FP8X4),
-                lhsT_scale=scales[:, g, :],
-                rhs=e_codes[:, g, :].bitcast(FP8X4),
-                rhs_scale=e_scales[:, g, :],
-                start=(g == 0),
-                stop=(g == G - 1),
-            )
-
-        def half_exit(copy, i, h):
-            dst = r_out[i // 2][:, i % 2, h * 2 * P : (h + 1) * 2 * P]
-            src = r_bank[i][:].rearrange("p (t m) -> p m t", t=4)[:, h * P // 2 : (h + 1) * P // 2]
-            copy(out=dst.rearrange("p (m t) -> p m t", t=4), in_=src)
-            nc.sync.dma_start(out=out_0[i * P : (i + 1) * P, h * 2 * P : (h + 1) * 2 * P], in_=dst)
 
         r_bf = {}
         p_bf = {}
 
-        def p_cast(copy, i, n, tag="r_bf", bufs=4):
-            cast = work.tile([P, 2, n * P, 2], BF16, name=tag, bufs=bufs, align_bytes=64)
+        def p_cast(copy, i, n, tag="r_one"):
+            cast = work.tile([P, 2, n * P, 2], BF16, name=tag, bufs=1, align_bytes=64)
             src = r_out[i // 2][:, i % 2 : i % 2 + n, :]
             copy(out=cast[:], in_=src.rearrange("p n (m v c) -> p v (n m) c", v=2, c=2))
             words = cast[:].rearrange("p v m c -> p (v m c)").bitcast(F32)
             for m in range(n):
                 r_bf[i + m] = [words[:, (n * v + m) * P : (n * v + m + 1) * P] for v in range(2)]
 
-        def p_turn(i, n, tag="p", bufs=P_BANKS):
-            p_bank[i] = psum.tile([P, n, 2, P], F32, name="p_bank", tag=tag, bufs=bufs)
+        def p_turn(i, n):
+            p_bank[i] = new_bank([P, n, 2, P], F32, "p_bank")
             for m in range(n):
                 for v in range(2):
                     nc.tensor.transpose(p_bank[i][:, m, v, :], r_bf[i + m][v], ident[:])
@@ -325,21 +287,6 @@ def tile_convnextdroppathlayerscaleweightgrad_x1_kernel(tc, x, w1, b1, r, dy, ga
             p_bf[i] = work.tile([P, n * P, 4], BF16, name="p_bf", bufs=4, align_bytes=64)
             dst = p_bf[i][:].rearrange("p f c -> p (f c)").bitcast(F32)
             copy(out=dst.rearrange("p (n f v) -> p n f v", n=n, v=2), in_=p_bank[i][:].rearrange("p n v f -> p n f v"))
-
-        def p_product(i):
-            codes, scales = uq[i]
-            p_bank[i] = psum.tile([P, 4, P], F32, name="d_bank", tag="h", bufs=H_BANKS)
-            for t in range(4):
-                for g in range(G):
-                    nc.tensor.matmul_mx(
-                        out=p_bank[i][:, t, :],
-                        lhsT=e_codes[:, g, t * P : (t + 1) * P].bitcast(FP8X4),
-                        lhsT_scale=e_scales[:, g, t * P : (t + 1) * P],
-                        rhs=codes[:, g, :].bitcast(FP8X4),
-                        rhs_scale=scales[:, g, :],
-                        start=(g == 0),
-                        stop=(g == G - 1),
-                    )
 
         def d_exit(copy, i):
             p_bf[i] = work.tile([P, P, 4], BF16, name="p_bf", bufs=4, align_bytes=64)
@@ -366,290 +313,163 @@ def tile_convnextdroppathlayerscaleweightgrad_x1_kernel(tc, x, w1, b1, r, dy, ga
                 scales=p_scales[:, c],
                 in_=p_bf[i][:].rearrange("p f c -> p (f c)"),
             )
-            if i in WORD_STORES:
-                store_words(*WORD_STORES[i])
-            if i in SCALE_STORES:
-                store_scales(*SCALE_STORES[i])
+
+        def halves(j):
+            return [(2 * j + m, g) for m in range(2) for g in range(G)]
+
+        def stage1(j):
+            for i, g in halves(j):
+                h_product(i, g)
+                gelu(i, g)
+
+        def stage2(j):
+            for i in (2 * j, 2 * j + 1):
+                r_product(i)
+                r_exit(scopy, i)
+
+        def turns(j):
+            for i, g in halves(j):
+                turn(i, g)
+                u_mult(i, g)
 
         nc.vector.memset(warm[:], 0.0)
         nc.vector.memset(b_rows[:], 0.0)
         make_identity(nc, ident[:])
         make_identity(nc, ident_bf[:])
         nc.scalar.activation(out=warm[:], in_=warm[:], func=GELU)
-        nc.sync.dma_start(out=gcols[:], in_=gamma.rearrange("(k q) -> k q", q=4))
+
+        def load_gamma():
+            nc.sync.dma_start(out=gcols[:], in_=gamma.rearrange("(k q) -> k q", q=4))
+
+        def load_bias():
+            nc.sync.dma_start(out=b_rows[0:TILES, :], in_=b1.rearrange("(i f) -> i f", f=P))
+
+        def load_r():
+            nc.sync.dma_start(out=r_sb[:], in_=r.rearrange("(g p t) -> p g t", g=G, t=4))
+
+        load_gamma()
+        load_dy(0, 0)
         load_x(0, 0)
+        load_dy(0, 1)
         load_x(0, 1)
         load_w(*W_LOADS[0])
-        nc.sync.dma_start(out=b_rows[0:TILES, :], in_=b1.rearrange("(i f) -> i f", f=P))
+        load_bias()
         load_x(1, 0)
         load_x(1, 1)
-        load_dy(0)
+        load_dy(1, 0)
+        load_dy(1, 1)
+        load_r()
         load_w(*W_LOADS[1])
-        load_dy(1)
-        nc.sync.dma_start(out=r_sb[:], in_=r.rearrange("(g p t) -> p g t", g=G, t=4))
         load_w(*W_LOADS[2])
         load_w(*W_LOADS[3])
-        load_w(*W_LOADS[4])
+
         gamma_turn()
         gamma_exit(scopy)
-        w_group(vcopy, 0, 2)
+        e_mult(0, 0)
+        e_mult(0, 1)
         x_turn(0, 0)
         x_exit(scopy, 0, 0)
-        w_quant(0, 2)
+        e_group(scopy, 0, 0)
+        e_group(vcopy, 0, 1)
         x_turn(0, 1)
         x_exit(scopy, 0, 1)
-        x_quant(0)
+        w_group(vcopy, 0)
         bias_turn()
         bias_exit(scopy)
-        e_mult(0)
+        w_group(scopy, 1)
+        e_quant(0)
+        w_quant(0)
+        x_quant(0)
         x_turn(1, 0)
         x_exit(scopy, 1, 0)
         x_turn(1, 1)
         x_exit(scopy, 1, 1)
+        e_mult(1, 0)
+        w_quant(1)
+        e_mult(1, 1)
         x_quant(1)
-        h_product(0, 0)
-        w_group(scopy, 2, 1)
-        w_group(vcopy, 3, 1)
-        h_product(1, 0)
-        gelu(0, 0)
-        e_mult(1)
-        h_product(0, 1, "r", R_BANKS)
-        gelu(1, 0)
-        w_quant(2, 1)
-        h_product(1, 1, "r", R_BANKS)
-        gelu(0, 1)
-        w_quant(3, 1)
-        turn(0, 0)
-        gelu(1, 1)
-        e_group(vcopy, 0, 0)
-        turn(0, 1)
-        w_group(scopy, 4, 1)
-        e_group(vcopy, 0, 1)
-        h_product(2, 0)
-        gelu(2, 0)
-        w_quant(4, 1)
-        w_group(gcopy, 5, 1)
-        h_product(2, 1)
-        gelu(2, 1)
-        u_mult(0, 0)
-        h_product(3, 0, "r", R_BANKS)
-        e_group(scopy, 1, 1)
-        u_mult(0, 1)
-        h_product(3, 1, "r", R_BANKS)
-        gelu(3, 0)
-        e_group(vcopy, 1, 0)
-        turn(1, 0)
-        gelu(3, 1)
-        w_quant(5, 1)
-        w_group(gcopy, 6, 1)
-        turn(1, 1)
-        e_quant(0)
-        h_product(4, 0)
-        gelu(4, 0)
-        u_mult(1, 0)
-        h_product(4, 1)
-        gelu(4, 1)
-        u_mult(1, 1)
-        turn(2, 0)
-        e_quant(1)
-        h_product(5, 0, "r", R_BANKS)
-        gelu(5, 0)
-        w_quant(6, 1)
-        w_group(gcopy, 7, 1)
-        h_product(5, 1, "p", P_BANKS)
-        gelu(5, 1)
-        u_quant(0, 1)
-        turn(2, 1)
-        u_mult(2, 0)
-        h_product(6, 0)
-        gelu(6, 0)
-        u_mult(2, 1)
-        h_product(6, 1)
-        gelu(6, 1)
-        w_quant(7, 1)
-        w_group(gcopy, 8, 1)
-        r_product(0)
-        r_exit(scopy, 0)
-        u_quant(1, 1)
-        turn(3, 0)
-        u_mult(3, 0)
-        turn(3, 1)
-        u_mult(3, 1)
-        h_product(7, 0)
-        gelu(7, 0)
-        u_quant(2, 1)
-        h_product(7, 1)
-        gelu(7, 1)
-        w_quant(8, 1)
-        w_group(gcopy, 9, 1)
-        r_product(1)
-        r_exit(scopy, 1)
-        u_quant(3, 1)
-        turn(4, 0)
-        u_mult(4, 0)
-        turn(4, 1)
-        u_mult(4, 1)
-        h_product(8, 0)
-        gelu(8, 0)
-        w_quant(9, 1)
-        w_group(gcopy, 10, 1)
-        h_product(8, 1)
-        gelu(8, 1)
-        p_cast(vcopy, 0, 2)
-        r_product(2)
-        r_exit(scopy, 2)
-        turn(5, 0)
-        u_mult(5, 0)
-        turn(5, 1)
-        u_mult(5, 1)
-        h_product(9, 0)
-        gelu(9, 0)
-        u_quant(4, 1)
-        h_product(9, 1)
-        gelu(9, 1)
-        w_quant(10, 1)
-        w_group(gcopy, 11, 1)
-        r_product(3)
-        r_exit(scopy, 3)
-        u_quant(5, 1)
-        turn(6, 0)
-        u_mult(6, 0)
-        turn(6, 1)
-        u_mult(6, 1)
-        p_turn(0, 2)
-        p_exit(scopy, 0, 2)
-        w_quant(11, 1)
-        w_group(gcopy, 12, 1)
-        h_product(10, 0)
-        gelu(10, 0)
-        p_cast(vcopy, 2, 2)
-        h_product(10, 1)
-        gelu(10, 1)
-        r_product(4)
-        r_exit(scopy, 4)
-        turn(7, 0)
-        u_mult(7, 0)
-        turn(7, 1)
-        u_mult(7, 1)
-        h_product(11, 0)
-        gelu(11, 0)
-        p_quant(0, 2)
-        h_product(11, 1)
-        gelu(11, 1)
-        w_quant(12, 1)
-        w_group(gcopy, 13, 1)
-        r_product(5)
-        r_exit(scopy, 5)
-        u_quant(6, 2)
-        turn(8, 0)
-        u_mult(8, 0)
-        turn(8, 1)
-        u_mult(8, 1)
-        p_turn(2, 2)
-        p_exit(scopy, 2, 2)
-        w_quant(13, 1)
-        w_group(gcopy, 14, 1)
-        h_product(12, 0)
-        gelu(12, 0)
-        p_cast(vcopy, 4, 2)
-        h_product(12, 1)
-        gelu(12, 1)
-        r_product(6)
-        r_exit(scopy, 6)
-        turn(9, 0)
-        u_mult(9, 0)
-        turn(9, 1)
-        u_mult(9, 1)
-        h_product(13, 0)
-        gelu(13, 0)
-        p_quant(2, 2)
-        h_product(13, 1)
-        gelu(13, 1)
-        w_quant(14, 1)
-        w_group(gcopy, 15, 1)
-        r_product(7)
-        r_exit(scopy, 7)
-        u_quant(8, 2)
-        turn(10, 0)
-        u_mult(10, 0)
-        turn(10, 1)
-        u_mult(10, 1)
-        p_turn(4, 2)
-        p_exit(scopy, 4, 2)
-        w_quant(15, 1)
-        h_product(14, 0)
-        gelu(14, 0)
-        p_cast(vcopy, 6, 2)
-        h_product(14, 1)
-        gelu(14, 1)
-        r_product(8)
-        r_exit(scopy, 8)
-        turn(11, 0)
-        u_mult(11, 0)
-        turn(11, 1)
-        u_mult(11, 1)
-        h_product(15, 0)
-        gelu(15, 0)
-        p_quant(4, 2)
-        h_product(15, 1)
-        gelu(15, 1)
-        u_quant(10, 2)
-        r_product(9)
-        r_exit(scopy, 9)
-        turn(12, 0)
-        u_mult(12, 0)
-        p_cast(gcopy, 8, 2, "u_bf", 2)
-        turn(12, 1)
-        u_mult(12, 1)
-        p_turn(6, 2)
-        p_exit(scopy, 6, 2)
-        turn(13, 0)
-        u_mult(13, 0)
-        r_product(10)
-        r_exit(scopy, 10)
-        u_quant(12, 1)
-        turn(13, 1)
-        u_mult(13, 1)
-        turn(14, 0, "h", H_BANKS)
-        p_quant(6, 2)
-        r_product(11)
-        r_exit(scopy, 11)
-        u_quant(13, 1)
-        p_cast(gcopy, 10, 2, "u_bf", 2)
-        turn(14, 1, "h", H_BANKS)
+        for i in range(4):
+            h_product(i, 0)
+            gelu(i, 0)
+        e_group(vcopy, 1, 1)
+        w_group(vcopy, 2, "w_one", 1)
+        for i in range(4):
+            h_product(i, 1)
+            gelu(i, 1)
+        e_group(scopy, 1, 0)
+        w_quant(2)
+
+        for s in range(PAIRS - 1):
+            if s == 1:
+                stage1(s + 1)
+            if s >= 2:
+                stage2(s - 2)
+            if s >= 2:
+                stage1(s + 1)
+            if s >= 3:
+                p_turn(2 * (s - 3), 2)
+                p_exit(vcopy if s < 5 else scopy, 2 * (s - 3), 2)
+            if s + 3 < PAIRS:
+                w_group(gcopy, s + 3, "w_one", 1)
+            if s >= 2:
+                p_cast(gcopy, 2 * (s - 2), 2 if s > 2 else 1)
+            for i, g in halves(s) if s else [(0, 0), (1, 0), (0, 1), (1, 1)]:
+                turn(i, g)
+                u_mult(i, g)
+            if s == 2:
+                p_cast(vcopy, 1, 1, "r_last")
+            if s >= 3:
+                p_quant(2 * (s - 3), 2)
+            if s == 0:
+                u_quant(0, 2)
+                w_quant(3)
+                e_quant(1)
+            else:
+                if s + 3 < PAIRS:
+                    w_quant(s + 3)
+                u_quant(2 * s, 2)
+            if s == 5:
+                store_words(0, 4)
+
+        stage2(5)
+        store_words(4, 8)
+        store_scales(0, 8)
         p_turn(8, 2)
         p_exit(scopy, 8, 2)
+        p_cast(gcopy, 10, 2)
+        turn(14, 0)
         u_mult(14, 0)
-        r_product(12)
-        r_exit(scopy, 12)
+        turn(14, 1)
         u_mult(14, 1)
         turn(15, 0)
-        p_cast(scopy, 12, 1)
         u_mult(15, 0)
         turn(15, 1)
+        stage2(6)
         u_quant(14, 1)
-        r_product(13)
-        r_exit(scopy, 13)
         u_mult(15, 1)
-        p_turn(10, 2)
-        p_exit(scopy, 10, 2)
         last_quant(15, 0)
+        last_quant(15, 1)
+        p_turn(10, 2)
+        p_cast(vcopy, 12, 2)
+        p_exit(scopy, 10, 2)
         r_product(14)
         r_exit(scopy, 14)
-        last_quant(15, 1)
-        last_products(15, 0)
-        p_cast(vcopy, 13, 1)
-        last_products(15, 1)
-        d_exit(scopy, 15)
+        p_product(15, 0)
+        p_product(15, 1)
+        r_product(15)
         p_quant(8, 2)
-        p_turn(12, 2, "t", T_BANKS)
-        p_exit(scopy, 12, 2)
+        p_cast(vcopy, 14, 1, "r_last")
+        d_exit(scopy, 15)
         p_quant(10, 2)
-        p_cast(vcopy, 14, 1)
-        p_turn(14, 1, "t", T_BANKS)
+        store_words(8, 12)
+        p_turn(12, 2)
+        p_turn(14, 1)
+        r_exit(vcopy, 15)
+        p_exit(scopy, 12, 2)
         p_exit(scopy, 14, 1)
-        half_exit(vcopy, 15, 0)
-        half_exit(vcopy, 15, 1)
         p_quant(15, 1)
         p_quant(12, 2)
+        store_words(12, 14)
         p_quant(14, 1)
+        store_words(14, 16)
+        store_scales(8, 16)

@@ -190,7 +190,7 @@ def tile_convnextdroppathlayerscaleweightgrad_x1_kernel(tc, x, w1, b1, r, dy, ga
 
         def u_mult(i, g):
             if i // 2 not in u:
-                u[i // 2] = work.tile([P, 2, G, P, 4], BF16, name="u_bf", bufs=2, align_bytes=64)
+                u[i // 2] = work.tile([P, 2, G, P, 4], BF16, name="u_bf", bufs=3, align_bytes=64)
             nc.vector.tensor_tensor(
                 out=u[i // 2][:, i % 2, g, :, :],
                 in0=turned[i, g][:].rearrange("p t f -> p f t"),
@@ -269,8 +269,8 @@ def tile_convnextdroppathlayerscaleweightgrad_x1_kernel(tc, x, w1, b1, r, dy, ga
         r_bf = {}
         p_bf = {}
 
-        def p_cast(copy, i, n, tag="r_one"):
-            cast = work.tile([P, 2, n * P, 2], BF16, name=tag, bufs=1, align_bytes=64)
+        def p_cast(copy, i, n, tag="u_bf", bufs=3):
+            cast = work.tile([P, 2, n * P, 2], BF16, name=tag, bufs=bufs, align_bytes=64)
             src = r_out[i // 2][:, i % 2 : i % 2 + n, :]
             copy(out=cast[:], in_=src.rearrange("p n (m v c) -> p v (n m) c", v=2, c=2))
             words = cast[:].rearrange("p v m c -> p (v m c)").bitcast(F32)
@@ -348,8 +348,8 @@ def tile_convnextdroppathlayerscaleweightgrad_x1_kernel(tc, x, w1, b1, r, dy, ga
             nc.sync.dma_start(out=r_sb[:], in_=r.rearrange("(g p t) -> p g t", g=G, t=4))
 
         load_gamma()
-        load_dy(0, 0)
         load_x(0, 0)
+        load_dy(0, 0)
         load_dy(0, 1)
         load_x(0, 1)
         load_w(*W_LOADS[0])
@@ -377,9 +377,9 @@ def tile_convnextdroppathlayerscaleweightgrad_x1_kernel(tc, x, w1, b1, r, dy, ga
         bias_turn()
         bias_exit(scopy)
         w_group(scopy, 1)
-        e_quant(0)
         w_quant(0)
         x_quant(0)
+        e_quant(0)
         x_turn(1, 0)
         x_exit(scopy, 1, 0)
         x_turn(1, 1)
@@ -388,69 +388,74 @@ def tile_convnextdroppathlayerscaleweightgrad_x1_kernel(tc, x, w1, b1, r, dy, ga
         w_quant(1)
         e_mult(1, 1)
         x_quant(1)
-        for i in range(4):
-            h_product(i, 0)
-            gelu(i, 0)
+        h_product(0, 0)
+        gelu(0, 0)
+        h_product(1, 0)
+        gelu(1, 0)
+        h_product(2, 0)
+        gelu(2, 0)
+        h_product(3, 0)
+        gelu(3, 0)
+        e_group(vcopy, 1, 0)
         e_group(vcopy, 1, 1)
         w_group(vcopy, 2, "w_one", 1)
-        for i in range(4):
-            h_product(i, 1)
-            gelu(i, 1)
-        e_group(scopy, 1, 0)
+        e_quant(1)
+        h_product(0, 1)
+        gelu(0, 1)
+        h_product(1, 1)
+        gelu(1, 1)
+        h_product(2, 1)
+        gelu(2, 1)
+        h_product(3, 1)
+        gelu(3, 1)
         w_quant(2)
 
         for s in range(PAIRS - 1):
-            if s == 1:
-                stage1(s + 1)
             if s >= 2:
                 stage2(s - 2)
-            if s >= 2:
+            if s >= 1:
                 stage1(s + 1)
-            if s >= 3:
-                p_turn(2 * (s - 3), 2)
-                p_exit(vcopy if s < 5 else scopy, 2 * (s - 3), 2)
             if s + 3 < PAIRS:
                 w_group(gcopy, s + 3, "w_one", 1)
-            if s >= 2:
-                p_cast(gcopy, 2 * (s - 2), 2 if s > 2 else 1)
             for i, g in halves(s) if s else [(0, 0), (1, 0), (0, 1), (1, 1)]:
                 turn(i, g)
                 u_mult(i, g)
+            if s >= 2:
+                p_cast(gcopy, 2 * (s - 2), 2 if s > 2 else 1)
             if s == 2:
-                p_cast(vcopy, 1, 1, "r_last")
+                p_cast(vcopy, 1, 1, "r_last", 1)
             if s >= 3:
-                p_quant(2 * (s - 3), 2)
-            if s == 0:
-                u_quant(0, 2)
-                w_quant(3)
-                e_quant(1)
-            else:
-                if s + 3 < PAIRS:
-                    w_quant(s + 3)
-                u_quant(2 * s, 2)
+                p_turn(2 * (s - 3), 2)
+                p_exit(vcopy if s < 5 else scopy, 2 * (s - 3), 2)
+            if s >= 4:
+                p_quant(2 * (s - 4), 2)
+            if s + 3 < PAIRS:
+                w_quant(s + 3)
+            u_quant(2 * s, 2)
             if s == 5:
                 store_words(0, 4)
 
         stage2(5)
-        store_words(4, 8)
-        store_scales(0, 8)
-        p_turn(8, 2)
-        p_exit(scopy, 8, 2)
-        p_cast(gcopy, 10, 2)
         turn(14, 0)
         u_mult(14, 0)
+        p_cast(gcopy, 10, 2)
         turn(14, 1)
         u_mult(14, 1)
         turn(15, 0)
         u_mult(15, 0)
         turn(15, 1)
+        p_turn(8, 2)
+        p_exit(scopy, 8, 2)
         stage2(6)
         u_quant(14, 1)
         u_mult(15, 1)
         last_quant(15, 0)
         last_quant(15, 1)
+        p_quant(6, 2)
+        store_words(4, 8)
+        store_scales(0, 8)
         p_turn(10, 2)
-        p_cast(vcopy, 12, 2)
+        p_cast(vcopy, 12, 2, "r_late", 1)
         p_exit(scopy, 10, 2)
         r_product(14)
         r_exit(scopy, 14)
@@ -458,7 +463,7 @@ def tile_convnextdroppathlayerscaleweightgrad_x1_kernel(tc, x, w1, b1, r, dy, ga
         p_product(15, 1)
         r_product(15)
         p_quant(8, 2)
-        p_cast(vcopy, 14, 1, "r_last")
+        p_cast(vcopy, 14, 1, "r_last", 1)
         d_exit(scopy, 15)
         p_quant(10, 2)
         store_words(8, 12)

@@ -434,6 +434,8 @@ def tile_convnextdroppathlayerscaleweightgrad_x1_kernel(tc, x, w1, b1, r, dy, ga
             u_quant(2 * s, 2)
             if s == 5:
                 store_words(0, 4)
+            if s == 6:
+                store_scales(0, 6)
 
         stage2(5)
         turn(14, 0)
@@ -453,7 +455,6 @@ def tile_convnextdroppathlayerscaleweightgrad_x1_kernel(tc, x, w1, b1, r, dy, ga
         last_quant(15, 1)
         p_quant(6, 2)
         store_words(4, 8)
-        store_scales(0, 8)
         p_turn(10, 2)
         p_cast(vcopy, 12, 2, "r_late", 1)
         p_exit(scopy, 10, 2)
@@ -474,7 +475,6 @@ def tile_convnextdroppathlayerscaleweightgrad_x1_kernel(tc, x, w1, b1, r, dy, ga
         p_exit(scopy, 14, 1)
         p_quant(15, 1)
         p_quant(12, 2)
-        store_words(12, 14)
         p_quant(14, 1)
-        store_words(14, 16)
-        store_scales(8, 16)
+        store_words(12, 16)
+        store_scales(6, 16)

@@ -20,7 +20,8 @@ P = 128
 G = N // 512
 TILES = F // P
 PAIRS = TILES // 2
-W_LOADS = ((0, 2), (2, 4), (4, 6), (6, 8))
+W_LOADS = ((0, 4), (4, 8), (8, 12), (12, 16))
+W_STEPS = ((6, 8), (8, 10), (10, 12), (12, 14), (14, 16))
 BANKS = 8
 A_BUFS = 12
 
@@ -47,10 +48,10 @@ def tile_convnextdroppathlayerscaleweightgrad_x1_kernel(tc, x, w1, b1, r, dy, ga
         x_codes = keep.tile([P, G, 512], U32, name="x_codes", align_bytes=64)
         x_scales = keep.tile([P, G, 512], U8, name="x_scales", align_bytes=64)
         w_raw = {}
-        for j0, j1 in W_LOADS:
-            raw = keep.tile([P, 4, (j1 - j0) * 2 * P], BF16, name=f"w_raw{j0}")
-            for j in range(j0, j1):
-                w_raw[j] = raw, j - j0
+        for i0, i1 in W_LOADS:
+            raw = keep.tile([P, 4, (i1 - i0) * P], BF16, name=f"w_raw{i0}")
+            for i in range(i0, i1):
+                w_raw[i] = raw, i - i0
         w_codes = keep.tile([P, F], U32, name="w_codes", align_bytes=64)
         w_scales = keep.tile([P, F], U8, name="w_scales", align_bytes=64)
         dy_raw = {(g, h): keep.tile([P, 2, C], BF16, name=f"dy_raw{g}{h}") for g in range(G) for h in range(2)}
@@ -61,8 +62,15 @@ def tile_convnextdroppathlayerscaleweightgrad_x1_kernel(tc, x, w1, b1, r, dy, ga
         p_codes = keep.tile([P, F], U32, name="p_codes", align_bytes=64)
         p_scales = keep.tile([P, F], U8, name="p_scales", align_bytes=64)
 
-        def new_bank(shape, dtype, name):
-            return psum.tile(shape, dtype, name=name, tag="bank", bufs=BANKS)
+        free = list(range(BANKS))
+        held = {}
+
+        def new_bank(shape, dtype, name, key):
+            held[key] = free.pop(0)
+            return psum.tile(shape, dtype, name=name, tag=f"bank{held[key]}", bufs=1)
+
+        def emptied(key):
+            free.append(held[key])
 
         def gcopy(out, in_):
             nc.gpsimd.tensor_scalar(out=out, in0=in_, scalar1=1.0, scalar2=0.0, op0=MULT, op1=ADD)
@@ -71,9 +79,9 @@ def tile_convnextdroppathlayerscaleweightgrad_x1_kernel(tc, x, w1, b1, r, dy, ga
             src = x[512 * g : 512 * g + 512, :].rearrange("(m h t) k -> m h (t k)", h=2, t=2)
             nc.sync.dma_start(out=x_raw[g, h][:], in_=src[:, h, :])
 
-        def load_w(j0, j1):
-            c = slice(j0 * 2 * P, j1 * 2 * P)
-            nc.sync.dma_start(out=w_raw[j0][0][:], in_=w1[:, c].rearrange("(p j) f -> p j f", j=4))
+        def load_w(i0, i1):
+            c = slice(i0 * P, i1 * P)
+            nc.sync.dma_start(out=w_raw[i0][0][:], in_=w1[:, c].rearrange("(p j) f -> p j f", j=4))
 
         def load_dy(g, h):
             src = dy[512 * g : 512 * g + 512, :].rearrange("(p j) c -> p j c", j=4)
@@ -83,7 +91,7 @@ def tile_convnextdroppathlayerscaleweightgrad_x1_kernel(tc, x, w1, b1, r, dy, ga
 
         def x_turn(g, h):
             words = x_raw[g, h][:].bitcast(F32)
-            x_turned[g, h] = new_bank([P, 2, 2, P], F32, "x_bank")
+            x_turned[g, h] = new_bank([P, 2, 2, P], F32, "x_bank", ("x", g, h))
             for n in range(2):
                 for u in range(2):
                     nc.tensor.transpose(x_turned[g, h][:, n, u, :], words[:, 256 * n + u : 256 * (n + 1) : 2], ident[:])
@@ -94,6 +102,7 @@ def tile_convnextdroppathlayerscaleweightgrad_x1_kernel(tc, x, w1, b1, r, dy, ga
                 out=dst.rearrange("p (t m u) -> p t m u", t=2, u=2),
                 in_=x_turned[g, h][:].rearrange("p t u m -> p t m u"),
             )
+            emptied(("x", g, h))
 
         def x_quant(g):
             nc.vector.quantize_mx(
@@ -105,39 +114,50 @@ def tile_convnextdroppathlayerscaleweightgrad_x1_kernel(tc, x, w1, b1, r, dy, ga
         small = {}
 
         def bias_turn():
-            small["b"] = new_bank([P, P], BF16, "b_bank")
+            small["b"] = new_bank([P, P], BF16, "b_bank", "b")
             nc.tensor.transpose(small["b"][:], b_rows[:], ident_bf[:])
 
         def bias_exit(copy):
             copy(out=bias[:], in_=small["b"][:, 0:TILES])
+            emptied("b")
 
         def gamma_turn():
-            bank = small["g"] = new_bank([P, 2, P], F32, "g_bank")
+            bank = small["g"] = new_bank([P, 2, P], F32, "g_bank", "g")
             words = gcols[:].bitcast(F32)
             for u in range(2):
                 nc.tensor.transpose(bank[:, u, :], words[:, u : u + 1].to_broadcast([P, P]), ident[:])
 
         def gamma_exit(copy):
             copy(out=gam[:].bitcast(F32), in_=small["g"][:].rearrange("p u k -> p (u k)"))
+            emptied("g")
 
         w_bf = {}
 
-        def w_group(copy, j, tag="w_bf", bufs=3):
-            raw, at = w_raw[j]
-            w_bf[j] = work.tile([P, 2 * P, 4], BF16, name=tag, bufs=bufs, align_bytes=64)
-            src = raw[:, :, at * 2 * P : (at + 1) * 2 * P]
-            if copy is gcopy:
-                gcopy(out=w_bf[j][:], in_=src.rearrange("p j c -> p c j"))
-            else:
-                copy(out=w_bf[j][:].rearrange("p (c q) j -> p c j q", q=4), in_=src.rearrange("p j (c q) -> p c j q", q=4))
+        def w_tile(i0, i1, tag, bufs):
+            tile = work.tile([P, (i1 - i0) * P, 4], BF16, name=tag, bufs=bufs, align_bytes=64)
+            for i in range(i0, i1):
+                w_bf[i] = tile, i - i0
 
-        def w_quant(j):
-            c = slice(j * 2 * P, (j + 1) * 2 * P)
-            nc.vector.quantize_mx(
-                out=w_codes[:, c].bitcast(FP8X4),
-                scales=w_scales[:, c],
-                in_=w_bf[j][:].rearrange("p c j -> p (c j)"),
-            )
+        def w_group(copy, i0, i1):
+            raw, at = w_raw[i0]
+            tile, to = w_bf[i0]
+            src = raw[:, :, at * P : (at + i1 - i0) * P]
+            dst = tile[:, to * P : (to + i1 - i0) * P, :]
+            if copy is gcopy:
+                gcopy(out=dst, in_=src.rearrange("p j c -> p c j"))
+            else:
+                copy(out=dst.rearrange("p (c q) j -> p c j q", q=4), in_=src.rearrange("p j (c q) -> p c j q", q=4))
+
+        def w_quant(i0, i1):
+            for j0 in range(i0, i1, 2):
+                j1 = min(j0 + 2, i1)
+                tile, to = w_bf[j0]
+                c = slice(j0 * P, j1 * P)
+                nc.vector.quantize_mx(
+                    out=w_codes[:, c].bitcast(FP8X4),
+                    scales=w_scales[:, c],
+                    in_=tile[:, to * P : (to + j1 - j0) * P, :].rearrange("p c j -> p (c j)"),
+                )
 
         def e_mult(g, h):
             nc.vector.tensor_tensor(
@@ -164,7 +184,7 @@ def tile_convnextdroppathlayerscaleweightgrad_x1_kernel(tc, x, w1, b1, r, dy, ga
         h_bank = {}
 
         def h_product(i, g):
-            bank = h_bank[i, g] = new_bank([P, 512], F32, "h_bank")
+            bank = h_bank[i, g] = new_bank([P, 512], F32, "h_bank", ("h", i, g))
             c = slice(i * P, (i + 1) * P)
             nc.tensor.matmul_mx(
                 out=bank[:],
@@ -179,12 +199,13 @@ def tile_convnextdroppathlayerscaleweightgrad_x1_kernel(tc, x, w1, b1, r, dy, ga
         def gelu(i, g):
             a[i, g] = work.tile([P, 512], F32, name="a_sb", bufs=A_BUFS)
             nc.scalar.activation(out=a[i, g][:], in_=h_bank[i, g][:], func=GELU, bias=bias[:, i : i + 1])
+            emptied(("h", i, g))
 
         turned = {}
         u = {}
 
         def turn(i, g):
-            turned[i, g] = new_bank([P, 4, P], F32, "t_bank")
+            turned[i, g] = new_bank([P, 4, P], F32, "t_bank", ("t", i, g))
             for t in range(4):
                 nc.tensor.transpose(turned[i, g][:, t, :], a[i, g][:, t * P : (t + 1) * P], ident[:])
 
@@ -197,6 +218,7 @@ def tile_convnextdroppathlayerscaleweightgrad_x1_kernel(tc, x, w1, b1, r, dy, ga
                 in1=r_sb[:, g, :].unsqueeze(1).to_broadcast([P, P, 4]),
                 op=MULT,
             )
+            emptied(("t", i, g))
 
         uq = {}
 
@@ -217,7 +239,7 @@ def tile_convnextdroppathlayerscaleweightgrad_x1_kernel(tc, x, w1, b1, r, dy, ga
 
         def r_product(i):
             codes, scales = uq[i]
-            r_bank[i] = new_bank([P, C], F32, "r_bank")
+            r_bank[i] = new_bank([P, C], F32, "r_bank", ("r", i))
             for g in range(G):
                 nc.tensor.matmul_mx(
                     out=r_bank[i][:],
@@ -237,6 +259,7 @@ def tile_convnextdroppathlayerscaleweightgrad_x1_kernel(tc, x, w1, b1, r, dy, ga
                 out=dst.rearrange("p (m t) -> p m t", t=4),
                 in_=r_bank[i][:].rearrange("p (t m) -> p m t", t=4),
             )
+            emptied(("r", i))
             nc.sync.dma_start(out=out_0[i * P : (i + 1) * P, :], in_=dst)
 
         def last_quant(i, g):
@@ -254,7 +277,7 @@ def tile_convnextdroppathlayerscaleweightgrad_x1_kernel(tc, x, w1, b1, r, dy, ga
         def p_product(i, g):
             codes, scales = uq[i]
             if g == 0:
-                p_bank[i] = new_bank([P, 4, P], F32, "d_bank")
+                p_bank[i] = new_bank([P, 4, P], F32, "d_bank", ("p", i))
             for t in range(4):
                 nc.tensor.matmul_mx(
                     out=p_bank[i][:, t, :],
@@ -278,7 +301,7 @@ def tile_convnextdroppathlayerscaleweightgrad_x1_kernel(tc, x, w1, b1, r, dy, ga
                 r_bf[i + m] = [words[:, (n * v + m) * P : (n * v + m + 1) * P] for v in range(2)]
 
         def p_turn(i, n):
-            p_bank[i] = new_bank([P, n, 2, P], F32, "p_bank")
+            p_bank[i] = new_bank([P, n, 2, P], F32, "p_bank", ("p", i))
             for m in range(n):
                 for v in range(2):
                     nc.tensor.transpose(p_bank[i][:, m, v, :], r_bf[i + m][v], ident[:])
@@ -287,10 +310,12 @@ def tile_convnextdroppathlayerscaleweightgrad_x1_kernel(tc, x, w1, b1, r, dy, ga
             p_bf[i] = work.tile([P, n * P, 4], BF16, name="p_bf", bufs=4, align_bytes=64)
             dst = p_bf[i][:].rearrange("p f c -> p (f c)").bitcast(F32)
             copy(out=dst.rearrange("p (n f v) -> p n f v", n=n, v=2), in_=p_bank[i][:].rearrange("p n v f -> p n f v"))
+            emptied(("p", i))
 
         def d_exit(copy, i):
             p_bf[i] = work.tile([P, P, 4], BF16, name="p_bf", bufs=4, align_bytes=64)
             copy(out=p_bf[i][:], in_=p_bank[i][:].rearrange("p t f -> p f t"))
+            emptied(("p", i))
 
         def store_words(i0, i1):
             nc.sync.dma_start(
@@ -373,11 +398,13 @@ def tile_convnextdroppathlayerscaleweightgrad_x1_kernel(tc, x, w1, b1, r, dy, ga
         e_group(vcopy, 0, 1)
         x_turn(0, 1)
         x_exit(scopy, 0, 1)
-        w_group(vcopy, 0)
+        w_tile(0, 2, "w_bf", 2)
+        w_group(vcopy, 0, 2)
         bias_turn()
         bias_exit(scopy)
-        w_group(scopy, 1)
-        w_quant(0)
+        w_tile(2, 4, "w_bf", 2)
+        w_group(scopy, 2, 4)
+        w_quant(0, 2)
         x_quant(0)
         e_quant(0)
         x_turn(1, 0)
@@ -385,7 +412,7 @@ def tile_convnextdroppathlayerscaleweightgrad_x1_kernel(tc, x, w1, b1, r, dy, ga
         x_turn(1, 1)
         x_exit(scopy, 1, 1)
         e_mult(1, 0)
-        w_quant(1)
+        w_quant(2, 4)
         e_mult(1, 1)
         x_quant(1)
         h_product(0, 0)
@@ -398,7 +425,8 @@ def tile_convnextdroppathlayerscaleweightgrad_x1_kernel(tc, x, w1, b1, r, dy, ga
         gelu(3, 0)
         e_group(vcopy, 1, 0)
         e_group(vcopy, 1, 1)
-        w_group(vcopy, 2, "w_one", 1)
+        w_tile(4, 6, "w_one", 1)
+        w_group(vcopy, 4, 6)
         e_quant(1)
         h_product(0, 1)
         gelu(0, 1)
@@ -408,16 +436,31 @@ def tile_convnextdroppathlayerscaleweightgrad_x1_kernel(tc, x, w1, b1, r, dy, ga
         gelu(2, 1)
         h_product(3, 1)
         gelu(3, 1)
-        w_quant(2)
+        w_quant(4, 6)
+        w_tile(6, 8, "w_one", 1)
+        w_group(gcopy, 6, 8)
+        turn(0, 0)
+        u_mult(0, 0)
+        turn(1, 0)
+        u_mult(1, 0)
+        turn(0, 1)
+        u_mult(0, 1)
+        turn(1, 1)
+        u_mult(1, 1)
+        w_quant(6, 8)
+        u_quant(0, 2)
 
-        for s in range(PAIRS - 1):
+        for s in range(1, PAIRS - 1):
+            if s in (1, 2):
+                stage1(s + 1)
             if s >= 2:
                 stage2(s - 2)
-            if s >= 1:
+            if s > 2:
                 stage1(s + 1)
-            if s + 3 < PAIRS:
-                w_group(gcopy, s + 3, "w_one", 1)
-            for i, g in halves(s) if s else [(0, 0), (1, 0), (0, 1), (1, 1)]:
+            if s < len(W_STEPS):
+                w_tile(*W_STEPS[s], "w_one", 1)
+                w_group(gcopy, *W_STEPS[s])
+            for i, g in halves(s):
                 turn(i, g)
                 u_mult(i, g)
             if s >= 2:
@@ -429,15 +472,20 @@ def tile_convnextdroppathlayerscaleweightgrad_x1_kernel(tc, x, w1, b1, r, dy, ga
                 p_exit(vcopy if s < 5 else scopy, 2 * (s - 3), 2)
             if s >= 4:
                 p_quant(2 * (s - 4), 2)
-            if s + 3 < PAIRS:
-                w_quant(s + 3)
+            if s == PAIRS - 2:
+                p_quant(2 * (s - 3), 2)
+            if s < len(W_STEPS):
+                w_quant(*W_STEPS[s])
             u_quant(2 * s, 2)
             if s == 5:
                 store_words(0, 4)
-            if s == 6:
-                store_scales(0, 6)
 
-        stage2(5)
+        r_product(10)
+        r_exit(scopy, 10)
+        r_product(11)
+        r_exit(scopy, 11)
+        store_words(4, 8)
+        store_scales(0, 8)
         turn(14, 0)
         u_mult(14, 0)
         p_cast(gcopy, 10, 2)
@@ -448,13 +496,15 @@ def tile_convnextdroppathlayerscaleweightgrad_x1_kernel(tc, x, w1, b1, r, dy, ga
         turn(15, 1)
         p_turn(8, 2)
         p_exit(scopy, 8, 2)
-        stage2(6)
+        r_product(12)
+        r_exit(scopy, 12)
+        r_product(13)
+        r_exit(scopy, 13)
         u_quant(14, 1)
         u_mult(15, 1)
         last_quant(15, 0)
         last_quant(15, 1)
-        p_quant(6, 2)
-        store_words(4, 8)
+        p_quant(8, 2)
         p_turn(10, 2)
         p_cast(vcopy, 12, 2, "r_late", 1)
         p_exit(scopy, 10, 2)
@@ -463,7 +513,6 @@ def tile_convnextdroppathlayerscaleweightgrad_x1_kernel(tc, x, w1, b1, r, dy, ga
         p_product(15, 0)
         p_product(15, 1)
         r_product(15)
-        p_quant(8, 2)
         p_cast(vcopy, 14, 1, "r_last", 1)
         d_exit(scopy, 15)
         p_quant(10, 2)
@@ -477,4 +526,4 @@ def tile_convnextdroppathlayerscaleweightgrad_x1_kernel(tc, x, w1, b1, r, dy, ga
         p_quant(12, 2)
         p_quant(14, 1)
         store_words(12, 16)
-        store_scales(6, 16)
+        store_scales(8, 16)

@@ -23,6 +23,7 @@ PAIRS = TILES // 2
 W_LOADS = ((0, 4), (4, 8), (8, 12), (12, 16))
 W_STEPS = ((6, 8), (8, 10), (10, 12), (12, 14), (14, 16))
 BANKS = 8
+EARLY = (13,)
 A_BUFS = 12
 
 
@@ -42,6 +43,7 @@ def tile_convnextdroppathlayerscaleweightgrad_x1_kernel(tc, x, w1, b1, r, dy, ga
         gcols = keep.tile([P, 4], BF16, name="gcols")
         gam = keep.tile([P, C], BF16, name="gam")
         r_sb = keep.tile([P, G, 4], BF16, name="r_sb")
+        r_wide = keep.tile([P, G, 512], BF16, name="r_wide")
         warm = keep.tile([P, 1], F32, name="warm")
         x_raw = {(g, h): keep.tile([P, 2 * C], BF16, name=f"x_raw{g}{h}") for g in range(G) for h in range(2)}
         x_bf = [keep.tile([P, 4 * P, 4], BF16, name=f"x_bf{g}", align_bytes=64) for g in range(G)]
@@ -131,6 +133,16 @@ def tile_convnextdroppathlayerscaleweightgrad_x1_kernel(tc, x, w1, b1, r, dy, ga
             copy(out=gam[:].bitcast(F32), in_=small["g"][:].rearrange("p u k -> p (u k)"))
             emptied("g")
 
+        def r_turn():
+            bank = small["r"] = new_bank([P, 2 * G, P], F32, "r_spread", "r")
+            words = r_sb[:].rearrange("p g t -> p (g t)").bitcast(F32)
+            for n in range(2 * G):
+                nc.tensor.transpose(bank[:, n, :], words[:, n : n + 1].to_broadcast([P, P]), ident[:])
+
+        def r_spread_exit(copy):
+            copy(out=r_wide[:].rearrange("p g c -> p (g c)").bitcast(F32), in_=small["r"][:].rearrange("p n m -> p (n m)"))
+            emptied("r")
+
         w_bf = {}
 
         def w_tile(i0, i1, tag, bufs):
@@ -143,8 +155,8 @@ def tile_convnextdroppathlayerscaleweightgrad_x1_kernel(tc, x, w1, b1, r, dy, ga
             tile, to = w_bf[i0]
             src = raw[:, :, at * P : (at + i1 - i0) * P]
             dst = tile[:, to * P : (to + i1 - i0) * P, :]
-            if copy is gcopy:
-                gcopy(out=dst, in_=src.rearrange("p j c -> p c j"))
+            if copy is not vcopy:
+                copy(out=dst, in_=src.rearrange("p j c -> p c j"))
             else:
                 copy(out=dst.rearrange("p (c q) j -> p c j q", q=4), in_=src.rearrange("p j (c q) -> p c j q", q=4))
 
@@ -168,6 +180,12 @@ def tile_convnextdroppathlayerscaleweightgrad_x1_kernel(tc, x, w1, b1, r, dy, ga
             )
 
         def e_group(copy, g, v):
+            if copy is scopy:
+                scopy(
+                    out=e_bf[g][:, 2 * v * P : 2 * (v + 1) * P, :].rearrange("p (c m) j -> p c m j", c=2),
+                    in_=e_nat[g][:, v].rearrange("p j m c -> p c m j"),
+                )
+                return
             copy(
                 out=e_bf[g][:, 2 * v * P : 2 * (v + 1) * P, :].rearrange("p (c n m) j -> p n j m c", c=2, m=2),
                 in_=e_nat[g][:, v].rearrange("p j (n m) c -> p n j m c", m=2),
@@ -197,8 +215,15 @@ def tile_convnextdroppathlayerscaleweightgrad_x1_kernel(tc, x, w1, b1, r, dy, ga
             )
 
         def gelu(i, g):
-            a[i, g] = work.tile([P, 512], F32, name="a_sb", bufs=A_BUFS)
-            nc.scalar.activation(out=a[i, g][:], in_=h_bank[i, g][:], func=GELU, bias=bias[:, i : i + 1])
+            if i in EARLY:
+                if g == 0:
+                    a[i] = work.tile([P, G, 512], F32, name="a_wide", bufs=2)
+                dst = a[i][:, g, :].rearrange("p (v m e) -> p v m e", v=2, e=2)
+                src = h_bank[i, g][:].rearrange("p (v e m) -> p v m e", v=2, e=2)
+            else:
+                a[i, g] = work.tile([P, 512], F32, name="a_sb", bufs=A_BUFS)
+                dst, src = a[i, g][:], h_bank[i, g][:]
+            nc.scalar.activation(out=dst, in_=src, func=GELU, bias=bias[:, i : i + 1])
             emptied(("h", i, g))
 
         turned = {}
@@ -219,6 +244,32 @@ def tile_convnextdroppathlayerscaleweightgrad_x1_kernel(tc, x, w1, b1, r, dy, ga
                 op=MULT,
             )
             emptied(("t", i, g))
+
+        u_rows = {}
+
+        def early_mult(i):
+            u_rows[i] = work.tile([P, G * 512], BF16, name="u_rows", bufs=2)
+            nc.vector.tensor_tensor(
+                out=u_rows[i][:],
+                in0=a[i][:].rearrange("p g c -> p (g c)"),
+                in1=r_wide[:].rearrange("p g c -> p (g c)"),
+                op=MULT,
+            )
+
+        def early_turn(i):
+            turned[i] = new_bank([P, G, 2, P], F32, "w_bank", ("t", i))
+            words = u_rows[i][:].bitcast(F32)
+            for g in range(G):
+                for v in range(2):
+                    n = 2 * g + v
+                    nc.tensor.transpose(turned[i][:, g, v, :], words[:, n * P : (n + 1) * P], ident[:])
+
+        def early_exit(copy, i):
+            if i // 2 not in u:
+                u[i // 2] = work.tile([P, 2, G, P, 4], BF16, name="u_bf", bufs=3, align_bytes=64)
+            dst = u[i // 2][:, i % 2].rearrange("p g f t -> p (g f t)").bitcast(F32)
+            copy(out=dst.rearrange("p (g f v) -> p g f v", g=G, v=2), in_=turned[i][:].rearrange("p g v f -> p g f v"))
+            emptied(("t", i))
 
         uq = {}
 
@@ -374,6 +425,7 @@ def tile_convnextdroppathlayerscaleweightgrad_x1_kernel(tc, x, w1, b1, r, dy, ga
 
         load_gamma()
         load_x(0, 0)
+        load_r()
         load_dy(0, 0)
         load_dy(0, 1)
         load_x(0, 1)
@@ -383,7 +435,6 @@ def tile_convnextdroppathlayerscaleweightgrad_x1_kernel(tc, x, w1, b1, r, dy, ga
         load_x(1, 1)
         load_dy(1, 0)
         load_dy(1, 1)
-        load_r()
         load_w(*W_LOADS[1])
         load_w(*W_LOADS[2])
         load_w(*W_LOADS[3])
@@ -394,6 +445,8 @@ def tile_convnextdroppathlayerscaleweightgrad_x1_kernel(tc, x, w1, b1, r, dy, ga
         e_mult(0, 1)
         x_turn(0, 0)
         x_exit(scopy, 0, 0)
+        r_turn()
+        r_spread_exit(scopy)
         e_group(scopy, 0, 0)
         e_group(vcopy, 0, 1)
         x_turn(0, 1)
@@ -461,15 +514,21 @@ def tile_convnextdroppathlayerscaleweightgrad_x1_kernel(tc, x, w1, b1, r, dy, ga
                 w_tile(*W_STEPS[s], "w_one", 1)
                 w_group(gcopy, *W_STEPS[s])
             for i, g in halves(s):
-                turn(i, g)
-                u_mult(i, g)
+                if i not in EARLY:
+                    turn(i, g)
+                    u_mult(i, g)
             if s >= 2:
                 p_cast(gcopy, 2 * (s - 2), 2 if s > 2 else 1)
             if s == 2:
                 p_cast(vcopy, 1, 1, "r_last", 1)
             if s >= 3:
                 p_turn(2 * (s - 3), 2)
-                p_exit(vcopy if s < 5 else scopy, 2 * (s - 3), 2)
+                p_exit(vcopy if s != 5 else scopy, 2 * (s - 3), 2)
+            if 2 * s + 1 in EARLY:
+                early_turn(2 * s + 1)
+                early_exit(scopy, 2 * s + 1)
+            if 2 * s + 3 in EARLY:
+                early_mult(2 * s + 3)
             if s >= 4:
                 p_quant(2 * (s - 4), 2)
             if s == PAIRS - 2:

@@ -155,8 +155,8 @@ def tile_convnextdroppathlayerscaleweightgrad_x1_kernel(tc, x, w1, b1, r, dy, ga
             tile, to = w_bf[i0]
             src = raw[:, :, at * P : (at + i1 - i0) * P]
             dst = tile[:, to * P : (to + i1 - i0) * P, :]
-            if copy is not vcopy:
-                copy(out=dst, in_=src.rearrange("p j c -> p c j"))
+            if copy is gcopy:
+                gcopy(out=dst, in_=src.rearrange("p j c -> p c j"))
             else:
                 copy(out=dst.rearrange("p (c q) j -> p c j q", q=4), in_=src.rearrange("p j (c q) -> p c j q", q=4))
 
@@ -180,12 +180,6 @@ def tile_convnextdroppathlayerscaleweightgrad_x1_kernel(tc, x, w1, b1, r, dy, ga
             )
 
         def e_group(copy, g, v):
-            if copy is scopy:
-                scopy(
-                    out=e_bf[g][:, 2 * v * P : 2 * (v + 1) * P, :].rearrange("p (c m) j -> p c m j", c=2),
-                    in_=e_nat[g][:, v].rearrange("p j m c -> p c m j"),
-                )
-                return
             copy(
                 out=e_bf[g][:, 2 * v * P : 2 * (v + 1) * P, :].rearrange("p (c n m) j -> p n j m c", c=2, m=2),
                 in_=e_nat[g][:, v].rearrange("p j (n m) c -> p n j m c", m=2),

@@ -21,9 +21,8 @@ G = N // 512
 TILES = F // P
 PAIRS = TILES // 2
 W_LOADS = ((0, 4), (4, 8), (8, 12), (12, 16))
-W_STEPS = ((6, 8), (8, 10), (10, 12), (12, 14), (14, 16))
 BANKS = 8
-EARLY = (13,)
+EARLY = (9, 11, 13)
 A_BUFS = 12
 
 
@@ -41,9 +40,7 @@ def tile_convnextdroppathlayerscaleweightgrad_x1_kernel(tc, x, w1, b1, r, dy, ga
         b_rows = keep.tile([P, P], BF16, name="b_rows")
         bias = keep.tile([P, TILES], F32, name="bias")
         gcols = keep.tile([P, 4], BF16, name="gcols")
-        gam = keep.tile([P, C], BF16, name="gam")
         r_sb = keep.tile([P, G, 4], BF16, name="r_sb")
-        r_wide = keep.tile([P, G, 512], BF16, name="r_wide")
         warm = keep.tile([P, 1], F32, name="warm")
         x_raw = {(g, h): keep.tile([P, 2 * C], BF16, name=f"x_raw{g}{h}") for g in range(G) for h in range(2)}
         x_bf = [keep.tile([P, 4 * P, 4], BF16, name=f"x_bf{g}", align_bytes=64) for g in range(G)]
@@ -58,7 +55,7 @@ def tile_convnextdroppathlayerscaleweightgrad_x1_kernel(tc, x, w1, b1, r, dy, ga
         w_scales = keep.tile([P, F], U8, name="w_scales", align_bytes=64)
         dy_raw = {(g, h): keep.tile([P, 2, C], BF16, name=f"dy_raw{g}{h}") for g in range(G) for h in range(2)}
         e_nat = [keep.tile([P, 2, 4, P, 2], BF16, name=f"e_nat{g}") for g in range(G)]
-        e_bf = [keep.tile([P, C, 4], BF16, name=f"e_bf{g}", align_bytes=64) for g in range(G)]
+        e_bf = [work.tile([P, C, 4], BF16, name=f"e_bf{g}", tag=f"grouped{g}", bufs=1, align_bytes=64) for g in range(G)]
         e_codes = keep.tile([P, G, C], U32, name="e_codes", align_bytes=64)
         e_scales = keep.tile([P, G, C], U8, name="e_scales", align_bytes=64)
         p_codes = keep.tile([P, F], U32, name="p_codes", align_bytes=64)
@@ -106,11 +103,12 @@ def tile_convnextdroppathlayerscaleweightgrad_x1_kernel(tc, x, w1, b1, r, dy, ga
             )
             emptied(("x", g, h))
 
-        def x_quant(g):
+        def x_quant(g, h0, h1):
+            c = slice(256 * h0, 256 * h1)
             nc.vector.quantize_mx(
-                out=x_codes[:, g, :].bitcast(FP8X4),
-                scales=x_scales[:, g, :],
-                in_=x_bf[g][:].rearrange("p c j -> p (c j)"),
+                out=x_codes[:, g, c].bitcast(FP8X4),
+                scales=x_scales[:, g, c],
+                in_=x_bf[g][:, c, :].rearrange("p c j -> p (c j)"),
             )
 
         small = {}
@@ -129,24 +127,16 @@ def tile_convnextdroppathlayerscaleweightgrad_x1_kernel(tc, x, w1, b1, r, dy, ga
             for u in range(2):
                 nc.tensor.transpose(bank[:, u, :], words[:, u : u + 1].to_broadcast([P, P]), ident[:])
 
-        def gamma_exit(copy):
-            copy(out=gam[:].bitcast(F32), in_=small["g"][:].rearrange("p u k -> p (u k)"))
-            emptied("g")
-
         def r_turn():
             bank = small["r"] = new_bank([P, 2 * G, P], F32, "r_spread", "r")
             words = r_sb[:].rearrange("p g t -> p (g t)").bitcast(F32)
             for n in range(2 * G):
                 nc.tensor.transpose(bank[:, n, :], words[:, n : n + 1].to_broadcast([P, P]), ident[:])
 
-        def r_spread_exit(copy):
-            copy(out=r_wide[:].rearrange("p g c -> p (g c)").bitcast(F32), in_=small["r"][:].rearrange("p n m -> p (n m)"))
-            emptied("r")
-
         w_bf = {}
 
         def w_tile(i0, i1, tag, bufs):
-            tile = work.tile([P, (i1 - i0) * P, 4], BF16, name=tag, bufs=bufs, align_bytes=64)
+            tile = work.tile([P, (i1 - i0) * P, 4], BF16, name="w_bf", tag=tag, bufs=bufs, align_bytes=64)
             for i in range(i0, i1):
                 w_bf[i] = tile, i - i0
 
@@ -172,14 +162,23 @@ def tile_convnextdroppathlayerscaleweightgrad_x1_kernel(tc, x, w1, b1, r, dy, ga
                 )
 
         def e_mult(g, h):
+            gam = small["g"][:].rearrange("p u k -> p (u k)").bitcast(BF16)
             nc.vector.tensor_tensor(
                 out=e_nat[g][:, :, 2 * h : 2 * h + 2],
                 in0=dy_raw[g, h][:].rearrange("p j (m v c) -> p v j m c", v=2, c=2),
-                in1=gam[:].rearrange("p (v m c) -> p v m c", v=2, c=2).unsqueeze(2).to_broadcast([P, 2, 2, P, 2]),
+                in1=gam.rearrange("p (v m c) -> p v m c", v=2, c=2).unsqueeze(2).to_broadcast([P, 2, 2, P, 2]),
                 op=MULT,
             )
+            if (g, h) == (G - 1, 1):
+                emptied("g")
 
         def e_group(copy, g, v):
+            if copy is gcopy:
+                gcopy(
+                    out=e_bf[g][:, 2 * v * P : 2 * (v + 1) * P, :].rearrange("p (c m) j -> p c m j", c=2),
+                    in_=e_nat[g][:, v].rearrange("p j m c -> p c m j"),
+                )
+                return
             copy(
                 out=e_bf[g][:, 2 * v * P : 2 * (v + 1) * P, :].rearrange("p (c n m) j -> p n j m c", c=2, m=2),
                 in_=e_nat[g][:, v].rearrange("p j (n m) c -> p n j m c", m=2),
@@ -246,9 +245,11 @@ def tile_convnextdroppathlayerscaleweightgrad_x1_kernel(tc, x, w1, b1, r, dy, ga
             nc.vector.tensor_tensor(
                 out=u_rows[i][:],
                 in0=a[i][:].rearrange("p g c -> p (g c)"),
-                in1=r_wide[:].rearrange("p g c -> p (g c)"),
+                in1=small["r"][:].rearrange("p n m -> p (n m)").bitcast(BF16),
                 op=MULT,
             )
+            if i == EARLY[-1]:
+                emptied("r")
 
         def early_turn(i):
             turned[i] = new_bank([P, G, 2, P], F32, "w_bank", ("t", i))
@@ -388,7 +389,7 @@ def tile_convnextdroppathlayerscaleweightgrad_x1_kernel(tc, x, w1, b1, r, dy, ga
             return [(2 * j + m, g) for m in range(2) for g in range(G)]
 
         def stage1(j):
-            for i, g in halves(j):
+            for i, g in sorted(halves(j), key=lambda ig: ig[0] not in EARLY):
                 h_product(i, g)
                 gelu(i, g)
 
@@ -402,12 +403,6 @@ def tile_convnextdroppathlayerscaleweightgrad_x1_kernel(tc, x, w1, b1, r, dy, ga
                 turn(i, g)
                 u_mult(i, g)
 
-        nc.vector.memset(warm[:], 0.0)
-        nc.vector.memset(b_rows[:], 0.0)
-        make_identity(nc, ident[:])
-        make_identity(nc, ident_bf[:])
-        nc.scalar.activation(out=warm[:], in_=warm[:], func=GELU)
-
         def load_gamma():
             nc.sync.dma_start(out=gcols[:], in_=gamma.rearrange("(k q) -> k q", q=4))
 
@@ -417,122 +412,133 @@ def tile_convnextdroppathlayerscaleweightgrad_x1_kernel(tc, x, w1, b1, r, dy, ga
         def load_r():
             nc.sync.dma_start(out=r_sb[:], in_=r.rearrange("(g p t) -> p g t", g=G, t=4))
 
+        def expand(j, g):
+            for i in (2 * j, 2 * j + 1):
+                h_product(i, g)
+                gelu(i, g)
+
+        def weigh(j, g):
+            for i in (2 * j, 2 * j + 1):
+                turn(i, g)
+                u_mult(i, g)
+
+        def w_pair(copy, j, tag="w_one", bufs=1):
+            w_tile(2 * j, 2 * j + 2, tag, bufs)
+            w_group(copy, 2 * j, 2 * j + 2)
+
+        def w_pair_quant(j):
+            w_quant(2 * j, 2 * j + 2)
+
+        nc.vector.memset(warm[:], 0.0)
+        nc.vector.memset(b_rows[:], 0.0)
+        make_identity(nc, ident[:])
+        make_identity(nc, ident_bf[:])
+        nc.scalar.activation(out=warm[:], in_=warm[:], func=GELU)
+
         load_gamma()
-        load_x(0, 0)
-        load_r()
         load_dy(0, 0)
         load_dy(0, 1)
+        load_x(0, 0)
         load_x(0, 1)
         load_w(*W_LOADS[0])
         load_bias()
         load_x(1, 0)
         load_x(1, 1)
+        load_r()
         load_dy(1, 0)
         load_dy(1, 1)
-        load_w(*W_LOADS[1])
-        load_w(*W_LOADS[2])
-        load_w(*W_LOADS[3])
+        for k in range(1, len(W_LOADS)):
+            load_w(*W_LOADS[k])
 
         gamma_turn()
-        gamma_exit(scopy)
         e_mult(0, 0)
         e_mult(0, 1)
-        x_turn(0, 0)
-        x_exit(scopy, 0, 0)
-        r_turn()
-        r_spread_exit(scopy)
         e_group(scopy, 0, 0)
-        e_group(vcopy, 0, 1)
+        e_group(gcopy, 0, 1)
+        x_turn(0, 0)
+        x_exit(vcopy, 0, 0)
         x_turn(0, 1)
-        x_exit(scopy, 0, 1)
-        w_tile(0, 2, "w_bf", 2)
-        w_group(vcopy, 0, 2)
+        x_exit(vcopy, 0, 1)
+        w_pair(vcopy, 0, "w_bf", 4)
+        w_pair(scopy, 1, "w_bf", 4)
         bias_turn()
         bias_exit(scopy)
-        w_tile(2, 4, "w_bf", 2)
-        w_group(scopy, 2, 4)
-        w_quant(0, 2)
-        x_quant(0)
-        e_quant(0)
         x_turn(1, 0)
         x_exit(scopy, 1, 0)
         x_turn(1, 1)
         x_exit(scopy, 1, 1)
-        e_mult(1, 0)
-        w_quant(2, 4)
-        e_mult(1, 1)
-        x_quant(1)
+        x_quant(0, 0, 2)
+        w_pair_quant(0)
+        w_pair_quant(1)
+        e_quant(0)
+        x_quant(1, 0, 2)
         h_product(0, 0)
-        gelu(0, 0)
         h_product(1, 0)
-        gelu(1, 0)
         h_product(2, 0)
+        gelu(0, 0)
+        gelu(1, 0)
         gelu(2, 0)
-        h_product(3, 0)
-        gelu(3, 0)
-        e_group(vcopy, 1, 0)
-        e_group(vcopy, 1, 1)
-        w_tile(4, 6, "w_one", 1)
-        w_group(vcopy, 4, 6)
-        e_quant(1)
         h_product(0, 1)
-        gelu(0, 1)
         h_product(1, 1)
+        gelu(0, 1)
         gelu(1, 1)
-        h_product(2, 1)
-        gelu(2, 1)
-        h_product(3, 1)
-        gelu(3, 1)
-        w_quant(4, 6)
-        w_tile(6, 8, "w_one", 1)
-        w_group(gcopy, 6, 8)
+        w_pair(gcopy, 2, "w_one", 1)
+        e_mult(1, 0)
+        e_mult(1, 1)
         turn(0, 0)
         u_mult(0, 0)
+        w_pair_quant(2)
+        w_pair(gcopy, 3, "w_one", 1)
         turn(1, 0)
         u_mult(1, 0)
-        turn(0, 1)
-        u_mult(0, 1)
-        turn(1, 1)
-        u_mult(1, 1)
-        w_quant(6, 8)
-        u_quant(0, 2)
+        h_product(3, 0)
+        h_product(2, 1)
+        h_product(3, 1)
+        gelu(3, 0)
+        gelu(2, 1)
+        gelu(3, 1)
+        weigh(0, 1)
+        e_group(scopy, 1, 1)
+        stage1(2)
+        r_turn()
+        e_group(vcopy, 1, 0)
+        w_pair_quant(3)
 
-        for s in range(1, PAIRS - 1):
-            if s in (1, 2):
-                stage1(s + 1)
-            if s >= 2:
-                stage2(s - 2)
-            if s > 2:
-                stage1(s + 1)
-            if s < len(W_STEPS):
-                w_tile(*W_STEPS[s], "w_one", 1)
-                w_group(gcopy, *W_STEPS[s])
+        u_quant(0, 2)
+        e_quant(1)
+        w_pair(gcopy, 4, "grouped1", 1)
+        weigh(1, 0)
+        weigh(1, 1)
+        w_pair_quant(4)
+        u_quant(2, 2)
+
+        for s in range(2, PAIRS - 1):
+            stage2(s - 2)
+            stage1(s + 1)
+            if s + 3 < PAIRS:
+                w_pair(gcopy, s + 3, "grouped1", 1)
+            if 2 * s + 1 in EARLY:
+                early_turn(2 * s + 1)
+                early_exit(vcopy, 2 * s + 1)
             for i, g in halves(s):
                 if i not in EARLY:
                     turn(i, g)
                     u_mult(i, g)
-            if s >= 2:
-                p_cast(gcopy, 2 * (s - 2), 2 if s > 2 else 1)
-            if s == 2:
-                p_cast(vcopy, 1, 1, "r_last", 1)
+            p_cast(gcopy, 2 * (s - 2), 2)
             if s >= 3:
                 p_turn(2 * (s - 3), 2)
-                p_exit(vcopy if s != 5 else scopy, 2 * (s - 3), 2)
-            if 2 * s + 1 in EARLY:
-                early_turn(2 * s + 1)
-                early_exit(scopy, 2 * s + 1)
+                p_exit(scopy, 2 * (s - 3), 2)
             if 2 * s + 3 in EARLY:
                 early_mult(2 * s + 3)
             if s >= 4:
                 p_quant(2 * (s - 4), 2)
             if s == PAIRS - 2:
                 p_quant(2 * (s - 3), 2)
-            if s < len(W_STEPS):
-                w_quant(*W_STEPS[s])
+            if s + 3 < PAIRS:
+                w_pair_quant(s + 3)
             u_quant(2 * s, 2)
             if s == 5:
                 store_words(0, 4)
-
         r_product(10)
         r_exit(scopy, 10)
         r_product(11)

@@ -21,8 +21,9 @@ G = N // 512
 TILES = F // P
 PAIRS = TILES // 2
 W_LOADS = ((0, 4), (4, 8), (8, 12), (12, 16))
+LONG_CAST = 2
 BANKS = 8
-EARLY = (9, 11, 13)
+EARLY = (7, 9, 11, 13)
 A_BUFS = 12
 
 
@@ -151,15 +152,13 @@ def tile_convnextdroppathlayerscaleweightgrad_x1_kernel(tc, x, w1, b1, r, dy, ga
                 copy(out=dst.rearrange("p (c q) j -> p c j q", q=4), in_=src.rearrange("p j (c q) -> p c j q", q=4))
 
         def w_quant(i0, i1):
-            for j0 in range(i0, i1, 2):
-                j1 = min(j0 + 2, i1)
-                tile, to = w_bf[j0]
-                c = slice(j0 * P, j1 * P)
-                nc.vector.quantize_mx(
-                    out=w_codes[:, c].bitcast(FP8X4),
-                    scales=w_scales[:, c],
-                    in_=tile[:, to * P : (to + j1 - j0) * P, :].rearrange("p c j -> p (c j)"),
-                )
+            tile, to = w_bf[i0]
+            c = slice(i0 * P, i1 * P)
+            nc.vector.quantize_mx(
+                out=w_codes[:, c].bitcast(FP8X4),
+                scales=w_scales[:, c],
+                in_=tile[:, to * P : (to + i1 - i0) * P, :].rearrange("p c j -> p (c j)"),
+            )
 
         def e_mult(g, h):
             gam = small["g"][:].rearrange("p u k -> p (u k)").bitcast(BF16)
@@ -229,7 +228,7 @@ def tile_convnextdroppathlayerscaleweightgrad_x1_kernel(tc, x, w1, b1, r, dy, ga
 
         def u_mult(i, g):
             if i // 2 not in u:
-                u[i // 2] = work.tile([P, 2, G, P, 4], BF16, name="u_bf", bufs=3, align_bytes=64)
+                u[i // 2] = work.tile([P, 2, G, P, 4], BF16, name="u_bf", tag=f"u{i // 2 % 3}", bufs=1, align_bytes=64)
             nc.vector.tensor_tensor(
                 out=u[i // 2][:, i % 2, g, :, :],
                 in0=turned[i, g][:].rearrange("p t f -> p f t"),
@@ -261,7 +260,7 @@ def tile_convnextdroppathlayerscaleweightgrad_x1_kernel(tc, x, w1, b1, r, dy, ga
 
         def early_exit(copy, i):
             if i // 2 not in u:
-                u[i // 2] = work.tile([P, 2, G, P, 4], BF16, name="u_bf", bufs=3, align_bytes=64)
+                u[i // 2] = work.tile([P, 2, G, P, 4], BF16, name="u_bf", tag=f"u{i // 2 % 3}", bufs=1, align_bytes=64)
             dst = u[i // 2][:, i % 2].rearrange("p g f t -> p (g f t)").bitcast(F32)
             copy(out=dst.rearrange("p (g f v) -> p g f v", g=G, v=2), in_=turned[i][:].rearrange("p g v f -> p g f v"))
             emptied(("t", i))
@@ -283,10 +282,11 @@ def tile_convnextdroppathlayerscaleweightgrad_x1_kernel(tc, x, w1, b1, r, dy, ga
         p_bank = {}
         r_out = {}
 
-        def r_product(i):
+        def r_product(i, groups=range(G)):
             codes, scales = uq[i]
-            r_bank[i] = new_bank([P, C], F32, "r_bank", ("r", i))
-            for g in range(G):
+            if 0 in groups:
+                r_bank[i] = new_bank([P, C], F32, "r_bank", ("r", i))
+            for g in groups:
                 nc.tensor.matmul_mx(
                     out=r_bank[i][:],
                     lhsT=codes[:, g, :].bitcast(FP8X4),
@@ -298,6 +298,9 @@ def tile_convnextdroppathlayerscaleweightgrad_x1_kernel(tc, x, w1, b1, r, dy, ga
                 )
 
         def r_exit(copy, i):
+            if i == LONG_CAST:
+                four = work.tile([P, 4, C], F32, name="r_four", bufs=1)
+                r_out["four"], r_out[i // 2], r_out[i // 2 + 1] = four, four[:, 0:2, :], four[:, 2:4, :]
             if i // 2 not in r_out:
                 r_out[i // 2] = work.tile([P, 2, C], F32, name="r_out", bufs=4)
             dst = r_out[i // 2][:, i % 2, :]
@@ -338,9 +341,9 @@ def tile_convnextdroppathlayerscaleweightgrad_x1_kernel(tc, x, w1, b1, r, dy, ga
         r_bf = {}
         p_bf = {}
 
-        def p_cast(copy, i, n, tag="u_bf", bufs=3):
-            cast = work.tile([P, 2, n * P, 2], BF16, name=tag, bufs=bufs, align_bytes=64)
-            src = r_out[i // 2][:, i % 2 : i % 2 + n, :]
+        def p_cast(copy, i, n, tag, bufs=1):
+            cast = work.tile([P, 2, n * P, 2], BF16, name="cast", tag=tag, bufs=bufs, align_bytes=64)
+            src = r_out["four"][:] if n == 4 else r_out[i // 2][:, i % 2 : i % 2 + n, :]
             copy(out=cast[:], in_=src.rearrange("p n (m v c) -> p v (n m) c", v=2, c=2))
             words = cast[:].rearrange("p v m c -> p (v m c)").bitcast(F32)
             for m in range(n):
@@ -426,6 +429,10 @@ def tile_convnextdroppathlayerscaleweightgrad_x1_kernel(tc, x, w1, b1, r, dy, ga
             w_tile(2 * j, 2 * j + 2, tag, bufs)
             w_group(copy, 2 * j, 2 * j + 2)
 
+        def w_run(i0, i1):
+            w_tile(i0, i1, "grouped1", 1)
+            w_group(gcopy, i0, i1)
+
         def w_pair_quant(j):
             w_quant(2 * j, 2 * j + 2)
 
@@ -444,11 +451,12 @@ def tile_convnextdroppathlayerscaleweightgrad_x1_kernel(tc, x, w1, b1, r, dy, ga
         load_bias()
         load_x(1, 0)
         load_x(1, 1)
-        load_r()
+        load_w(*W_LOADS[1])
         load_dy(1, 0)
         load_dy(1, 1)
-        for k in range(1, len(W_LOADS)):
-            load_w(*W_LOADS[k])
+        load_r()
+        load_w(*W_LOADS[2])
+        load_w(*W_LOADS[3])
 
         gamma_turn()
         e_mult(0, 0)
@@ -472,6 +480,7 @@ def tile_convnextdroppathlayerscaleweightgrad_x1_kernel(tc, x, w1, b1, r, dy, ga
         w_pair_quant(1)
         e_quant(0)
         x_quant(1, 0, 2)
+        w_pair(vcopy, 2, "w_one", 1)
         h_product(0, 0)
         h_product(1, 0)
         h_product(2, 0)
@@ -480,92 +489,114 @@ def tile_convnextdroppathlayerscaleweightgrad_x1_kernel(tc, x, w1, b1, r, dy, ga
         gelu(2, 0)
         h_product(0, 1)
         h_product(1, 1)
+        h_product(3, 0)
         gelu(0, 1)
         gelu(1, 1)
-        w_pair(gcopy, 2, "w_one", 1)
         e_mult(1, 0)
+        w_pair_quant(2)
         e_mult(1, 1)
+        w_pair(gcopy, 3, "w_one", 1)
+        e_group(gcopy, 1, 0)
         turn(0, 0)
         u_mult(0, 0)
-        w_pair_quant(2)
-        w_pair(gcopy, 3, "w_one", 1)
         turn(1, 0)
         u_mult(1, 0)
-        h_product(3, 0)
+        gelu(3, 0)
+        e_group(scopy, 1, 1)
         h_product(2, 1)
         h_product(3, 1)
-        gelu(3, 0)
         gelu(2, 1)
         gelu(3, 1)
-        weigh(0, 1)
-        e_group(scopy, 1, 1)
+        turn(0, 1)
+        u_mult(0, 1)
+        turn(1, 1)
+        u_mult(1, 1)
+        turn(2, 0)
+        u_mult(2, 0)
         stage1(2)
-        r_turn()
-        e_group(vcopy, 1, 0)
         w_pair_quant(3)
-
-        u_quant(0, 2)
         e_quant(1)
+        u_quant(0, 2)
         w_pair(gcopy, 4, "grouped1", 1)
-        weigh(1, 0)
-        weigh(1, 1)
+        turn(3, 0)
+        u_mult(3, 0)
+        turn(2, 1)
+        u_mult(2, 1)
+        turn(3, 1)
+        u_mult(3, 1)
         w_pair_quant(4)
         u_quant(2, 2)
 
         for s in range(2, PAIRS - 1):
             stage2(s - 2)
             stage1(s + 1)
-            if s + 3 < PAIRS:
-                w_pair(gcopy, s + 3, "grouped1", 1)
-            if 2 * s + 1 in EARLY:
+            if s == 2:
+                w_run(10, 12)
+            if s == 3:
+                w_run(12, 16)
+            turn(2 * s, 0)
+            u_mult(2 * s, 0)
+            turn(2 * s, 1)
+            u_mult(2 * s, 1)
+            if s == 2:
+                turn(5, 0)
+                u_mult(5, 0)
+                turn(5, 1)
+                u_mult(5, 1)
+                r_turn()
+                p_cast(gcopy, 0, 2, "u1")
+            else:
                 early_turn(2 * s + 1)
-                early_exit(vcopy, 2 * s + 1)
-            for i, g in halves(s):
-                if i not in EARLY:
-                    turn(i, g)
-                    u_mult(i, g)
-            p_cast(gcopy, 2 * (s - 2), 2)
-            if s >= 3:
-                p_turn(2 * (s - 3), 2)
-                p_exit(scopy, 2 * (s - 3), 2)
-            if 2 * s + 3 in EARLY:
+            if s == 4:
+                p_cast(gcopy, 2, 4, "u0")
+            if s > 4:
+                p_cast(gcopy, 2 * (s - 2), 2, f"u{(s - 1) % 3}")
+            planes = {3: (0,), 5: (2, 4), 6: (6,)}.get(s, ())
+            for i in planes:
+                p_turn(i, 2)
+            if s > 2:
+                early_exit(vcopy if s % 2 == 0 else scopy, 2 * s + 1)
+            for i in planes:
+                p_exit(vcopy if i < 4 else scopy, i, 2)
+            if s < PAIRS - 2:
                 early_mult(2 * s + 3)
-            if s >= 4:
-                p_quant(2 * (s - 4), 2)
-            if s == PAIRS - 2:
-                p_quant(2 * (s - 3), 2)
-            if s + 3 < PAIRS:
-                w_pair_quant(s + 3)
+            if s == 2:
+                w_quant(10, 12)
+
+            if s == 6:
+                p_quant(4, 2)
             u_quant(2 * s, 2)
+            if s == 3:
+                w_quant(12, 16)
+            if s == 4:
+                p_quant(0, 2)
             if s == 5:
+                p_quant(2, 2)
                 store_words(0, 4)
-        r_product(10)
-        r_exit(scopy, 10)
-        r_product(11)
-        r_exit(scopy, 11)
+            if s == 6:
+                p_quant(6, 2)
+
+        stage2(5)
         store_words(4, 8)
         store_scales(0, 8)
+        p_turn(8, 2)
+        p_exit(scopy, 8, 2)
+        p_cast(scopy, 10, 2, "r_late", 2)
         turn(14, 0)
         u_mult(14, 0)
-        p_cast(gcopy, 10, 2)
         turn(14, 1)
         u_mult(14, 1)
         turn(15, 0)
         u_mult(15, 0)
         turn(15, 1)
-        p_turn(8, 2)
-        p_exit(scopy, 8, 2)
-        r_product(12)
-        r_exit(scopy, 12)
-        r_product(13)
-        r_exit(scopy, 13)
+        stage2(6)
         u_quant(14, 1)
         u_mult(15, 1)
         last_quant(15, 0)
-        last_quant(15, 1)
         p_quant(8, 2)
+        last_quant(15, 1)
         p_turn(10, 2)
-        p_cast(vcopy, 12, 2, "r_late", 1)
+        p_cast(vcopy, 12, 2, "r_late", 2)
         p_exit(scopy, 10, 2)
         r_product(14)
         r_exit(scopy, 14)

@@ -505,14 +505,14 @@ def tile_convnextdroppathlayerscaleweightgrad_x1_kernel(tc, x, w1, b1, r, dy, ga
         e_group(scopy, 1, 1)
         h_product(2, 1)
         h_product(3, 1)
-        gelu(2, 1)
-        gelu(3, 1)
         turn(0, 1)
         u_mult(0, 1)
         turn(1, 1)
         u_mult(1, 1)
         turn(2, 0)
         u_mult(2, 0)
+        gelu(2, 1)
+        gelu(3, 1)
         stage1(2)
         w_pair_quant(3)
         e_quant(1)
@@ -528,8 +528,18 @@ def tile_convnextdroppathlayerscaleweightgrad_x1_kernel(tc, x, w1, b1, r, dy, ga
         u_quant(2, 2)
 
         for s in range(2, PAIRS - 1):
-            stage2(s - 2)
-            stage1(s + 1)
+            if s == 2:
+                h_product(7, 0)
+                h_product(7, 1)
+                stage2(0)
+                gelu(7, 0)
+                gelu(7, 1)
+                for g in range(G):
+                    h_product(6, g)
+                    gelu(6, g)
+            else:
+                stage2(s - 2)
+                stage1(s + 1)
             if s == 2:
                 w_run(10, 12)
             if s == 3:
@@ -557,7 +567,8 @@ def tile_convnextdroppathlayerscaleweightgrad_x1_kernel(tc, x, w1, b1, r, dy, ga
             if s > 2:
                 early_exit(vcopy if s % 2 == 0 else scopy, 2 * s + 1)
             for i in planes:
-                p_exit(vcopy if i < 4 else scopy, i, 2)
+                if i < 6:
+                    p_exit(vcopy if i < 4 else scopy, i, 2)
             if s < PAIRS - 2:
                 early_mult(2 * s + 3)
             if s == 2:
@@ -573,40 +584,40 @@ def tile_convnextdroppathlayerscaleweightgrad_x1_kernel(tc, x, w1, b1, r, dy, ga
             if s == 5:
                 p_quant(2, 2)
                 store_words(0, 4)
-            if s == 6:
-                p_quant(6, 2)
 
         stage2(5)
-        store_words(4, 8)
-        store_scales(0, 8)
-        p_turn(8, 2)
-        p_exit(scopy, 8, 2)
-        p_cast(scopy, 10, 2, "r_late", 2)
+        store_words(4, 6)
+        store_scales(0, 6)
+        p_exit(scopy, 6, 2)
         turn(14, 0)
         u_mult(14, 0)
+        p_cast(gcopy, 10, 2, "u0")
         turn(14, 1)
         u_mult(14, 1)
         turn(15, 0)
         u_mult(15, 0)
         turn(15, 1)
+        p_turn(8, 2)
+        p_exit(scopy, 8, 2)
         stage2(6)
-        u_quant(14, 1)
         u_mult(15, 1)
+        u_quant(14, 1)
         last_quant(15, 0)
-        p_quant(8, 2)
+        p_quant(6, 2)
         last_quant(15, 1)
         p_turn(10, 2)
-        p_cast(vcopy, 12, 2, "r_late", 2)
+        p_cast(vcopy, 12, 2, "r_late", 1)
         p_exit(scopy, 10, 2)
         r_product(14)
         r_exit(scopy, 14)
         p_product(15, 0)
         p_product(15, 1)
         r_product(15)
+        p_quant(8, 2)
         p_cast(vcopy, 14, 1, "r_last", 1)
         d_exit(scopy, 15)
         p_quant(10, 2)
-        store_words(8, 12)
+        store_words(6, 12)
         p_turn(12, 2)
         p_turn(14, 1)
         r_exit(vcopy, 15)
@@ -616,4 +627,4 @@ def tile_convnextdroppathlayerscaleweightgrad_x1_kernel(tc, x, w1, b1, r, dy, ga
         p_quant(12, 2)
         p_quant(14, 1)
         store_words(12, 16)
-        store_scales(8, 16)
+        store_scales(6, 16)

@@ -20,11 +20,11 @@ P = 128
 G = N // 512
 TILES = F // P
 PAIRS = TILES // 2
-W_LOADS = ((0, 4), (4, 8), (8, 12), (12, 16))
-LONG_CAST = 2
 BANKS = 8
+W_LOADS = ((0, 4), (4, 8), (8, 12), (12, 16))
 EARLY = (7, 9, 11, 13)
-A_BUFS = 12
+A_BUFS = 14
+SLOTS = 13
 
 
 def tile_convnextdroppathlayerscaleweightgrad_x1_kernel(tc, x, w1, b1, r, dy, gamma, out_0, out_1, out_2):
@@ -32,7 +32,7 @@ def tile_convnextdroppathlayerscaleweightgrad_x1_kernel(tc, x, w1, b1, r, dy, ga
     vcopy, scopy = nc.vector.tensor_copy, nc.scalar.copy
     with ExitStack() as ctx:
         keep = ctx.enter_context(tc.tile_pool(name="keep", bufs=1))
-        work = ctx.enter_context(tc.tile_pool(name="work", bufs=3))
+        work = ctx.enter_context(tc.tile_pool(name="work", bufs=1))
         psum = ctx.enter_context(tc.psum_pool(name="psum", bufs=1))
         ctx.enter_context(tc.manual_schedule())
 
@@ -44,7 +44,6 @@ def tile_convnextdroppathlayerscaleweightgrad_x1_kernel(tc, x, w1, b1, r, dy, ga
         r_sb = keep.tile([P, G, 4], BF16, name="r_sb")
         warm = keep.tile([P, 1], F32, name="warm")
         x_raw = {(g, h): keep.tile([P, 2 * C], BF16, name=f"x_raw{g}{h}") for g in range(G) for h in range(2)}
-        x_bf = [keep.tile([P, 4 * P, 4], BF16, name=f"x_bf{g}", align_bytes=64) for g in range(G)]
         x_codes = keep.tile([P, G, 512], U32, name="x_codes", align_bytes=64)
         x_scales = keep.tile([P, G, 512], U8, name="x_scales", align_bytes=64)
         w_raw = {}
@@ -56,24 +55,45 @@ def tile_convnextdroppathlayerscaleweightgrad_x1_kernel(tc, x, w1, b1, r, dy, ga
         w_scales = keep.tile([P, F], U8, name="w_scales", align_bytes=64)
         dy_raw = {(g, h): keep.tile([P, 2, C], BF16, name=f"dy_raw{g}{h}") for g in range(G) for h in range(2)}
         e_nat = [keep.tile([P, 2, 4, P, 2], BF16, name=f"e_nat{g}") for g in range(G)]
-        e_bf = [work.tile([P, C, 4], BF16, name=f"e_bf{g}", tag=f"grouped{g}", bufs=1, align_bytes=64) for g in range(G)]
         e_codes = keep.tile([P, G, C], U32, name="e_codes", align_bytes=64)
         e_scales = keep.tile([P, G, C], U8, name="e_scales", align_bytes=64)
         p_codes = keep.tile([P, F], U32, name="p_codes", align_bytes=64)
         p_scales = keep.tile([P, F], U8, name="p_scales", align_bytes=64)
 
-        free = list(range(BANKS))
+        free_banks = list(range(BANKS))
+        free_slots = list(range(SLOTS))
         held = {}
 
         def new_bank(shape, dtype, name, key):
-            held[key] = free.pop(0)
-            return psum.tile(shape, dtype, name=name, tag=f"bank{held[key]}", bufs=1)
+            held[key] = free_banks.pop(0)
+            return psum.tile(shape, dtype, name=name, tag=f"bank{held[key]}")
 
         def emptied(key):
-            free.append(held[key])
+            free_banks.append(held[key])
+
+        def new_slot(shape, name, key, newest=False):
+            held[key] = free_slots.pop(-1 if newest else 0)
+            return work.tile(shape, BF16, name=name, tag=f"slot{held[key]}", align_bytes=64)
+
+        def used_up(key):
+            free_slots.append(held[key])
 
         def gcopy(out, in_):
             nc.gpsimd.tensor_scalar(out=out, in0=in_, scalar1=1.0, scalar2=0.0, op0=MULT, op1=ADD)
+
+        def quantize(codes, scales, values):
+            nc.vector.quantize_mx(out=codes.bitcast(FP8X4), scales=scales, in_=values)
+
+        def product(out, stat, stat_scales, mov, mov_scales, start=True, stop=True):
+            nc.tensor.matmul_mx(
+                out=out,
+                lhsT=stat.bitcast(FP8X4),
+                lhsT_scale=stat_scales,
+                rhs=mov.bitcast(FP8X4),
+                rhs_scale=mov_scales,
+                start=start,
+                stop=stop,
+            )
 
         def load_x(g, h):
             src = x[512 * g : 512 * g + 512, :].rearrange("(m h t) k -> m h (t k)", h=2, t=2)
@@ -87,30 +107,37 @@ def tile_convnextdroppathlayerscaleweightgrad_x1_kernel(tc, x, w1, b1, r, dy, ga
             src = dy[512 * g : 512 * g + 512, :].rearrange("(p j) c -> p j c", j=4)
             nc.sync.dma_start(out=dy_raw[g, h][:], in_=src[:, 2 * h : 2 * h + 2, :])
 
+        def load_gamma(queue):
+            queue.dma_start(out=gcols[:], in_=gamma.rearrange("(k q) -> k q", q=4))
+
+        def load_bias(queue):
+            queue.dma_start(out=b_rows[0:TILES, :], in_=b1.rearrange("(i f) -> i f", f=P))
+
+        def load_r(queue):
+            queue.dma_start(out=r_sb[:], in_=r.rearrange("(g p t) -> p g t", g=G, t=4))
+
         x_turned = {}
+        x_bf = {}
 
         def x_turn(g, h):
             words = x_raw[g, h][:].bitcast(F32)
-            x_turned[g, h] = new_bank([P, 2, 2, P], F32, "x_bank", ("x", g, h))
+            x_turned[g, h] = new_bank([P, 2, 2, P], F32, "x_bank", ("xb", g, h))
             for n in range(2):
-                for u in range(2):
-                    nc.tensor.transpose(x_turned[g, h][:, n, u, :], words[:, 256 * n + u : 256 * (n + 1) : 2], ident[:])
+                for v in range(2):
+                    nc.tensor.transpose(x_turned[g, h][:, n, v, :], words[:, 256 * n + v : 256 * (n + 1) : 2], ident[:])
 
         def x_exit(copy, g, h):
-            dst = x_bf[g][:, 256 * h : 256 * h + 256, :].rearrange("p c j -> p (c j)").bitcast(F32)
+            x_bf[g, h] = new_slot([P, 1024], "x_bf", ("x", g, h))
             copy(
-                out=dst.rearrange("p (t m u) -> p t m u", t=2, u=2),
-                in_=x_turned[g, h][:].rearrange("p t u m -> p t m u"),
+                out=x_bf[g, h][:].bitcast(F32).rearrange("p (t m v) -> p t m v", t=2, v=2),
+                in_=x_turned[g, h][:].rearrange("p t v m -> p t m v"),
             )
-            emptied(("x", g, h))
+            emptied(("xb", g, h))
 
-        def x_quant(g, h0, h1):
-            c = slice(256 * h0, 256 * h1)
-            nc.vector.quantize_mx(
-                out=x_codes[:, g, c].bitcast(FP8X4),
-                scales=x_scales[:, g, c],
-                in_=x_bf[g][:, c, :].rearrange("p c j -> p (c j)"),
-            )
+        def x_quant(g, h):
+            c = slice(256 * h, 256 * h + 256)
+            quantize(x_codes[:, g, c], x_scales[:, g, c], x_bf[g, h][:])
+            used_up(("x", g, h))
 
         small = {}
 
@@ -125,8 +152,8 @@ def tile_convnextdroppathlayerscaleweightgrad_x1_kernel(tc, x, w1, b1, r, dy, ga
         def gamma_turn():
             bank = small["g"] = new_bank([P, 2, P], F32, "g_bank", "g")
             words = gcols[:].bitcast(F32)
-            for u in range(2):
-                nc.tensor.transpose(bank[:, u, :], words[:, u : u + 1].to_broadcast([P, P]), ident[:])
+            for v in range(2):
+                nc.tensor.transpose(bank[:, v, :], words[:, v : v + 1].to_broadcast([P, P]), ident[:])
 
         def r_turn():
             bank = small["r"] = new_bank([P, 2 * G, P], F32, "r_spread", "r")
@@ -136,32 +163,22 @@ def tile_convnextdroppathlayerscaleweightgrad_x1_kernel(tc, x, w1, b1, r, dy, ga
 
         w_bf = {}
 
-        def w_tile(i0, i1, tag, bufs):
-            tile = work.tile([P, (i1 - i0) * P, 4], BF16, name="w_bf", tag=tag, bufs=bufs, align_bytes=64)
-            for i in range(i0, i1):
-                w_bf[i] = tile, i - i0
-
-        def w_group(copy, i0, i1):
+        def w_group(copy, i0, i1, newest=False):
             raw, at = w_raw[i0]
-            tile, to = w_bf[i0]
+            dst = w_bf[i0] = new_slot([P, (i1 - i0) * P, 4], "w_bf", ("w", i0), newest)
             src = raw[:, :, at * P : (at + i1 - i0) * P]
-            dst = tile[:, to * P : (to + i1 - i0) * P, :]
             if copy is gcopy:
-                gcopy(out=dst, in_=src.rearrange("p j c -> p c j"))
+                gcopy(out=dst[:], in_=src.rearrange("p j c -> p c j"))
             else:
-                copy(out=dst.rearrange("p (c q) j -> p c j q", q=4), in_=src.rearrange("p j (c q) -> p c j q", q=4))
+                copy(out=dst[:].rearrange("p (c q) j -> p c j q", q=4), in_=src.rearrange("p j (c q) -> p c j q", q=4))
 
         def w_quant(i0, i1):
-            tile, to = w_bf[i0]
             c = slice(i0 * P, i1 * P)
-            nc.vector.quantize_mx(
-                out=w_codes[:, c].bitcast(FP8X4),
-                scales=w_scales[:, c],
-                in_=tile[:, to * P : (to + i1 - i0) * P, :].rearrange("p c j -> p (c j)"),
-            )
+            quantize(w_codes[:, c], w_scales[:, c], w_bf[i0][:].rearrange("p c j -> p (c j)"))
+            used_up(("w", i0))
 
         def e_mult(g, h):
-            gam = small["g"][:].rearrange("p u k -> p (u k)").bitcast(BF16)
+            gam = small["g"][:].rearrange("p v k -> p (v k)").bitcast(BF16)
             nc.vector.tensor_tensor(
                 out=e_nat[g][:, :, 2 * h : 2 * h + 2],
                 in0=dy_raw[g, h][:].rearrange("p j (m v c) -> p v j m c", v=2, c=2),
@@ -171,55 +188,53 @@ def tile_convnextdroppathlayerscaleweightgrad_x1_kernel(tc, x, w1, b1, r, dy, ga
             if (g, h) == (G - 1, 1):
                 emptied("g")
 
-        def e_group(copy, g, v):
-            if copy is gcopy:
-                gcopy(
-                    out=e_bf[g][:, 2 * v * P : 2 * (v + 1) * P, :].rearrange("p (c m) j -> p c m j", c=2),
-                    in_=e_nat[g][:, v].rearrange("p j m c -> p c m j"),
-                )
-                return
-            copy(
-                out=e_bf[g][:, 2 * v * P : 2 * (v + 1) * P, :].rearrange("p (c n m) j -> p n j m c", c=2, m=2),
-                in_=e_nat[g][:, v].rearrange("p j (n m) c -> p n j m c", m=2),
-            )
+        e_bf = {}
 
-        def e_quant(g):
-            nc.vector.quantize_mx(
-                out=e_codes[:, g, :].bitcast(FP8X4),
-                scales=e_scales[:, g, :],
-                in_=e_bf[g][:].rearrange("p c j -> p (c j)"),
-            )
+        def e_group(copy, g, v, newest=False):
+            dst = e_bf[g, v] = new_slot([P, 2 * P, 4], "e_bf", ("e", g, v), newest)
+            if copy is gcopy:
+                gcopy(out=dst[:].rearrange("p (c m) j -> p c m j", c=2), in_=e_nat[g][:, v].rearrange("p j m c -> p c m j"))
+            else:
+                copy(
+                    out=dst[:].rearrange("p (c n m) j -> p n j m c", c=2, m=2),
+                    in_=e_nat[g][:, v].rearrange("p j (n m) c -> p n j m c", m=2),
+                )
+
+        def e_quant(g, v):
+            c = slice(256 * v, 256 * v + 256)
+            quantize(e_codes[:, g, c], e_scales[:, g, c], e_bf[g, v][:].rearrange("p c j -> p (c j)"))
+            used_up(("e", g, v))
 
         a = {}
         h_bank = {}
 
-        def h_product(i, g):
-            bank = h_bank[i, g] = new_bank([P, 512], F32, "h_bank", ("h", i, g))
+        def h_product(i, g, h=None):
             c = slice(i * P, (i + 1) * P)
-            nc.tensor.matmul_mx(
-                out=bank[:],
-                lhsT=w_codes[:, c].bitcast(FP8X4),
-                lhsT_scale=w_scales[:, c],
-                rhs=x_codes[:, g, :].bitcast(FP8X4),
-                rhs_scale=x_scales[:, g, :],
-                start=True,
-                stop=True,
-            )
+            t = slice(0, 512) if h is None else slice(256 * h, 256 * h + 256)
+            bank = h_bank[i, g, h] = new_bank([P, t.stop - t.start], F32, "h_bank", ("h", i, g, h))
+            product(bank[:], w_codes[:, c], w_scales[:, c], x_codes[:, g, t], x_scales[:, g, t])
 
-        def gelu(i, g):
+        def gelu(i, g, h=None):
+            src = h_bank[i, g, h][:]
             if i in EARLY:
                 if g == 0:
-                    a[i] = work.tile([P, G, 512], F32, name="a_wide", bufs=2)
+                    a[i] = work.tile([P, G, 512], F32, name="a_wide", bufs=3)
                 dst = a[i][:, g, :].rearrange("p (v m e) -> p v m e", v=2, e=2)
-                src = h_bank[i, g][:].rearrange("p (v e m) -> p v m e", v=2, e=2)
+                src = src.rearrange("p (v e m) -> p v m e", v=2, e=2)
             else:
-                a[i, g] = work.tile([P, 512], F32, name="a_sb", bufs=A_BUFS)
-                dst, src = a[i, g][:], h_bank[i, g][:]
+                if not h:
+                    a[i, g] = work.tile([P, 512], F32, name="a_sb", bufs=A_BUFS)
+                dst = a[i, g][:] if h is None else a[i, g][:, 256 * h : 256 * h + 256]
             nc.scalar.activation(out=dst, in_=src, func=GELU, bias=bias[:, i : i + 1])
-            emptied(("h", i, g))
+            emptied(("h", i, g, h))
 
         turned = {}
         u = {}
+
+        def u_tile(i):
+            if i // 2 not in u:
+                u[i // 2] = new_slot([P, 2, G, P, 4], "u_bf", ("u", i // 2))
+            return u[i // 2]
 
         def turn(i, g):
             turned[i, g] = new_bank([P, 4, P], F32, "t_bank", ("t", i, g))
@@ -227,10 +242,8 @@ def tile_convnextdroppathlayerscaleweightgrad_x1_kernel(tc, x, w1, b1, r, dy, ga
                 nc.tensor.transpose(turned[i, g][:, t, :], a[i, g][:, t * P : (t + 1) * P], ident[:])
 
         def u_mult(i, g):
-            if i // 2 not in u:
-                u[i // 2] = work.tile([P, 2, G, P, 4], BF16, name="u_bf", tag=f"u{i // 2 % 3}", bufs=1, align_bytes=64)
             nc.vector.tensor_tensor(
-                out=u[i // 2][:, i % 2, g, :, :],
+                out=u_tile(i)[:, i % 2, g, :, :],
                 in0=turned[i, g][:].rearrange("p t f -> p f t"),
                 in1=r_sb[:, g, :].unsqueeze(1).to_broadcast([P, P, 4]),
                 op=MULT,
@@ -259,112 +272,101 @@ def tile_convnextdroppathlayerscaleweightgrad_x1_kernel(tc, x, w1, b1, r, dy, ga
                     nc.tensor.transpose(turned[i][:, g, v, :], words[:, n * P : (n + 1) * P], ident[:])
 
         def early_exit(copy, i):
-            if i // 2 not in u:
-                u[i // 2] = work.tile([P, 2, G, P, 4], BF16, name="u_bf", tag=f"u{i // 2 % 3}", bufs=1, align_bytes=64)
-            dst = u[i // 2][:, i % 2].rearrange("p g f t -> p (g f t)").bitcast(F32)
+            dst = u_tile(i)[:, i % 2].rearrange("p g f t -> p (g f t)").bitcast(F32)
             copy(out=dst.rearrange("p (g f v) -> p g f v", g=G, v=2), in_=turned[i][:].rearrange("p g v f -> p g f v"))
             emptied(("t", i))
 
         uq = {}
+        u_left = {j: 2 * G for j in range(PAIRS)}
 
-        def u_quant(i, n):
-            codes = work.tile([P, n, G, P], U32, name="u_codes", bufs=4, align_bytes=64)
-            scales = work.tile([P, n, G, P], U8, name="u_scales", bufs=4, align_bytes=64)
-            nc.vector.quantize_mx(
-                out=codes[:].rearrange("p n g f -> p (n g f)").bitcast(FP8X4),
-                scales=scales[:].rearrange("p n g f -> p (n g f)"),
-                in_=u[i // 2][:, i % 2 : i % 2 + n].rearrange("p n g f t -> p (n g f t)"),
-            )
-            for m in range(n):
-                uq[i + m] = codes[:, m], scales[:, m]
+        def u_quant(i, n, g=None):
+            if g is None:
+                codes = work.tile([P, n, G, P], U32, name="u_codes", bufs=4, align_bytes=64)
+                scales = work.tile([P, n, G, P], U8, name="u_scales", bufs=4, align_bytes=64)
+                quantize(
+                    codes[:].rearrange("p n g f -> p (n g f)"),
+                    scales[:].rearrange("p n g f -> p (n g f)"),
+                    u[i // 2][:, i % 2 : i % 2 + n].rearrange("p n g f t -> p (n g f t)"),
+                )
+                for m in range(n):
+                    uq[i + m] = codes[:, m], scales[:, m]
+                u_left[i // 2] -= n * G
+            else:
+                if i not in uq:
+                    codes = work.tile([P, G, P], U32, name="l_codes", bufs=2, align_bytes=64)
+                    scales = work.tile([P, G, P], U8, name="l_scales", bufs=2, align_bytes=64)
+                    uq[i] = codes, scales
+                codes, scales = uq[i]
+                quantize(codes[:, g, :], scales[:, g, :], u[i // 2][:, i % 2, g].rearrange("p f t -> p (f t)"))
+                u_left[i // 2] -= 1
+            if u_left[i // 2] == 0:
+                used_up(("u", i // 2))
 
         r_bank = {}
         p_bank = {}
-        r_out = {}
+        rows = {}
 
-        def r_product(i, groups=range(G)):
+        def r_product(i):
             codes, scales = uq[i]
-            if 0 in groups:
-                r_bank[i] = new_bank([P, C], F32, "r_bank", ("r", i))
-            for g in groups:
-                nc.tensor.matmul_mx(
-                    out=r_bank[i][:],
-                    lhsT=codes[:, g, :].bitcast(FP8X4),
-                    lhsT_scale=scales[:, g, :],
-                    rhs=e_codes[:, g, :].bitcast(FP8X4),
-                    rhs_scale=e_scales[:, g, :],
-                    start=(g == 0),
-                    stop=(g == G - 1),
-                )
+            r_bank[i] = new_bank([P, C], F32, "r_bank", ("r", i))
+            for g in range(G):
+                product(r_bank[i][:], codes[:, g, :], scales[:, g, :], e_codes[:, g, :], e_scales[:, g, :], g == 0, g == G - 1)
 
         def r_exit(copy, i):
-            if i == LONG_CAST:
-                four = work.tile([P, 4, C], F32, name="r_four", bufs=1)
-                r_out["four"], r_out[i // 2], r_out[i // 2 + 1] = four, four[:, 0:2, :], four[:, 2:4, :]
-            if i // 2 not in r_out:
-                r_out[i // 2] = work.tile([P, 2, C], F32, name="r_out", bufs=4)
-            dst = r_out[i // 2][:, i % 2, :]
-            copy(
-                out=dst.rearrange("p (m t) -> p m t", t=4),
-                in_=r_bank[i][:].rearrange("p (t m) -> p m t", t=4),
-            )
+            if i // 4 not in rows:
+                rows[i // 4] = work.tile([P, 4, C], F32, name="rows", bufs=4)
+            dst = rows[i // 4][:, i % 4, :]
+            copy(out=dst.rearrange("p (m t) -> p m t", t=4), in_=r_bank[i][:].rearrange("p (t m) -> p m t", t=4))
             emptied(("r", i))
             nc.sync.dma_start(out=out_0[i * P : (i + 1) * P, :], in_=dst)
-
-        def last_quant(i, g):
-            if g == 0:
-                codes = work.tile([P, G, P], U32, name="l_codes", bufs=1, align_bytes=64)
-                scales = work.tile([P, G, P], U8, name="l_scales", bufs=1, align_bytes=64)
-                uq[i] = codes, scales
-            codes, scales = uq[i]
-            nc.vector.quantize_mx(
-                out=codes[:, g, :].bitcast(FP8X4),
-                scales=scales[:, g, :],
-                in_=u[i // 2][:, i % 2, g].rearrange("p f t -> p (f t)"),
-            )
 
         def p_product(i, g):
             codes, scales = uq[i]
             if g == 0:
                 p_bank[i] = new_bank([P, 4, P], F32, "d_bank", ("p", i))
             for t in range(4):
-                nc.tensor.matmul_mx(
-                    out=p_bank[i][:, t, :],
-                    lhsT=e_codes[:, g, t * P : (t + 1) * P].bitcast(FP8X4),
-                    lhsT_scale=e_scales[:, g, t * P : (t + 1) * P],
-                    rhs=codes[:, g, :].bitcast(FP8X4),
-                    rhs_scale=scales[:, g, :],
-                    start=(g == 0 and t == 0),
-                    stop=(g == G - 1 and t == 3),
-                )
+                c = slice(t * P, (t + 1) * P)
+                first, last = g == 0 and t == 0, g == G - 1 and t == 3
+                product(p_bank[i][:, t, :], e_codes[:, g, c], e_scales[:, g, c], codes[:, g, :], scales[:, g, :], first, last)
 
         r_bf = {}
+        cast_left = {}
         p_bf = {}
 
-        def p_cast(copy, i, n, tag, bufs=1):
-            cast = work.tile([P, 2, n * P, 2], BF16, name="cast", tag=tag, bufs=bufs, align_bytes=64)
-            src = r_out["four"][:] if n == 4 else r_out[i // 2][:, i % 2 : i % 2 + n, :]
+        def p_cast(copy, i, n, newest=False):
+            cast = new_slot([P, 2, n * P, 2], "cast", ("c", i), newest)
+            src = rows[i // 4][:, i % 4 : i % 4 + n, :]
             copy(out=cast[:], in_=src.rearrange("p n (m v c) -> p v (n m) c", v=2, c=2))
             words = cast[:].rearrange("p v m c -> p (v m c)").bitcast(F32)
+            cast_left[i] = n
             for m in range(n):
-                r_bf[i + m] = [words[:, (n * v + m) * P : (n * v + m + 1) * P] for v in range(2)]
+                r_bf[i + m] = i, [words[:, (n * v + m) * P : (n * v + m + 1) * P] for v in range(2)]
 
         def p_turn(i, n):
             p_bank[i] = new_bank([P, n, 2, P], F32, "p_bank", ("p", i))
             for m in range(n):
+                first, words = r_bf[i + m]
                 for v in range(2):
-                    nc.tensor.transpose(p_bank[i][:, m, v, :], r_bf[i + m][v], ident[:])
+                    nc.tensor.transpose(p_bank[i][:, m, v, :], words[v], ident[:])
+                cast_left[first] -= 1
+                if cast_left[first] == 0:
+                    used_up(("c", first))
 
         def p_exit(copy, i, n):
-            p_bf[i] = work.tile([P, n * P, 4], BF16, name="p_bf", bufs=4, align_bytes=64)
+            p_bf[i] = new_slot([P, n * P, 4], "p_bf", ("q", i))
             dst = p_bf[i][:].rearrange("p f c -> p (f c)").bitcast(F32)
             copy(out=dst.rearrange("p (n f v) -> p n f v", n=n, v=2), in_=p_bank[i][:].rearrange("p n v f -> p n f v"))
             emptied(("p", i))
 
         def d_exit(copy, i):
-            p_bf[i] = work.tile([P, P, 4], BF16, name="p_bf", bufs=4, align_bytes=64)
+            p_bf[i] = new_slot([P, P, 4], "p_bf", ("q", i))
             copy(out=p_bf[i][:], in_=p_bank[i][:].rearrange("p t f -> p f t"))
             emptied(("p", i))
+
+        def p_quant(i, n):
+            c = slice(i * P, (i + n) * P)
+            quantize(p_codes[:, c], p_scales[:, c], p_bf[i][:].rearrange("p f c -> p (f c)"))
+            used_up(("q", i))
 
         def store_words(i0, i1):
             nc.sync.dma_start(
@@ -380,241 +382,176 @@ def tile_convnextdroppathlayerscaleweightgrad_x1_kernel(tc, x, w1, b1, r, dy, ga
                     in_=p_scales[32 * quadrant : 32 * quadrant + 4, i0 * P : i1 * P].bitcast(I32),
                 )
 
-        def p_quant(i, n):
-            c = slice(i * P, (i + n) * P)
-            nc.vector.quantize_mx(
-                out=p_codes[:, c].bitcast(FP8X4),
-                scales=p_scales[:, c],
-                in_=p_bf[i][:].rearrange("p f c -> p (f c)"),
-            )
+        def expand(i, g, h=None):
+            h_product(i, g, h)
+            gelu(i, g, h)
 
-        def halves(j):
-            return [(2 * j + m, g) for m in range(2) for g in range(G)]
+        def weigh(i, g):
+            turn(i, g)
+            u_mult(i, g)
 
-        def stage1(j):
-            for i, g in sorted(halves(j), key=lambda ig: ig[0] not in EARLY):
-                h_product(i, g)
-                gelu(i, g)
-
-        def stage2(j):
-            for i in (2 * j, 2 * j + 1):
-                r_product(i)
-                r_exit(scopy, i)
-
-        def turns(j):
-            for i, g in halves(j):
-                turn(i, g)
-                u_mult(i, g)
-
-        def load_gamma():
-            nc.sync.dma_start(out=gcols[:], in_=gamma.rearrange("(k q) -> k q", q=4))
-
-        def load_bias():
-            nc.sync.dma_start(out=b_rows[0:TILES, :], in_=b1.rearrange("(i f) -> i f", f=P))
-
-        def load_r():
-            nc.sync.dma_start(out=r_sb[:], in_=r.rearrange("(g p t) -> p g t", g=G, t=4))
-
-        def expand(j, g):
-            for i in (2 * j, 2 * j + 1):
-                h_product(i, g)
-                gelu(i, g)
-
-        def weigh(j, g):
-            for i in (2 * j, 2 * j + 1):
-                turn(i, g)
-                u_mult(i, g)
-
-        def w_pair(copy, j, tag="w_one", bufs=1):
-            w_tile(2 * j, 2 * j + 2, tag, bufs)
-            w_group(copy, 2 * j, 2 * j + 2)
-
-        def w_run(i0, i1):
-            w_tile(i0, i1, "grouped1", 1)
-            w_group(gcopy, i0, i1)
-
-        def w_pair_quant(j):
-            w_quant(2 * j, 2 * j + 2)
+        def result(copy, i):
+            r_product(i)
+            r_exit(copy, i)
 
         nc.vector.memset(warm[:], 0.0)
         nc.vector.memset(b_rows[:], 0.0)
         make_identity(nc, ident[:])
         make_identity(nc, ident_bf[:])
         nc.scalar.activation(out=warm[:], in_=warm[:], func=GELU)
-
-        load_gamma()
-        load_dy(0, 0)
-        load_dy(0, 1)
         load_x(0, 0)
         load_x(0, 1)
-        load_w(*W_LOADS[0])
-        load_bias()
+        load_w(0, 4)
+        load_bias(nc.sync)
+        load_gamma(nc.sync)
         load_x(1, 0)
         load_x(1, 1)
-        load_w(*W_LOADS[1])
+        load_w(4, 8)
+        load_dy(0, 0)
+        load_dy(0, 1)
+        load_r(nc.sync)
         load_dy(1, 0)
         load_dy(1, 1)
-        load_r()
-        load_w(*W_LOADS[2])
-        load_w(*W_LOADS[3])
-
+        load_w(8, 12)
+        load_w(12, 16)
+        for h in range(2):
+            x_turn(0, h)
+            x_exit(scopy, 0, h)
+        bias_turn()
         gamma_turn()
+        x_quant(0, 0)
+        w_group(vcopy, 0, 2)
+        w_group(scopy, 2, 4)
+        x_quant(0, 1)
+        w_quant(0, 2)
+        w_quant(2, 4)
+        bias_exit(vcopy)
+        for h in range(2):
+            x_turn(1, h)
+            x_exit(scopy, 1, h)
+        for i in range(4):
+            expand(i, 0)
+        x_quant(1, 0)
+        w_group(vcopy, 4, 6)
+        x_quant(1, 1)
+        w_group(gcopy, 6, 8, True)
+        w_quant(4, 6)
+        for i in range(4):
+            expand(i, 1)
         e_mult(0, 0)
         e_mult(0, 1)
-        e_group(scopy, 0, 0)
-        e_group(gcopy, 0, 1)
-        x_turn(0, 0)
-        x_exit(vcopy, 0, 0)
-        x_turn(0, 1)
-        x_exit(vcopy, 0, 1)
-        w_pair(vcopy, 0, "w_bf", 4)
-        w_pair(scopy, 1, "w_bf", 4)
-        bias_turn()
-        bias_exit(scopy)
-        x_turn(1, 0)
-        x_exit(scopy, 1, 0)
-        x_turn(1, 1)
-        x_exit(scopy, 1, 1)
-        x_quant(0, 0, 2)
-        w_pair_quant(0)
-        w_pair_quant(1)
-        e_quant(0)
-        x_quant(1, 0, 2)
-        w_pair(vcopy, 2, "w_one", 1)
-        h_product(0, 0)
-        h_product(1, 0)
-        h_product(2, 0)
-        gelu(0, 0)
-        gelu(1, 0)
-        gelu(2, 0)
-        h_product(0, 1)
-        h_product(1, 1)
-        h_product(3, 0)
-        gelu(0, 1)
-        gelu(1, 1)
+        e_group(gcopy, 0, 0)
+        for i in range(4):
+            turn(i, 0)
         e_mult(1, 0)
-        w_pair_quant(2)
         e_mult(1, 1)
-        w_pair(gcopy, 3, "w_one", 1)
-        e_group(gcopy, 1, 0)
-        turn(0, 0)
         u_mult(0, 0)
-        turn(1, 0)
         u_mult(1, 0)
-        gelu(3, 0)
-        e_group(scopy, 1, 1)
-        h_product(2, 1)
-        h_product(3, 1)
-        turn(0, 1)
-        u_mult(0, 1)
-        turn(1, 1)
-        u_mult(1, 1)
-        turn(2, 0)
+        w_group(gcopy, 8, 10)
         u_mult(2, 0)
-        gelu(2, 1)
-        gelu(3, 1)
-        stage1(2)
-        w_pair_quant(3)
-        e_quant(1)
-        u_quant(0, 2)
-        w_pair(gcopy, 4, "grouped1", 1)
-        turn(3, 0)
+        for i in (4, 5):
+            expand(i, 0)
+            expand(i, 1)
         u_mult(3, 0)
-        turn(2, 1)
-        u_mult(2, 1)
-        turn(3, 1)
-        u_mult(3, 1)
-        w_pair_quant(4)
+        w_quant(6, 8)
+        e_quant(0, 0)
+        e_group(gcopy, 0, 1, True)
+        w_quant(8, 10)
+        e_group(gcopy, 1, 0)
+        for i in range(4):
+            weigh(i, 1)
+        for i in (7, 6):
+            expand(i, 0)
+            expand(i, 1)
+        e_group(scopy, 1, 1)
+        weigh(4, 0)
+        weigh(4, 1)
+        r_turn()
+        for i in (9, 8):
+            expand(i, 0)
+            expand(i, 1)
+        e_quant(0, 1)
+        e_quant(1, 0)
+        u_quant(0, 2)
+        e_quant(1, 1)
+        w_group(gcopy, 10, 12, True)
         u_quant(2, 2)
-
-        for s in range(2, PAIRS - 1):
-            if s == 2:
-                h_product(7, 0)
-                h_product(7, 1)
-                stage2(0)
-                gelu(7, 0)
-                gelu(7, 1)
-                for g in range(G):
-                    h_product(6, g)
-                    gelu(6, g)
-            else:
-                stage2(s - 2)
-                stage1(s + 1)
-            if s == 2:
-                w_run(10, 12)
-            if s == 3:
-                w_run(12, 16)
-            turn(2 * s, 0)
-            u_mult(2 * s, 0)
-            turn(2 * s, 1)
-            u_mult(2 * s, 1)
-            if s == 2:
-                turn(5, 0)
-                u_mult(5, 0)
-                turn(5, 1)
-                u_mult(5, 1)
-                r_turn()
-                p_cast(gcopy, 0, 2, "u1")
-            else:
-                early_turn(2 * s + 1)
-            if s == 4:
-                p_cast(gcopy, 2, 4, "u0")
+        turn(5, 0)
+        turn(5, 1)
+        for i in range(4):
+            result(scopy, i)
+        early_mult(7)
+        u_mult(5, 0)
+        u_mult(5, 1)
+        w_quant(10, 12)
+        w_group(gcopy, 12, 16, True)
+        u_quant(4, 2)
+        for s in range(3, PAIRS - 1):
             if s > 4:
-                p_cast(gcopy, 2 * (s - 2), 2, f"u{(s - 1) % 3}")
-            planes = {3: (0,), 5: (2, 4), 6: (6,)}.get(s, ())
+                result(scopy, 2 * s - 4)
+                result(scopy, 2 * s - 3)
+            if s > 3:
+                for i in ((2 * s + 3, 2 * s + 2) if 2 * s + 3 in EARLY else (2 * s + 2, 2 * s + 3)):
+                    expand(i, 0)
+                    expand(i, 1)
+            if s == 4:
+                result(scopy, 4)
+                result(scopy, 5)
+            if s == 5:
+                p_cast(gcopy, 4, 4, True)
+            if s == 6:
+                p_cast(gcopy, 8, 2, True)
+            weigh(2 * s, 0)
+            weigh(2 * s, 1)
+            early_turn(2 * s + 1)
+            planes = {5: (0, 2), 6: (4, 6)}.get(s, ())
             for i in planes:
                 p_turn(i, 2)
-            if s > 2:
-                early_exit(vcopy if s % 2 == 0 else scopy, 2 * s + 1)
+            early_exit(vcopy if s in (3, 4, 6) else scopy, 2 * s + 1)
             for i in planes:
                 if i < 6:
-                    p_exit(vcopy if i < 4 else scopy, i, 2)
+                    p_exit(vcopy if i in (0,) else scopy, i, 2)
             if s < PAIRS - 2:
                 early_mult(2 * s + 3)
-            if s == 2:
-                w_quant(10, 12)
-
             if s == 6:
-                p_quant(4, 2)
-            u_quant(2 * s, 2)
-            if s == 3:
-                w_quant(12, 16)
-            if s == 4:
-                p_quant(0, 2)
-            if s == 5:
                 p_quant(2, 2)
                 store_words(0, 4)
-
-        stage2(5)
+            u_quant(2 * s, 2)
+            if s == 3:
+                p_cast(gcopy, 0, 4, True)
+                w_quant(12, 16)
+            if s == 5:
+                p_quant(0, 2)
+            if s == 6:
+                p_quant(4, 2)
+        result(scopy, 10)
+        result(scopy, 11)
         store_words(4, 6)
         store_scales(0, 6)
         p_exit(scopy, 6, 2)
-        turn(14, 0)
-        u_mult(14, 0)
-        p_cast(gcopy, 10, 2, "u0")
-        turn(14, 1)
-        u_mult(14, 1)
-        turn(15, 0)
-        u_mult(15, 0)
+        weigh(14, 0)
+        p_cast(gcopy, 10, 2, True)
+        weigh(14, 1)
+        weigh(15, 0)
         turn(15, 1)
         p_turn(8, 2)
         p_exit(scopy, 8, 2)
-        stage2(6)
+        result(scopy, 12)
+        result(scopy, 13)
         u_mult(15, 1)
         u_quant(14, 1)
-        last_quant(15, 0)
+        u_quant(15, 1, 0)
         p_quant(6, 2)
-        last_quant(15, 1)
+        u_quant(15, 1, 1)
         p_turn(10, 2)
-        p_cast(vcopy, 12, 2, "r_late", 1)
+        p_cast(vcopy, 12, 2)
         p_exit(scopy, 10, 2)
-        r_product(14)
-        r_exit(scopy, 14)
+        result(scopy, 14)
         p_product(15, 0)
         p_product(15, 1)
         r_product(15)
         p_quant(8, 2)
-        p_cast(vcopy, 14, 1, "r_last", 1)
+        p_cast(vcopy, 14, 1)
         d_exit(scopy, 15)
         p_quant(10, 2)
         store_words(6, 12)

@@ -458,18 +458,28 @@ def tile_convnextdroppathlayerscaleweightgrad_x1_kernel(tc, x, w1, b1, r, dy, ga
         e_group(gcopy, 0, 1, True)
         w_quant(8, 10)
         e_group(gcopy, 1, 0)
-        for i in range(4):
-            weigh(i, 1)
-        for i in (7, 6):
-            expand(i, 0)
-            expand(i, 1)
         e_group(scopy, 1, 1)
-        weigh(4, 0)
-        weigh(4, 1)
-        r_turn()
-        for i in (9, 8):
-            expand(i, 0)
-            expand(i, 1)
+        for i in range(4):
+            turn(i, 1)
+        u_mult(0, 1)
+        u_mult(1, 1)
+        turn(4, 0)
+        turn(4, 1)
+        u_mult(2, 1)
+        for i in (7, 6):
+            h_product(i, 0)
+            h_product(i, 1)
+        u_mult(3, 1)
+        u_mult(4, 0)
+        gelu(7, 0)
+        h_product(9, 0)
+        h_product(9, 1)
+        u_mult(4, 1)
+        gelu(7, 1)
+        gelu(6, 0)
+        gelu(6, 1)
+        gelu(9, 0)
+        gelu(9, 1)
         e_quant(0, 1)
         e_quant(1, 0)
         u_quant(0, 2)
@@ -478,11 +488,16 @@ def tile_convnextdroppathlayerscaleweightgrad_x1_kernel(tc, x, w1, b1, r, dy, ga
         u_quant(2, 2)
         turn(5, 0)
         turn(5, 1)
+        r_turn()
+        turn(6, 0)
+        turn(6, 1)
+        u_mult(5, 0)
+        u_mult(5, 1)
+        expand(8, 0)
+        expand(8, 1)
         for i in range(4):
             result(scopy, i)
         early_mult(7)
-        u_mult(5, 0)
-        u_mult(5, 1)
         w_quant(10, 12)
         w_group(gcopy, 12, 16, True)
         u_quant(4, 2)
@@ -501,8 +516,10 @@ def tile_convnextdroppathlayerscaleweightgrad_x1_kernel(tc, x, w1, b1, r, dy, ga
                 p_cast(gcopy, 4, 4, True)
             if s == 6:
                 p_cast(gcopy, 8, 2, True)
-            weigh(2 * s, 0)
-            weigh(2 * s, 1)
+            for g in range(G):
+                if s > 3:
+                    turn(2 * s, g)
+                u_mult(2 * s, g)
             early_turn(2 * s + 1)
             planes = {5: (0, 2), 6: (4, 6)}.get(s, ())
             for i in planes:

@@ -21,7 +21,7 @@ G = N // 512
 TILES = F // P
 PAIRS = TILES // 2
 BANKS = 8
-W_LOADS = ((0, 4), (4, 8), (8, 12), (12, 16))
+W_LOADS = ((0, 4), (4, 8), (8, 10), (10, 16))
 EARLY = (7, 9, 11, 13)
 A_BUFS = 14
 SLOTS = 13
@@ -253,14 +253,14 @@ def tile_convnextdroppathlayerscaleweightgrad_x1_kernel(tc, x, w1, b1, r, dy, ga
         u_rows = {}
 
         def early_mult(i):
-            u_rows[i] = work.tile([P, G * 512], BF16, name="u_rows", bufs=2)
+            u_rows[i] = work.tile([P, G * 512], BF16, name="u_rows", bufs=3)
             nc.vector.tensor_tensor(
                 out=u_rows[i][:],
                 in0=a[i][:].rearrange("p g c -> p (g c)"),
                 in1=small["r"][:].rearrange("p n m -> p (n m)").bitcast(BF16),
                 op=MULT,
             )
-            if i == EARLY[-1]:
+            if i == max(EARLY):
                 emptied("r")
 
         def early_turn(i):
@@ -304,7 +304,7 @@ def tile_convnextdroppathlayerscaleweightgrad_x1_kernel(tc, x, w1, b1, r, dy, ga
 
         r_bank = {}
         p_bank = {}
-        rows = {}
+        rows = keep.tile([P, TILES, C], F32, name="rows")
 
         def r_product(i):
             codes, scales = uq[i]
@@ -313,9 +313,7 @@ def tile_convnextdroppathlayerscaleweightgrad_x1_kernel(tc, x, w1, b1, r, dy, ga
                 product(r_bank[i][:], codes[:, g, :], scales[:, g, :], e_codes[:, g, :], e_scales[:, g, :], g == 0, g == G - 1)
 
         def r_exit(copy, i):
-            if i // 4 not in rows:
-                rows[i // 4] = work.tile([P, 4, C], F32, name="rows", bufs=4)
-            dst = rows[i // 4][:, i % 4, :]
+            dst = rows[:, i, :]
             copy(out=dst.rearrange("p (m t) -> p m t", t=4), in_=r_bank[i][:].rearrange("p (t m) -> p m t", t=4))
             emptied(("r", i))
             nc.sync.dma_start(out=out_0[i * P : (i + 1) * P, :], in_=dst)
@@ -335,7 +333,7 @@ def tile_convnextdroppathlayerscaleweightgrad_x1_kernel(tc, x, w1, b1, r, dy, ga
 
         def p_cast(copy, i, n, newest=False):
             cast = new_slot([P, 2, n * P, 2], "cast", ("c", i), newest)
-            src = rows[i // 4][:, i % 4 : i % 4 + n, :]
+            src = rows[:, i : i + n, :]
             copy(out=cast[:], in_=src.rearrange("p n (m v c) -> p v (n m) c", v=2, c=2))
             words = cast[:].rearrange("p v m c -> p (v m c)").bitcast(F32)
             cast_left[i] = n
@@ -412,8 +410,8 @@ def tile_convnextdroppathlayerscaleweightgrad_x1_kernel(tc, x, w1, b1, r, dy, ga
         load_r(nc.sync)
         load_dy(1, 0)
         load_dy(1, 1)
-        load_w(8, 12)
-        load_w(12, 16)
+        load_w(8, 10)
+        load_w(10, 16)
         for h in range(2):
             x_turn(0, h)
             x_exit(scopy, 0, h)
@@ -484,7 +482,7 @@ def tile_convnextdroppathlayerscaleweightgrad_x1_kernel(tc, x, w1, b1, r, dy, ga
         e_quant(1, 0)
         u_quant(0, 2)
         e_quant(1, 1)
-        w_group(gcopy, 10, 12, True)
+        w_group(gcopy, 10, 13, True)
         u_quant(2, 2)
         turn(5, 0)
         turn(5, 1)
@@ -498,8 +496,8 @@ def tile_convnextdroppathlayerscaleweightgrad_x1_kernel(tc, x, w1, b1, r, dy, ga
         for i in range(4):
             result(scopy, i)
         early_mult(7)
-        w_quant(10, 12)
-        w_group(gcopy, 12, 16, True)
+        w_quant(10, 13)
+        w_group(gcopy, 13, 16, True)
         u_quant(4, 2)
         for s in range(3, PAIRS - 1):
             if s > 4:
@@ -524,7 +522,7 @@ def tile_convnextdroppathlayerscaleweightgrad_x1_kernel(tc, x, w1, b1, r, dy, ga
             planes = {5: (0, 2), 6: (4, 6)}.get(s, ())
             for i in planes:
                 p_turn(i, 2)
-            early_exit(vcopy if s in (3, 4, 6) else scopy, 2 * s + 1)
+            early_exit(vcopy if s in (4, 6) else scopy, 2 * s + 1)
             for i in planes:
                 if i < 6:
                     p_exit(vcopy if i in (0,) else scopy, i, 2)
@@ -536,7 +534,7 @@ def tile_convnextdroppathlayerscaleweightgrad_x1_kernel(tc, x, w1, b1, r, dy, ga
             u_quant(2 * s, 2)
             if s == 3:
                 p_cast(gcopy, 0, 4, True)
-                w_quant(12, 16)
+                w_quant(13, 16)
             if s == 5:
                 p_quant(0, 2)
             if s == 6:

@@ -24,7 +24,7 @@ BANKS = 8
 W_LOADS = ((0, 4), (4, 8), (8, 10), (10, 16))
 EARLY = (7, 9, 11, 13)
 A_BUFS = 14
-SLOTS = 13
+SLOTS = 16
 
 
 def tile_convnextdroppathlayerscaleweightgrad_x1_kernel(tc, x, w1, b1, r, dy, gamma, out_0, out_1, out_2):
@@ -54,7 +54,7 @@ def tile_convnextdroppathlayerscaleweightgrad_x1_kernel(tc, x, w1, b1, r, dy, ga
         w_codes = keep.tile([P, F], U32, name="w_codes", align_bytes=64)
         w_scales = keep.tile([P, F], U8, name="w_scales", align_bytes=64)
         dy_raw = {(g, h): keep.tile([P, 2, C], BF16, name=f"dy_raw{g}{h}") for g in range(G) for h in range(2)}
-        e_nat = [keep.tile([P, 2, 4, P, 2], BF16, name=f"e_nat{g}") for g in range(G)]
+        e_nat = [keep.tile([P, 4, 2, P, 2], BF16, name=f"e_nat{g}") for g in range(G)]
         e_codes = keep.tile([P, G, C], U32, name="e_codes", align_bytes=64)
         e_scales = keep.tile([P, G, C], U8, name="e_scales", align_bytes=64)
         p_codes = keep.tile([P, F], U32, name="p_codes", align_bytes=64)
@@ -71,9 +71,9 @@ def tile_convnextdroppathlayerscaleweightgrad_x1_kernel(tc, x, w1, b1, r, dy, ga
         def emptied(key):
             free_banks.append(held[key])
 
-        def new_slot(shape, name, key, newest=False):
+        def new_slot(shape, name, key, newest=False, dtype=BF16):
             held[key] = free_slots.pop(-1 if newest else 0)
-            return work.tile(shape, BF16, name=name, tag=f"slot{held[key]}", align_bytes=64)
+            return work.tile(shape, dtype, name=name, tag=f"slot{held[key]}", align_bytes=64)
 
         def used_up(key):
             free_slots.append(held[key])
@@ -127,17 +127,19 @@ def tile_convnextdroppathlayerscaleweightgrad_x1_kernel(tc, x, w1, b1, r, dy, ga
                     nc.tensor.transpose(x_turned[g, h][:, n, v, :], words[:, 256 * n + v : 256 * (n + 1) : 2], ident[:])
 
         def x_exit(copy, g, h):
-            x_bf[g, h] = new_slot([P, 1024], "x_bf", ("x", g, h))
+            if g not in x_bf:
+                x_bf[g] = new_slot([P, 2048], "x_bf", ("x", g))
             copy(
-                out=x_bf[g, h][:].bitcast(F32).rearrange("p (t m v) -> p t m v", t=2, v=2),
+                out=x_bf[g][:, 1024 * h : 1024 * h + 1024].bitcast(F32).rearrange("p (t m v) -> p t m v", t=2, v=2),
                 in_=x_turned[g, h][:].rearrange("p t v m -> p t m v"),
             )
             emptied(("xb", g, h))
 
-        def x_quant(g, h):
-            c = slice(256 * h, 256 * h + 256)
-            quantize(x_codes[:, g, c], x_scales[:, g, c], x_bf[g, h][:])
-            used_up(("x", g, h))
+        def x_quant(g, h0, h1):
+            c = slice(256 * h0, 256 * h1)
+            quantize(x_codes[:, g, c], x_scales[:, g, c], x_bf[g][:, 1024 * h0 : 1024 * h1])
+            if h1 == 2:
+                used_up(("x", g))
 
         small = {}
 
@@ -180,7 +182,7 @@ def tile_convnextdroppathlayerscaleweightgrad_x1_kernel(tc, x, w1, b1, r, dy, ga
         def e_mult(g, h):
             gam = small["g"][:].rearrange("p v k -> p (v k)").bitcast(BF16)
             nc.vector.tensor_tensor(
-                out=e_nat[g][:, :, 2 * h : 2 * h + 2],
+                out=e_nat[g][:, 2 * h : 2 * h + 2].rearrange("p j v m c -> p v j m c"),
                 in0=dy_raw[g, h][:].rearrange("p j (m v c) -> p v j m c", v=2, c=2),
                 in1=gam.rearrange("p (v m c) -> p v m c", v=2, c=2).unsqueeze(2).to_broadcast([P, 2, 2, P, 2]),
                 op=MULT,
@@ -190,19 +192,23 @@ def tile_convnextdroppathlayerscaleweightgrad_x1_kernel(tc, x, w1, b1, r, dy, ga
 
         e_bf = {}
 
-        def e_group(copy, g, v, newest=False):
-            dst = e_bf[g, v] = new_slot([P, 2 * P, 4], "e_bf", ("e", g, v), newest)
+        def e_group(copy, g, v=None, newest=False):
+            if v is None:
+                dst = e_bf[g, v] = new_slot([P, 2, 2, P, 4], "e_bf", ("e", g, v), newest)
+                gcopy(out=dst[:].rearrange("p v c m j -> p c v m j"), in_=e_nat[g][:].rearrange("p j v m c -> p c v m j"))
+                return
+            dst = e_bf[g, v] = new_slot([P, 1, 2, P, 4], "e_bf", ("e", g, v), newest)
             if copy is gcopy:
-                gcopy(out=dst[:].rearrange("p (c m) j -> p c m j", c=2), in_=e_nat[g][:, v].rearrange("p j m c -> p c m j"))
+                gcopy(out=dst[:, 0], in_=e_nat[g][:, :, v].rearrange("p j m c -> p c m j"))
             else:
                 copy(
-                    out=dst[:].rearrange("p (c n m) j -> p n j m c", c=2, m=2),
-                    in_=e_nat[g][:, v].rearrange("p j (n m) c -> p n j m c", m=2),
+                    out=dst[:, 0].rearrange("p c (n m) j -> p n j m c", m=2),
+                    in_=e_nat[g][:, :, v].rearrange("p j (n m) c -> p n j m c", m=2),
                 )
 
-        def e_quant(g, v):
-            c = slice(256 * v, 256 * v + 256)
-            quantize(e_codes[:, g, c], e_scales[:, g, c], e_bf[g, v][:].rearrange("p c j -> p (c j)"))
+        def e_quant(g, v=None):
+            c = slice(0, C) if v is None else slice(256 * v, 256 * v + 256)
+            quantize(e_codes[:, g, c], e_scales[:, g, c], e_bf[g, v][:].rearrange("p v c m j -> p (v c m j)"))
             used_up(("e", g, v))
 
         a = {}
@@ -218,7 +224,7 @@ def tile_convnextdroppathlayerscaleweightgrad_x1_kernel(tc, x, w1, b1, r, dy, ga
             src = h_bank[i, g, h][:]
             if i in EARLY:
                 if g == 0:
-                    a[i] = work.tile([P, G, 512], F32, name="a_wide", bufs=3)
+                    a[i] = new_slot([P, G, 512], "a_wide", ("a", i), dtype=F32)
                 dst = a[i][:, g, :].rearrange("p (v m e) -> p v m e", v=2, e=2)
                 src = src.rearrange("p (v e m) -> p v m e", v=2, e=2)
             else:
@@ -260,6 +266,7 @@ def tile_convnextdroppathlayerscaleweightgrad_x1_kernel(tc, x, w1, b1, r, dy, ga
                 in1=small["r"][:].rearrange("p n m -> p (n m)").bitcast(BF16),
                 op=MULT,
             )
+            used_up(("a", i))
             if i == max(EARLY):
                 emptied("r")
 
@@ -350,9 +357,11 @@ def tile_convnextdroppathlayerscaleweightgrad_x1_kernel(tc, x, w1, b1, r, dy, ga
                 if cast_left[first] == 0:
                     used_up(("c", first))
 
-        def p_exit(copy, i, n):
-            p_bf[i] = new_slot([P, n * P, 4], "p_bf", ("q", i))
-            dst = p_bf[i][:].rearrange("p f c -> p (f c)").bitcast(F32)
+        def p_exit(copy, i, n, first=None, width=None):
+            first = i if first is None else first
+            if first not in p_bf:
+                p_bf[first] = new_slot([P, (width or n) * P, 4], "p_bf", ("q", first))
+            dst = p_bf[first][:, (i - first) * P : (i - first + n) * P].rearrange("p f c -> p (f c)").bitcast(F32)
             copy(out=dst.rearrange("p (n f v) -> p n f v", n=n, v=2), in_=p_bank[i][:].rearrange("p n v f -> p n f v"))
             emptied(("p", i))
 
@@ -417,10 +426,10 @@ def tile_convnextdroppathlayerscaleweightgrad_x1_kernel(tc, x, w1, b1, r, dy, ga
             x_exit(scopy, 0, h)
         bias_turn()
         gamma_turn()
-        x_quant(0, 0)
+        x_quant(0, 0, 1)
         w_group(vcopy, 0, 2)
         w_group(scopy, 2, 4)
-        x_quant(0, 1)
+        x_quant(0, 1, 2)
         w_quant(0, 2)
         w_quant(2, 4)
         bias_exit(vcopy)
@@ -429,9 +438,9 @@ def tile_convnextdroppathlayerscaleweightgrad_x1_kernel(tc, x, w1, b1, r, dy, ga
             x_exit(scopy, 1, h)
         for i in range(4):
             expand(i, 0)
-        x_quant(1, 0)
+        x_quant(1, 0, 1)
         w_group(vcopy, 4, 6)
-        x_quant(1, 1)
+        x_quant(1, 1, 2)
         w_group(gcopy, 6, 8, True)
         w_quant(4, 6)
         for i in range(4):
@@ -500,9 +509,6 @@ def tile_convnextdroppathlayerscaleweightgrad_x1_kernel(tc, x, w1, b1, r, dy, ga
         w_group(gcopy, 13, 16, True)
         u_quant(4, 2)
         for s in range(3, PAIRS - 1):
-            if s > 4:
-                result(scopy, 2 * s - 4)
-                result(scopy, 2 * s - 3)
             if s > 3:
                 for i in ((2 * s + 3, 2 * s + 2) if 2 * s + 3 in EARLY else (2 * s + 2, 2 * s + 3)):
                     expand(i, 0)
@@ -510,10 +516,6 @@ def tile_convnextdroppathlayerscaleweightgrad_x1_kernel(tc, x, w1, b1, r, dy, ga
             if s == 4:
                 result(scopy, 4)
                 result(scopy, 5)
-            if s == 5:
-                p_cast(gcopy, 4, 4, True)
-            if s == 6:
-                p_cast(gcopy, 8, 2, True)
             for g in range(G):
                 if s > 3:
                     turn(2 * s, g)
@@ -528,15 +530,23 @@ def tile_convnextdroppathlayerscaleweightgrad_x1_kernel(tc, x, w1, b1, r, dy, ga
                     p_exit(vcopy if i in (0,) else scopy, i, 2)
             if s < PAIRS - 2:
                 early_mult(2 * s + 3)
+            if s == 4:
+                result(scopy, 6)
+                result(scopy, 7)
+                p_cast(gcopy, 4, 4, True)
             if s == 6:
                 p_quant(2, 2)
-                store_words(0, 4)
+                store_words(2, 4)
             u_quant(2 * s, 2)
             if s == 3:
                 p_cast(gcopy, 0, 4, True)
                 w_quant(13, 16)
             if s == 5:
+                result(scopy, 8)
+                result(scopy, 9)
+                p_cast(gcopy, 8, 2, True)
                 p_quant(0, 2)
+                store_words(0, 2)
             if s == 6:
                 p_quant(4, 2)
         result(scopy, 10)
@@ -548,35 +558,35 @@ def tile_convnextdroppathlayerscaleweightgrad_x1_kernel(tc, x, w1, b1, r, dy, ga
         p_cast(gcopy, 10, 2, True)
         weigh(14, 1)
         weigh(15, 0)
-        turn(15, 1)
-        p_turn(8, 2)
-        p_exit(scopy, 8, 2)
         result(scopy, 12)
         result(scopy, 13)
-        u_mult(15, 1)
         u_quant(14, 1)
         u_quant(15, 1, 0)
-        p_quant(6, 2)
-        u_quant(15, 1, 1)
+        weigh(15, 1)
+        p_turn(8, 2)
         p_turn(10, 2)
-        p_cast(vcopy, 12, 2)
+        p_exit(scopy, 8, 2)
+        p_quant(6, 2)
+        store_words(6, 8)
+        u_quant(15, 1, 1)
         p_exit(scopy, 10, 2)
         result(scopy, 14)
+        p_cast(vcopy, 12, 2)
+        p_quant(8, 2)
         p_product(15, 0)
         p_product(15, 1)
         r_product(15)
-        p_quant(8, 2)
         p_cast(vcopy, 14, 1)
         d_exit(scopy, 15)
         p_quant(10, 2)
-        store_words(6, 12)
+        store_words(8, 12)
         p_turn(12, 2)
         p_turn(14, 1)
-        r_exit(vcopy, 15)
-        p_exit(scopy, 12, 2)
-        p_exit(scopy, 14, 1)
+        r_exit(scopy, 15)
         p_quant(15, 1)
-        p_quant(12, 2)
+        p_exit(vcopy, 12, 2)
+        p_exit(scopy, 14, 1)
         p_quant(14, 1)
+        p_quant(12, 2)
         store_words(12, 16)
         store_scales(6, 16)

@@ -497,13 +497,13 @@ def tile_convnextdroppathlayerscaleweightgrad_x1_kernel(tc, x, w1, b1, r, dy, ga
         turn(5, 1)
         r_turn()
         turn(6, 0)
-        turn(6, 1)
         u_mult(5, 0)
         u_mult(5, 1)
         expand(8, 0)
         expand(8, 1)
         for i in range(4):
             result(scopy, i)
+        turn(6, 1)
         early_mult(7)
         w_quant(10, 13)
         w_group(gcopy, 13, 16, True)
@@ -580,13 +580,15 @@ def tile_convnextdroppathlayerscaleweightgrad_x1_kernel(tc, x, w1, b1, r, dy, ga
         d_exit(scopy, 15)
         p_quant(10, 2)
         store_words(8, 12)
-        p_turn(12, 2)
+        p_turn(12, 1)
+        p_turn(13, 1)
         p_turn(14, 1)
         r_exit(scopy, 15)
         p_quant(15, 1)
-        p_exit(vcopy, 12, 2)
-        p_exit(scopy, 14, 1)
-        p_quant(14, 1)
+        p_exit(vcopy, 12, 1, 12, 2)
+        p_exit(scopy, 13, 1, 12, 2)
+        p_exit(vcopy, 14, 1)
         p_quant(12, 2)
+        p_quant(14, 1)
         store_words(12, 16)
         store_scales(6, 16)

@@ -58,7 +58,7 @@ def tile_convnextdroppathlayerscaleweightgrad_x1_kernel(tc, x, w1, b1, r, dy, ga
         e_codes = keep.tile([P, G, C], U32, name="e_codes", align_bytes=64)
         e_scales = keep.tile([P, G, C], U8, name="e_scales", align_bytes=64)
         p_codes = keep.tile([P, F], U32, name="p_codes", align_bytes=64)
-        p_scales = keep.tile([P, F], U8, name="p_scales", align_bytes=64)
+        p_scales = keep.tile([P, F // 4], U8, name="p_scales", align_bytes=64)
 
         free_banks = list(range(BANKS))
         free_slots = list(range(SLOTS))
@@ -372,7 +372,8 @@ def tile_convnextdroppathlayerscaleweightgrad_x1_kernel(tc, x, w1, b1, r, dy, ga
 
         def p_quant(i, n):
             c = slice(i * P, (i + n) * P)
-            quantize(p_codes[:, c], p_scales[:, c], p_bf[i][:].rearrange("p f c -> p (f c)"))
+            rows_from, at = 4 * (i // 4), (i % 4) * P
+            quantize(p_codes[:, c], p_scales[rows_from:, at : at + n * P], p_bf[i][:].rearrange("p f c -> p (f c)"))
             used_up(("q", i))
 
         def store_words(i0, i1):
@@ -381,12 +382,13 @@ def tile_convnextdroppathlayerscaleweightgrad_x1_kernel(tc, x, w1, b1, r, dy, ga
                 in_=p_codes[:, i0 * P : i1 * P].bitcast(I32),
             )
 
-        def store_scales(i0, i1):
+        def store_scales():
             for quadrant in range(4):
-                queue = nc.scalar if i1 == TILES and quadrant % 2 else nc.sync
+                queue = nc.scalar if quadrant % 2 else nc.sync
+                dst = out_2[0, 4 * quadrant : 4 * quadrant + 4, :].bitcast(I32)
                 queue.dma_start(
-                    out=out_2[0, 4 * quadrant : 4 * quadrant + 4, i0 * P : i1 * P].bitcast(I32),
-                    in_=p_scales[32 * quadrant : 32 * quadrant + 4, i0 * P : i1 * P].bitcast(I32),
+                    out=dst.rearrange("r (j c) -> j r c", j=4),
+                    in_=p_scales[32 * quadrant : 32 * quadrant + 16, :].bitcast(I32),
                 )
 
         def expand(i, g, h=None):
@@ -552,7 +554,6 @@ def tile_convnextdroppathlayerscaleweightgrad_x1_kernel(tc, x, w1, b1, r, dy, ga
         result(scopy, 10)
         result(scopy, 11)
         store_words(4, 6)
-        store_scales(0, 6)
         p_exit(scopy, 6, 2)
         weigh(14, 0)
         p_cast(gcopy, 10, 2, True)
@@ -584,11 +585,11 @@ def tile_convnextdroppathlayerscaleweightgrad_x1_kernel(tc, x, w1, b1, r, dy, ga
         p_turn(13, 1)
         p_turn(14, 1)
         r_exit(scopy, 15)
-        p_quant(15, 1)
         p_exit(vcopy, 12, 1, 12, 2)
+        p_quant(15, 1)
         p_exit(scopy, 13, 1, 12, 2)
         p_exit(vcopy, 14, 1)
         p_quant(12, 2)
         p_quant(14, 1)
         store_words(12, 16)
-        store_scales(6, 16)
+        store_scales()

from contextlib import ExitStack

import concourse.mybir as mybir
from concourse.masks import make_identity

N, C, F = 1024, 512, 2048
FLOPS = 4 * N * C * F

F32 = mybir.dt.float32
BF16 = mybir.dt.bfloat16
I32 = mybir.dt.int32
U32 = mybir.dt.uint32
U8 = mybir.dt.uint8
FP8X4 = mybir.dt.float8_e4m3fn_x4
GELU = mybir.ActivationFunctionType.Gelu_apprx_tanh
MULT = mybir.AluOpType.mult
ADD = mybir.AluOpType.add

P = 128
G = N // 512
TILES = F // P
PAIRS = TILES // 2
BANKS = 8
W_LOADS = ((0, 4), (4, 8), (8, 10), (10, 16))
EARLY = (7, 9, 11, 13)
A_BUFS = 14
SLOTS = 16


def tile_convnextdroppathlayerscaleweightgrad_x1_kernel(tc, x, w1, b1, r, dy, gamma, out_0, out_1, out_2):
    nc = tc.nc
    vcopy, scopy = nc.vector.tensor_copy, nc.scalar.copy
    with ExitStack() as ctx:
        keep = ctx.enter_context(tc.tile_pool(name="keep", bufs=1))
        work = ctx.enter_context(tc.tile_pool(name="work", bufs=1))
        psum = ctx.enter_context(tc.psum_pool(name="psum", bufs=1))
        ctx.enter_context(tc.manual_schedule())

        ident = keep.tile([P, P], F32, name="ident")
        ident_bf = keep.tile([P, P], BF16, name="ident_bf")
        b_rows = keep.tile([P, P], BF16, name="b_rows")
        bias = keep.tile([P, TILES], F32, name="bias")
        gcols = keep.tile([P, 4], BF16, name="gcols")
        r_sb = keep.tile([P, G, 4], BF16, name="r_sb")
        warm = keep.tile([P, 1], F32, name="warm")
        x_raw = {(g, h): keep.tile([P, 2 * C], BF16, name=f"x_raw{g}{h}") for g in range(G) for h in range(2)}
        x_codes = keep.tile([P, G, 512], U32, name="x_codes", align_bytes=64)
        x_scales = keep.tile([P, G, 512], U8, name="x_scales", align_bytes=64)
        w_raw = {}
        for i0, i1 in W_LOADS:
            raw = keep.tile([P, 4, (i1 - i0) * P], BF16, name=f"w_raw{i0}")
            for i in range(i0, i1):
                w_raw[i] = raw, i - i0
        w_codes = keep.tile([P, F], U32, name="w_codes", align_bytes=64)
        w_scales = keep.tile([P, F], U8, name="w_scales", align_bytes=64)
        dy_raw = {(g, h): keep.tile([P, 2, C], BF16, name=f"dy_raw{g}{h}") for g in range(G) for h in range(2)}
        e_nat = [keep.tile([P, 4, 2, P, 2], BF16, name=f"e_nat{g}") for g in range(G)]
        e_codes = keep.tile([P, G, C], U32, name="e_codes", align_bytes=64)
        e_scales = keep.tile([P, G, C], U8, name="e_scales", align_bytes=64)
        p_codes = keep.tile([P, F], U32, name="p_codes", align_bytes=64)
        p_scales = keep.tile([P, F // 4], U8, name="p_scales", align_bytes=64)

        free_banks = list(range(BANKS))
        free_slots = list(range(SLOTS))
        held = {}

        def new_bank(shape, dtype, name, key):
            held[key] = free_banks.pop(0)
            return psum.tile(shape, dtype, name=name, tag=f"bank{held[key]}")

        def emptied(key):
            free_banks.append(held[key])

        def new_slot(shape, name, key, newest=False, dtype=BF16):
            held[key] = free_slots.pop(-1 if newest else 0)
            return work.tile(shape, dtype, name=name, tag=f"slot{held[key]}", align_bytes=64)

        def used_up(key):
            free_slots.append(held[key])

        def gcopy(out, in_):
            nc.gpsimd.tensor_scalar(out=out, in0=in_, scalar1=1.0, scalar2=0.0, op0=MULT, op1=ADD)

        def quantize(codes, scales, values):
            nc.vector.quantize_mx(out=codes.bitcast(FP8X4), scales=scales, in_=values)

        def product(out, stat, stat_scales, mov, mov_scales, start=True, stop=True):
            nc.tensor.matmul_mx(
                out=out,
                lhsT=stat.bitcast(FP8X4),
                lhsT_scale=stat_scales,
                rhs=mov.bitcast(FP8X4),
                rhs_scale=mov_scales,
                start=start,
                stop=stop,
            )

        def load_x(g, h):
            src = x[512 * g : 512 * g + 512, :].rearrange("(m h t) k -> m h (t k)", h=2, t=2)
            nc.sync.dma_start(out=x_raw[g, h][:], in_=src[:, h, :])

        def load_w(i0, i1):
            c = slice(i0 * P, i1 * P)
            nc.sync.dma_start(out=w_raw[i0][0][:], in_=w1[:, c].rearrange("(p j) f -> p j f", j=4))

        def load_dy(g, h):
            src = dy[512 * g : 512 * g + 512, :].rearrange("(p j) c -> p j c", j=4)
            nc.sync.dma_start(out=dy_raw[g, h][:], in_=src[:, 2 * h : 2 * h + 2, :])

        def load_gamma(queue):
            queue.dma_start(out=gcols[:], in_=gamma.rearrange("(k q) -> k q", q=4))

        def load_bias(queue):
            queue.dma_start(out=b_rows[0:TILES, :], in_=b1.rearrange("(i f) -> i f", f=P))

        def load_r(queue):
            queue.dma_start(out=r_sb[:], in_=r.rearrange("(g p t) -> p g t", g=G, t=4))

        x_turned = {}
        x_bf = {}

        def x_turn(g, h):
            words = x_raw[g, h][:].bitcast(F32)
            x_turned[g, h] = new_bank([P, 2, 2, P], F32, "x_bank", ("xb", g, h))
            for n in range(2):
                for v in range(2):
                    nc.tensor.transpose(x_turned[g, h][:, n, v, :], words[:, 256 * n + v : 256 * (n + 1) : 2], ident[:])

        def x_exit(copy, g, h):
            if g not in x_bf:
                x_bf[g] = new_slot([P, 2048], "x_bf", ("x", g))
            copy(
                out=x_bf[g][:, 1024 * h : 1024 * h + 1024].bitcast(F32).rearrange("p (t m v) -> p t m v", t=2, v=2),
                in_=x_turned[g, h][:].rearrange("p t v m -> p t m v"),
            )
            emptied(("xb", g, h))

        def x_quant(g, h0, h1):
            c = slice(256 * h0, 256 * h1)
            quantize(x_codes[:, g, c], x_scales[:, g, c], x_bf[g][:, 1024 * h0 : 1024 * h1])
            if h1 == 2:
                used_up(("x", g))

        small = {}

        def bias_turn():
            small["b"] = new_bank([P, P], BF16, "b_bank", "b")
            nc.tensor.transpose(small["b"][:], b_rows[:], ident_bf[:])

        def bias_exit(copy):
            copy(out=bias[:], in_=small["b"][:, 0:TILES])
            emptied("b")

        def gamma_turn():
            bank = small["g"] = new_bank([P, 2, P], F32, "g_bank", "g")
            words = gcols[:].bitcast(F32)
            for v in range(2):
                nc.tensor.transpose(bank[:, v, :], words[:, v : v + 1].to_broadcast([P, P]), ident[:])

        def r_turn():
            bank = small["r"] = new_bank([P, 2 * G, P], F32, "r_spread", "r")
            words = r_sb[:].rearrange("p g t -> p (g t)").bitcast(F32)
            for n in range(2 * G):
                nc.tensor.transpose(bank[:, n, :], words[:, n : n + 1].to_broadcast([P, P]), ident[:])

        w_bf = {}

        def w_group(copy, i0, i1, newest=False):
            raw, at = w_raw[i0]
            dst = w_bf[i0] = new_slot([P, (i1 - i0) * P, 4], "w_bf", ("w", i0), newest)
            src = raw[:, :, at * P : (at + i1 - i0) * P]
            if copy is gcopy:
                gcopy(out=dst[:], in_=src.rearrange("p j c -> p c j"))
            else:
                copy(out=dst[:].rearrange("p (c q) j -> p c j q", q=4), in_=src.rearrange("p j (c q) -> p c j q", q=4))

        def w_quant(i0, i1):
            c = slice(i0 * P, i1 * P)
            quantize(w_codes[:, c], w_scales[:, c], w_bf[i0][:].rearrange("p c j -> p (c j)"))
            used_up(("w", i0))

        def e_mult(g, h):
            gam = small["g"][:].rearrange("p v k -> p (v k)").bitcast(BF16)
            nc.vector.tensor_tensor(
                out=e_nat[g][:, 2 * h : 2 * h + 2].rearrange("p j v m c -> p v j m c"),
                in0=dy_raw[g, h][:].rearrange("p j (m v c) -> p v j m c", v=2, c=2),
                in1=gam.rearrange("p (v m c) -> p v m c", v=2, c=2).unsqueeze(2).to_broadcast([P, 2, 2, P, 2]),
                op=MULT,
            )
            if (g, h) == (G - 1, 1):
                emptied("g")

        e_bf = {}

        def e_group(copy, g, v=None, newest=False):
            if v is None:
                dst = e_bf[g, v] = new_slot([P, 2, 2, P, 4], "e_bf", ("e", g, v), newest)
                gcopy(out=dst[:].rearrange("p v c m j -> p c v m j"), in_=e_nat[g][:].rearrange("p j v m c -> p c v m j"))
                return
            dst = e_bf[g, v] = new_slot([P, 1, 2, P, 4], "e_bf", ("e", g, v), newest)
            if copy is gcopy:
                gcopy(out=dst[:, 0], in_=e_nat[g][:, :, v].rearrange("p j m c -> p c m j"))
            else:
                copy(
                    out=dst[:, 0].rearrange("p c (n m) j -> p n j m c", m=2),
                    in_=e_nat[g][:, :, v].rearrange("p j (n m) c -> p n j m c", m=2),
                )

        def e_quant(g, v=None):
            c = slice(0, C) if v is None else slice(256 * v, 256 * v + 256)
            quantize(e_codes[:, g, c], e_scales[:, g, c], e_bf[g, v][:].rearrange("p v c m j -> p (v c m j)"))
            used_up(("e", g, v))

        a = {}
        h_bank = {}

        def h_product(i, g, h=None):
            c = slice(i * P, (i + 1) * P)
            t = slice(0, 512) if h is None else slice(256 * h, 256 * h + 256)
            bank = h_bank[i, g, h] = new_bank([P, t.stop - t.start], F32, "h_bank", ("h", i, g, h))
            product(bank[:], w_codes[:, c], w_scales[:, c], x_codes[:, g, t], x_scales[:, g, t])

        def gelu(i, g, h=None):
            src = h_bank[i, g, h][:]
            if i in EARLY:
                if g == 0:
                    a[i] = new_slot([P, G, 512], "a_wide", ("a", i), dtype=F32)
                dst = a[i][:, g, :].rearrange("p (v m e) -> p v m e", v=2, e=2)
                src = src.rearrange("p (v e m) -> p v m e", v=2, e=2)
            else:
                if not h:
                    a[i, g] = work.tile([P, 512], F32, name="a_sb", bufs=A_BUFS)
                dst = a[i, g][:] if h is None else a[i, g][:, 256 * h : 256 * h + 256]
            nc.scalar.activation(out=dst, in_=src, func=GELU, bias=bias[:, i : i + 1])
            emptied(("h", i, g, h))

        turned = {}
        u = {}

        def u_tile(i):
            if i // 2 not in u:
                u[i // 2] = new_slot([P, 2, G, P, 4], "u_bf", ("u", i // 2))
            return u[i // 2]

        def turn(i, g):
            turned[i, g] = new_bank([P, 4, P], F32, "t_bank", ("t", i, g))
            for t in range(4):
                nc.tensor.transpose(turned[i, g][:, t, :], a[i, g][:, t * P : (t + 1) * P], ident[:])

        def u_mult(i, g):
            nc.vector.tensor_tensor(
                out=u_tile(i)[:, i % 2, g, :, :],
                in0=turned[i, g][:].rearrange("p t f -> p f t"),
                in1=r_sb[:, g, :].unsqueeze(1).to_broadcast([P, P, 4]),
                op=MULT,
            )
            emptied(("t", i, g))

        u_rows = {}

        def early_mult(i):
            u_rows[i] = work.tile([P, G * 512], BF16, name="u_rows", bufs=3)
            nc.vector.tensor_tensor(
                out=u_rows[i][:],
                in0=a[i][:].rearrange("p g c -> p (g c)"),
                in1=small["r"][:].rearrange("p n m -> p (n m)").bitcast(BF16),
                op=MULT,
            )
            used_up(("a", i))
            if i == max(EARLY):
                emptied("r")

        def early_turn(i):
            turned[i] = new_bank([P, G, 2, P], F32, "w_bank", ("t", i))
            words = u_rows[i][:].bitcast(F32)
            for g in range(G):
                for v in range(2):
                    n = 2 * g + v
                    nc.tensor.transpose(turned[i][:, g, v, :], words[:, n * P : (n + 1) * P], ident[:])

        def early_exit(copy, i):
            dst = u_tile(i)[:, i % 2].rearrange("p g f t -> p (g f t)").bitcast(F32)
            copy(out=dst.rearrange("p (g f v) -> p g f v", g=G, v=2), in_=turned[i][:].rearrange("p g v f -> p g f v"))
            emptied(("t", i))

        uq = {}
        u_left = {j: 2 * G for j in range(PAIRS)}

        def u_quant(i, n, g=None):
            if g is None:
                codes = work.tile([P, n, G, P], U32, name="u_codes", bufs=4, align_bytes=64)
                scales = work.tile([P, n, G, P], U8, name="u_scales", bufs=4, align_bytes=64)
                quantize(
                    codes[:].rearrange("p n g f -> p (n g f)"),
                    scales[:].rearrange("p n g f -> p (n g f)"),
                    u[i // 2][:, i % 2 : i % 2 + n].rearrange("p n g f t -> p (n g f t)"),
                )
                for m in range(n):
                    uq[i + m] = codes[:, m], scales[:, m]
                u_left[i // 2] -= n * G
            else:
                if i not in uq:
                    codes = work.tile([P, G, P], U32, name="l_codes", bufs=2, align_bytes=64)
                    scales = work.tile([P, G, P], U8, name="l_scales", bufs=2, align_bytes=64)
                    uq[i] = codes, scales
                codes, scales = uq[i]
                quantize(codes[:, g, :], scales[:, g, :], u[i // 2][:, i % 2, g].rearrange("p f t -> p (f t)"))
                u_left[i // 2] -= 1
            if u_left[i // 2] == 0:
                used_up(("u", i // 2))

        r_bank = {}
        p_bank = {}
        rows = keep.tile([P, TILES, C], F32, name="rows")

        def r_product(i):
            codes, scales = uq[i]
            r_bank[i] = new_bank([P, C], F32, "r_bank", ("r", i))
            for g in range(G):
                product(r_bank[i][:], codes[:, g, :], scales[:, g, :], e_codes[:, g, :], e_scales[:, g, :], g == 0, g == G - 1)

        def r_exit(copy, i):
            dst = rows[:, i, :]
            copy(out=dst.rearrange("p (m t) -> p m t", t=4), in_=r_bank[i][:].rearrange("p (t m) -> p m t", t=4))
            emptied(("r", i))
            nc.sync.dma_start(out=out_0[i * P : (i + 1) * P, :], in_=dst)

        def p_product(i, g):
            codes, scales = uq[i]
            if g == 0:
                p_bank[i] = new_bank([P, 4, P], F32, "d_bank", ("p", i))
            for t in range(4):
                c = slice(t * P, (t + 1) * P)
                first, last = g == 0 and t == 0, g == G - 1 and t == 3
                product(p_bank[i][:, t, :], e_codes[:, g, c], e_scales[:, g, c], codes[:, g, :], scales[:, g, :], first, last)

        r_bf = {}
        cast_left = {}
        p_bf = {}

        def p_cast(copy, i, n, newest=False):
            cast = new_slot([P, 2, n * P, 2], "cast", ("c", i), newest)
            src = rows[:, i : i + n, :]
            copy(out=cast[:], in_=src.rearrange("p n (m v c) -> p v (n m) c", v=2, c=2))
            words = cast[:].rearrange("p v m c -> p (v m c)").bitcast(F32)
            cast_left[i] = n
            for m in range(n):
                r_bf[i + m] = i, [words[:, (n * v + m) * P : (n * v + m + 1) * P] for v in range(2)]

        def p_turn(i, n):
            p_bank[i] = new_bank([P, n, 2, P], F32, "p_bank", ("p", i))
            for m in range(n):
                first, words = r_bf[i + m]
                for v in range(2):
                    nc.tensor.transpose(p_bank[i][:, m, v, :], words[v], ident[:])
                cast_left[first] -= 1
                if cast_left[first] == 0:
                    used_up(("c", first))

        def p_exit(copy, i, n, first=None, width=None):
            first = i if first is None else first
            if first not in p_bf:
                p_bf[first] = new_slot([P, (width or n) * P, 4], "p_bf", ("q", first))
            dst = p_bf[first][:, (i - first) * P : (i - first + n) * P].rearrange("p f c -> p (f c)").bitcast(F32)
            copy(out=dst.rearrange("p (n f v) -> p n f v", n=n, v=2), in_=p_bank[i][:].rearrange("p n v f -> p n f v"))
            emptied(("p", i))

        def d_exit(copy, i):
            p_bf[i] = new_slot([P, P, 4], "p_bf", ("q", i))
            copy(out=p_bf[i][:], in_=p_bank[i][:].rearrange("p t f -> p f t"))
            emptied(("p", i))

        def p_quant(i, n):
            c = slice(i * P, (i + n) * P)
            rows_from, at = 4 * (i // 4), (i % 4) * P
            quantize(p_codes[:, c], p_scales[rows_from:, at : at + n * P], p_bf[i][:].rearrange("p f c -> p (f c)"))
            used_up(("q", i))

        def store_words(i0, i1):
            nc.sync.dma_start(
                out=out_1[0, :, i0 * P : i1 * P, :].rearrange("p m t -> p (m t)").bitcast(I32),
                in_=p_codes[:, i0 * P : i1 * P].bitcast(I32),
            )

        def store_scales():
            for quadrant in range(4):
                queue = nc.scalar if quadrant % 2 else nc.sync
                dst = out_2[0, 4 * quadrant : 4 * quadrant + 4, :].bitcast(I32)
                queue.dma_start(
                    out=dst.rearrange("r (j c) -> j r c", j=4),
                    in_=p_scales[32 * quadrant : 32 * quadrant + 16, :].bitcast(I32),
                )

        def expand(i, g, h=None):
            h_product(i, g, h)
            gelu(i, g, h)

        def weigh(i, g):
            turn(i, g)
            u_mult(i, g)

        def result(copy, i):
            r_product(i)
            r_exit(copy, i)

        nc.vector.memset(warm[:], 0.0)
        nc.vector.memset(b_rows[:], 0.0)
        make_identity(nc, ident[:])
        make_identity(nc, ident_bf[:])
        nc.scalar.activation(out=warm[:], in_=warm[:], func=GELU)
        load_x(0, 0)
        load_x(0, 1)
        load_w(0, 4)
        load_bias(nc.sync)
        load_gamma(nc.sync)
        load_x(1, 0)
        load_x(1, 1)
        load_w(4, 8)
        load_dy(0, 0)
        load_dy(0, 1)
        load_r(nc.sync)
        load_dy(1, 0)
        load_dy(1, 1)
        load_w(8, 10)
        load_w(10, 16)
        for h in range(2):
            x_turn(0, h)
            x_exit(scopy, 0, h)
        bias_turn()
        gamma_turn()
        x_quant(0, 0, 1)
        w_group(vcopy, 0, 2)
        w_group(scopy, 2, 4)
        x_quant(0, 1, 2)
        w_quant(0, 2)
        w_quant(2, 4)
        bias_exit(vcopy)
        for h in range(2):
            x_turn(1, h)
            x_exit(scopy, 1, h)
        for i in range(4):
            expand(i, 0)
        x_quant(1, 0, 1)
        w_group(vcopy, 4, 6)
        x_quant(1, 1, 2)
        w_group(gcopy, 6, 8, True)
        w_quant(4, 6)
        for i in range(4):
            expand(i, 1)
        e_mult(0, 0)
        e_mult(0, 1)
        e_group(gcopy, 0, 0)
        for i in range(4):
            turn(i, 0)
        e_mult(1, 0)
        e_mult(1, 1)
        u_mult(0, 0)
        u_mult(1, 0)
        w_group(gcopy, 8, 10)
        u_mult(2, 0)
        for i in (4, 5):
            expand(i, 0)
            expand(i, 1)
        u_mult(3, 0)
        w_quant(6, 8)
        e_quant(0, 0)
        e_group(gcopy, 0, 1, True)
        w_quant(8, 10)
        e_group(gcopy, 1, 0)
        e_group(scopy, 1, 1)
        for i in range(4):
            turn(i, 1)
        u_mult(0, 1)
        u_mult(1, 1)
        turn(4, 0)
        turn(4, 1)
        u_mult(2, 1)
        for i in (7, 6):
            h_product(i, 0)
            h_product(i, 1)
        u_mult(3, 1)
        u_mult(4, 0)
        gelu(7, 0)
        h_product(9, 0)
        h_product(9, 1)
        u_mult(4, 1)
        gelu(7, 1)
        gelu(6, 0)
        gelu(6, 1)
        gelu(9, 0)
        gelu(9, 1)
        e_quant(0, 1)
        e_quant(1, 0)
        u_quant(0, 2)
        e_quant(1, 1)
        w_group(gcopy, 10, 13, True)
        u_quant(2, 2)
        turn(5, 0)
        turn(5, 1)
        r_turn()
        turn(6, 0)
        u_mult(5, 0)
        u_mult(5, 1)
        expand(8, 0)
        expand(8, 1)
        for i in range(4):
            result(scopy, i)
        turn(6, 1)
        early_mult(7)
        w_quant(10, 13)
        w_group(gcopy, 13, 16, True)
        u_quant(4, 2)
        for s in range(3, PAIRS - 1):
            if s > 3:
                for i in ((2 * s + 3, 2 * s + 2) if 2 * s + 3 in EARLY else (2 * s + 2, 2 * s + 3)):
                    expand(i, 0)
                    expand(i, 1)
            if s == 4:
                result(scopy, 4)
                result(scopy, 5)
            for g in range(G):
                if s > 3:
                    turn(2 * s, g)
                u_mult(2 * s, g)
            early_turn(2 * s + 1)
            planes = {5: (0, 2), 6: (4, 6)}.get(s, ())
            for i in planes:
                p_turn(i, 2)
            early_exit(vcopy if s in (4, 6) else scopy, 2 * s + 1)
            for i in planes:
                if i < 6:
                    p_exit(vcopy if i in (0,) else scopy, i, 2)
            if s < PAIRS - 2:
                early_mult(2 * s + 3)
            if s == 4:
                result(scopy, 6)
                result(scopy, 7)
                p_cast(gcopy, 4, 4, True)
            if s == 6:
                p_quant(2, 2)
                store_words(2, 4)
            u_quant(2 * s, 2)
            if s == 3:
                p_cast(gcopy, 0, 4, True)
                w_quant(13, 16)
            if s == 5:
                result(scopy, 8)
                result(scopy, 9)
                p_cast(gcopy, 8, 2, True)
                p_quant(0, 2)
                store_words(0, 2)
            if s == 6:
                p_quant(4, 2)
        result(scopy, 10)
        result(scopy, 11)
        store_words(4, 6)
        p_exit(scopy, 6, 2)
        weigh(14, 0)
        p_cast(gcopy, 10, 2, True)
        weigh(14, 1)
        weigh(15, 0)
        result(scopy, 12)
        result(scopy, 13)
        u_quant(14, 1)
        u_quant(15, 1, 0)
        weigh(15, 1)
        p_turn(8, 2)
        p_turn(10, 2)
        p_exit(scopy, 8, 2)
        p_quant(6, 2)
        store_words(6, 8)
        u_quant(15, 1, 1)
        p_exit(scopy, 10, 2)
        result(scopy, 14)
        p_cast(vcopy, 12, 2)
        p_quant(8, 2)
        p_product(15, 0)
        p_product(15, 1)
        r_product(15)
        p_cast(vcopy, 14, 1)
        d_exit(scopy, 15)
        p_quant(10, 2)
        store_words(8, 12)
        p_turn(12, 1)
        p_turn(13, 1)
        p_turn(14, 1)
        r_exit(scopy, 15)
        p_exit(vcopy, 12, 1, 12, 2)
        p_quant(15, 1)
        p_exit(scopy, 13, 1, 12, 2)
        p_exit(vcopy, 14, 1)
        p_quant(12, 2)
        p_quant(14, 1)
        store_words(12, 16)
        store_scales()
